import numpy as np, ml_dtypes
CORES = [48,51,52,55]
N = 4
BF = ml_dtypes.bfloat16
def gentries(a):
    return np.ascontiguousarray(a.reshape(8, 16, -1).transpose(0, 2, 1)).reshape(8, -1)
def gtable(e):
    e = np.asarray(e); return np.ascontiguousarray(e.reshape(8, -1, 16).transpose(0, 2, 1)).reshape(128, -1).astype(np.int32)
V, B, P, T, RO = 512, 3072, 256, 128, 4
C, M, GH = V + P * RO, B + P * RO, (N - 1) * T
I, SEV = B - GH, 176
THETA, DELTA = (470, 540, 620, 560), (8, 6, 9, 7)
def wire(rng, bias, edge=False, crowd=None, hole=None, full=()):
    en = np.zeros((N, 8, 2, B), np.int64); bl = np.full((N, 8, 16, V), -1, np.int64); snd = np.zeros((N, 8, N - 1, T), np.int64)
    for q in range(N):
        for g in range(8):
            if crowd is not None and crowd[g] >= 0:
                s = (rng.permutation(V)[:, None] * 16 + np.arange(16)).reshape(-1)
                a, z, w = s[:I].copy(), np.roll(s[I:2 * I], crowd[g]), s[2 * I:2 * I + GH].copy()
            else:
                key = rng.random((V, 16)) + bias[q, g][:, None]
                if hole is not None: key = key + 99.0 * (np.arange(16)[None, :] == hole[q, g][:, None])
                s = np.argsort(key.reshape(-1))[:2 * I + GH]; s = s[rng.permutation(2 * I + GH)]
                a, z, w = s[:I].copy(), s[I:2 * I].copy(), s[2 * I:].copy()
                if g in full:
                    s = s[np.argsort(bias[q, g][s // 16] >= 0, kind="stable")]; w, a, z = s[:GH].copy(), s[GH:GH + I].copy(), s[GH + I:].copy()
                    m = rng.random(I) < 0.5; a, z = np.where(m, z, a), np.where(m, a, z)
                for i in np.flatnonzero(a // 16 == z // 16):
                    if a[i] // 16 == z[i] // 16:
                        j = np.flatnonzero((z // 16 != a[i] // 16) & (a // 16 != z[i] // 16)); j = int(j[rng.integers(0, len(j))])
                        zi, zj = int(z[i]), int(z[j]); z[i] = zj; z[j] = zi
            if edge: o = np.concatenate([GH // 2 + rng.permutation(I), rng.permutation(np.concatenate([np.arange(GH // 2), np.arange(GH // 2 + I, B)]))])
            else: o = rng.permutation(B)
            k, tw = o[:I], o[I:]
            en[q, g, 0, k] = a // 16; en[q, g, 1, k] = z // 16
            bl[q, g, a % 16, a // 16] = k; bl[q, g, z % 16, z // 16] = k; bl[q, g, w % 16, w // 16] = tw
            snd[q, g] = tw.reshape(N - 1, T); far = C + np.arange(GH); first = (q + 1 + np.arange(GH) // T) % N > q
            en[q, g, 0, tw] = np.where(first, w // 16, far); en[q, g, 1, tw] = np.where(first, far, w // 16)
    return en, bl, snd
def cells(rng, s, swing):
    lead, n = s.shape[:-1], s.shape[-1]; base = (s >> 4)[..., None, :]
    x = base + (np.argsort(rng.random(lead + (16, n)), axis=-2) < (s & 15)[..., None, :])
    room = np.clip(np.minimum(base, 62 - base), 0, swing)
    z = (rng.random(lead + (8, n)) * (room + 1)).astype(np.int64) * (1 - 2 * rng.integers(0, 2, lead + (8, n)))
    x[..., 0::2, :] += z; x[..., 1::2, :] -= z
    return x
def twin(y, snd):
    for q in range(N):
        for d in range(1, N):
            r = (q + d) % N
            if q < r:
                for g in range(8): y[r, g][:, snd[r, g, N - 1 - d]] = y[q, g][:, snd[q, g, d - 1]]
    return y
def xsums(rng): return np.clip(rng.integers(100, 901, (N, 8, V)) + rng.integers(-260, 65, (N, 8, 1)), 0, 1008)
def ysums(rng, share): return np.where(rng.random((N, 8, B)) < share, SEV + (rng.integers(0, 640, (N, 8, B)) * rng.random((N, 8, B))).astype(np.int64), rng.integers(0, SEV, (N, 8, B)))
def pack(x, y, en, bl, snd):
    return {"x0": np.ascontiguousarray(x.reshape(N, 128, V)).astype(np.float32).astype(BF), "y0": np.ascontiguousarray(y.reshape(N, 128, B)).astype(np.float32).astype(BF),
            "bl0": np.ascontiguousarray(bl.reshape(N, 128, V)).astype(np.int32), "en0": np.ascontiguousarray(en.reshape(N, 16, B)).astype(np.int32), "snd": np.stack([gtable(a.reshape(8, -1)) for a in snd])}
def setup_inputs(rng):
    en, bl, snd = wire(rng, 0.6 * rng.random((N, 8, V)))
    return pack(cells(rng, xsums(rng), 12), twin(cells(rng, ysums(rng, 0.92), 12), snd), en, bl, snd)
def setup_inputs_spread(rng):
    en, bl, snd = wire(rng, 2.0 * rng.random((N, 8, V)))
    ex = rng.choice(np.array([0.3, 0.7, 1.0, 2.0, 4.0]), (N, 8, 1, V)); ey = rng.choice(np.array([0.2, 1.0, 3.0, 6.0]), (N, 8, 1, B))
    x = np.minimum((64 * rng.random((N, 8, 16, V)) ** ex).astype(np.int64), 63); y = np.minimum((64 * rng.random((N, 8, 16, B)) ** ey).astype(np.int64), 63)
    return pack(x, twin(y, snd), en, bl, snd)
def setup_inputs_ends(rng):
    en, bl, snd = wire(rng, np.zeros((N, 8, 1)) - np.abs(2 * np.arange(V) - (V - 1)) * 9.0 / V, edge=True)
    pat = np.argsort(rng.random((8, 16)), axis=1) < 8; gi = np.arange(8)[None, :, None]
    kinds = np.stack([np.ones((8, 16), bool), pat, ~pat, np.zeros((8, 16), bool)]).astype(np.int64) * 63
    key = rng.random((N, 8, V)); key[..., 0] = -1.0; key[..., V - 1] = -2.0
    go = np.where(gi % 2 == 0, key < 0.75, np.argsort(np.argsort(key, axis=2), axis=2) < P)
    kx = rng.integers(0, 3, (N, 8, V)); kx[..., 0] = 0; kx[..., V - 1] = 0
    x = kinds[np.where(go, kx, 3), gi].transpose(0, 1, 3, 2)
    ky = rng.choice(5, (N, 8, B), p=[0.2, 0.35, 0.2, 0.1, 0.15]); ky[:, 7] = np.where(ky[:, 7] >= 3, 1, ky[:, 7])
    y = np.ascontiguousarray(kinds[np.minimum(ky, 3), gi].transpose(0, 1, 3, 2))
    y = np.where((ky == 4)[:, :, None, :], 63 * rng.integers(0, 2, y.shape), y)
    return pack(x, twin(y, snd), en, bl, snd)
def setup_inputs_corners(rng):
    bias = rng.choice(np.array([-9.0, 0.0, 9.0]), (N, 8, V), p=[0.25, 0.55, 0.2]); bias[..., 0] = -9.0; bias[..., V - 1] = -9.0
    hole = np.where(rng.random((N, 8, V)) < 0.6, 15, rng.integers(0, 16, (N, 8, V))); hole = np.where((bias < 0) & (rng.random((N, 8, V)) < 0.6), hole, -1); hole[..., 0] = -1; hole[..., V - 1] = -1
    en, bl, snd = wire(rng, bias, hole=hole)
    s = rng.choice(np.array([SEV, SEV - 1, SEV + 1, 1008, 0]), (N, 8, B), p=[0.3, 0.2, 0.2, 0.15, 0.15]); s = np.where(rng.random((N, 8, B)) < 0.5, s, ysums(rng, 0.9))
    y = cells(rng, s, 12); y[:, 3] = 22; y[:, 5] = 52; y = twin(y, snd)
    thr = THETA[0] + (np.add.reduce((np.add.reduce(y, axis=2) >= SEV).astype(np.int64), axis=2) & 31)[:, :, None]
    n = rng.choice(np.array([0, 1, P - 1, P, P + 1, V]), (N, 8)); n[:, 3] = P; n[:, 5] = P + 1; n[0] = (0, 1, P - 1, P, P + 1, P + 1, V, P)
    hot = np.argsort(rng.random((N, 8, V)), axis=2) < n[:, :, None]
    up = np.where(rng.random((N, 8, V)) < 0.5, thr, thr + (rng.random((N, 8, V)) * (1009 - thr)).astype(np.int64))
    down = np.where(rng.random((N, 8, V)) < 0.5, thr - 1, (rng.random((N, 8, V)) * thr).astype(np.int64))
    x = cells(rng, np.where(hot, up, down), 12); x[:, 3] = np.where(hot[:, 3], 63, 0)[:, None, :]; x[:, 5] = np.where(hot[:, 5], 32, 0)[:, None, :]
    return pack(x, y, en, bl, snd)
def setup_inputs_crowd(rng):
    go = np.argsort(rng.random((N, 8, V)), axis=2) < P; two = [2, 7]
    bias = np.zeros((N, 8, V)); bias[:, two] = np.where(go[:, two], -9.0, 0.0)
    en, bl, snd = wire(rng, bias, crowd=(0, 1, -1, 0, 1, 0, 1, -1), full=(2, 7))
    s = xsums(rng); s[:, :2] = rng.integers(510, 1009, (N, 2, V)); s[:, 3] = rng.integers(510, 1009, (N, V)); s[np.arange(N), 3, rng.integers(0, V, N)] = rng.integers(0, 400, N)
    s[:, 5:7] = THETA[0] + np.array([B & 31, (B - 1) & 31])[None, :, None] + rng.choice(np.array([-40, -1, 0, 1, 40]), (N, 2, V), p=[0.1, 0.4, 0.3, 0.1, 0.1])
    t = ysums(rng, 0.9); live = ysums(rng, 2.0)
    for g in (0, 1, 3, 4, 5, 6): t[:, g] = live[:, g]
    y = cells(rng, t, 12); y[:, two] = rng.integers(52, 64, (N, 2, 16, B)); y = twin(y, snd)
    for q in range(N):
        for g in (1, 4, 6): y[q, g][:, int(rng.choice(np.setdiff1d(np.arange(B), snd[q, g].reshape(-1))))] = 10
        go[q, 2, int(rng.choice(np.flatnonzero(go[q, 2])))] = False
    x = cells(rng, s, 12); x[:, two] = np.where(go[:, two][:, :, None, :], rng.integers(32, 41, (N, 2, 16, V)), rng.integers(0, 8, (N, 2, 16, V)))
    return pack(x, y, en, bl, snd)
def check_inputs(d):
    bad = []
    for k, lo, hi in (("x0", 0, 63), ("y0", 0, 63), ("bl0", -1, B - 1), ("en0", 0, C + GH - 1), ("snd", 0, B - 1)):
        a = np.asarray(d[k]).astype(np.float64)
        if not (np.min(a) >= lo and np.max(a) <= hi and np.all(a == np.floor(a))): bad.append("range of " + k)
    if bad: return bad
    en = d["en0"].astype(np.int64).reshape(N, 8, 2, B); bl = d["bl0"].astype(np.int64).reshape(N, 8, 16, V)
    sl = np.stack([gentries(a) for a in d["snd"]]).astype(np.int64); y = d["y0"].astype(np.float32).reshape(N, 8, 16, B)
    for q in range(N):
        for g in range(8):
            s, e = sl[q, g], en[q, g]; tw = np.zeros(B, bool); tw[s] = True
            if len(np.unique(s)) < GH: bad.append("twins of snd differ")
            if np.any(e[:, ~tw] >= V) or np.any(e[0, ~tw] == e[1, ~tw]): bad.append("ends of en0 on one rank")
            first = (q + 1 + np.arange(GH) // T) % N > q; own = np.where(first, e[0, s], e[1, s]); far = np.where(first, e[1, s], e[0, s])
            if np.any(own >= V) or np.any(far != C + np.arange(GH)): bad.append("ends of en0 of twins")
            r, c = np.nonzero(bl[q, g] >= 0); have = np.sort(bl[q, g][r, c] * V + c)
            want = np.sort((np.arange(B)[None, :] * V + e)[e < V])
            if len(have) != len(want) or np.any(have != want): bad.append("slots of bl0")
        for k in range(1, N):
            r = (q + k) % N
            for g in range(8):
                if np.any(y[q, g][:, sl[q, g].reshape(N - 1, T)[k - 1]] != y[r, g][:, sl[r, g].reshape(N - 1, T)[N - 1 - k]]): bad.append("y0 of twins alike")
    return sorted(set(bad))
def reference(x0, y0, bl0, en0, snd):
    x = np.zeros((N, 8, 16, C), np.int32); x[..., :V] = x0.astype(np.float32).astype(np.int32).reshape(N, 8, 16, V)
    y = np.zeros((N, 8, 16, M), np.int32); y[..., :B] = y0.astype(np.float32).astype(np.int32).reshape(N, 8, 16, B)
    bits = y[..., :1024] & 7
    exists = np.zeros((N, 8, C), bool); exists[..., :V] = True
    bl = np.full((N, 8, 16, C), -1, np.int64); bl[..., :V] = bl0.reshape(N, 8, 16, V)
    en = np.zeros((N, 8, 2, M), np.int64); en[..., :B] = en0.reshape(N, 8, 2, B)
    sl = np.stack([gentries(a) for a in snd]).astype(np.int64).reshape(N, 8, N - 1, T)
    take = np.take_along_axis
    for t in range(RO):
        live = np.add.reduce(y, axis=2) >= SEV
        count = np.add.reduce(live.astype(np.int64), axis=2)
        cand = np.add.reduce(x, axis=2) >= THETA[t] + (count & 31)[:, :, None]
        place = np.add.accumulate(cand.astype(np.int64), axis=2) - cand
        div = cand & (place < P)
        low = np.where(div[:, :, None], np.maximum(x - DELTA[t], 0), x); high = np.where(div[:, :, None], np.minimum(x + DELTA[t], 63), x)
        own = [[take(en[q, :, 0 if q < (q + d) % N else 1], sl[q, :, d - 1], 1) for d in range(1, N)] for q in range(N)]
        for q in range(N):
            wl, wh, wd = [low[q]], [high[q]], [div[q]]
            for d in range(1, N):
                r = (q + d) % N; c = own[r][N - 1 - d]
                wl.append(take(low[r], c[:, None, :], 2)); wh.append(take(high[r], c[:, None, :], 2)); wd.append(take(div[r], c, 1))
            wl, wh, wd = np.concatenate(wl, axis=2), np.concatenate(wh, axis=2), np.concatenate(wd, axis=1)
            e = en[q].copy(); a = [take(w, e[:, 0][:, None, :], 2) for w in (wl, wh)]; z = [take(w, e[:, 1][:, None, :], 2) for w in (wl, wh)]
            score = np.stack([np.add.reduce(np.abs(2 * y[q] - a[i] - z[j]), axis=1) for i in (0, 1) for j in (0, 1)])
            best = np.argmin(score, axis=0); pole = np.stack([best >> 1, best & 1], axis=1)
            touched = live[q] & (take(wd, e[:, 0], 1) | take(wd, e[:, 1], 1))
            gap = np.abs(np.where((pole[:, 0] == 1)[:, None], a[1], a[0]) - np.where((pole[:, 1] == 1)[:, None], z[1], z[0]))
            yn = np.where(touched[:, None], (y[q] + gap) >> 1, y[q]); stays_live = np.add.reduce(yn, axis=1) >= SEV
            move = touched[:, None] & (e < C) & (pole == 1); ne = np.where(move, V + P * t + take(place[q][:, None, :], np.minimum(e, C - 1), 2), e)
            for g in range(8):
                v = np.flatnonzero(div[q, g]); n = V + P * t + np.arange(len(v)); old = bl[q, g][:, v]; b = np.maximum(old, 0)
                keep = (old >= 0) & stays_live[g][b]; side = np.where(e[g, 0][b] == v[None, :], pole[g, 0][b], pole[g, 1][b])
                tv = np.where(keep & (side == 0), old, -1); tn = np.where(keep & (side == 1), old, -1)
                k = np.flatnonzero(np.any(tv < 0, axis=0) & np.any(tn < 0, axis=0)); nb = B + P * t + k
                rv, rn = np.argmax(tv < 0, axis=0)[k], np.argmax(tn < 0, axis=0)[k]
                tv[rv, k] = nb; tn[rn, k] = nb
                bl[q, g][:, v] = tv; bl[q, g][:, n] = tn
                yn[g][:, nb] = high[q, g][:, v[k]] - low[q, g][:, v[k]]; ne[g, 0, nb] = v[k]; ne[g, 1, nb] = n[k]
                x[q, g][:, v] = low[q, g][:, v]; x[q, g][:, n] = high[q, g][:, v]; exists[q, g, n] = True
            y[q] = yn; en[q] = ne
        if t + 1 < RO:
            x = np.where(exists[:, :, None], np.minimum(np.maximum(x + np.take(bits, (np.arange(C) + 331 * t) & 1023, axis=3) - 3, 0), 63), x)
    return {"yx": x.reshape(N, 128, C).astype(np.float32).astype(BF), "yy": y.reshape(N, 128, M).astype(np.float32).astype(BF),
            "yl": bl.reshape(N, 128, C).astype(np.float32), "ye": en.reshape(N, 16, M).astype(np.float32)}

@@ -1,0 +1,562 @@
+import numpy as np
+from concourse.bass import DstId, RemoteDMATransfer
+from concourse.mybir import dt, AluOpType, AxisListType, ActivationFunctionType
+
+A = AluOpType
+F = ActivationFunctionType
+THETA, DELTA = (470, 540, 620, 560), (8, 6, 9, 7)
+BF, HF, F32, I32, U16 = "bfloat16", "float16", "float32", "int32", "uint16"
+CST, LOO, HIO, CST2, YBO, WBW = 3584, 3600, 5520, 7440, 7456, 11296
+XO = 1280
+RH = 8192
+SB = {
+    "Y0N": ([3072], BF), "WB": ([WBW], BF), "YF": ([4096], BF), "HH": ([1920], BF), "WP": ([1920], F32), "XT": ([XO + 2560], BF),
+    "UH": ([3840], HF), "WA": ([3840], HF), "WZ": ([3840], HF), "HZ": ([3840], BF), "AB": ([4 * 3840], BF),
+    "R": ([RH + 4112], BF), "BL": ([1792], F32), "BLF": ([1792], F32), "VD": ([1792], BF), "DR": ([1024], BF),
+    "DLD": ([1536], BF), "BTG": ([1280], BF), "NXT": ([1024], BF), "TI": ([1024], I32), "BC": ([8], F32), "IO1": ([256], BF),
+    "EI": ([2, 192], I32), "ED": ([2, 192], I32), "DG": ([4, 192], BF), "BI": ([512], I32), "SI": ([24], I32),
+    "E0": ([2, 256], F32), "E1": ([2, 256], F32), "EU0": ([2, 256], U16), "EU1": ([2, 256], U16),
+    "LV0": ([256], BF), "LV1": ([256], BF), "PT": ([2, 256], BF), "IX": ([2, 256], U16),
+    "SS": ([360], F32), "MM": ([480], F32), "FL": ([480], HF), "FF": ([504], F32), "MX": ([120], HF), "TT": ([256], BF), "TOP": ([480], BF),
+    "IA": ([120], F32), "JK": ([256], BF), "SX": ([80], F32), "CA": ([80], BF), "CU": ([80], F32), "PL": ([80], F32), "ND": ([80], F32),
+    "B1": ([80], F32), "B2": ([80], F32), "B3": ([80], F32), "B4": ([80], F32), "UHI": ([80], U16), "ULO": ([80], U16), "UBT": ([80], U16), "USC": ([80], U16),
+    "COL": ([32], F32), "CI": ([8], I32), "DL2": ([16], U16), "DLF": ([16], F32), "DLM": ([16], U16), "S16": ([64], F32), "ULAST": ([64], U16),
+    "OLD": ([256], F32), "OLU": ([512], U16), "LIW": ([256], BF), "LI": ([256], BF), "SM": ([512], BF), "NM": ([512], BF),
+    "ML": ([256], BF), "T1": ([512], F32), "T2": ([512], F32), "TVF": ([256], F32),
+    "TW": ([24], U16), "TWF": ([24], F32), "OWN": ([24], F32), "OWU": ([24], U16), "GT": ([384], BF), "GW": ([384], HF), "F2": ([24], HF), "P2": ([24], HF), "M2": ([24], BF),
+    "ONE": ([512], BF), "ONES": ([128], BF), "TRI": ([128], BF), "S": ([144], BF), "PK": ([144], BF), "PK8": ([144], BF), "PKA": ([128], BF),
+    "TM": ([128], BF), "TF": ([128], BF), "ID": ([15 * 128], BF), "IF": ([128], F32), "ONF": ([128], F32), "PQ": ([128], BF), "ETA": ([512], BF), "BT": ([272], BF),
+    "VC": ([256], F32), "ALT": ([512], F32), "VM": ([80], F32), "IO": ([512], F32), "ZE": ([80], F32),
+    "SN0": ([3, 256], BF), "SN1": ([3, 256], BF), "LN0": ([3, 256], BF), "LN1": ([3, 256], BF), "LN2": ([3, 256], BF), "LN3": ([3, 256], BF),
+}
+SCRATCH = {k: ("sbuf", [128] + v[0], v[1]) for k, v in SB.items()}
+SCRATCH["PS"] = ("psum", [128, 4096], F32)
+NDMA = 84
+SEMAPHORES = ["v", "s", "p", "q"] + ["ar%d" % t for t in range(4)] + ["ls%d" % t for t in range(4)] + ["d%d" % i for i in range(NDMA)]
+IDW = (1.0, -1.0, 2.0, 0.5, -0.5, 128.0, -128.0, 64.0, 32768.0, 2048.0, 1920.0, 8192.0, -8192.0, 16384.0, -16384.0)
+G_CYC, S_CYC = 1.5, 3.8
+BMODE = [[1] * 4, [1] * 4, [1] * 4]
+NA, LAST, GP, BP, FIRST = [3], [64], [48], [32], [64, 72, 80, 80]
+
+
+def bits(idx):
+    m = np.zeros(16384, np.uint8); m[idx] = 1
+    return int.from_bytes(np.packbits(m, bitorder="little").tobytes(), "little")
+
+
+def ap(buf, *idx, p=None):
+    ps = slice(0, 128) if p is None else p
+    if buf not in SCRATCH:
+        return (buf, p, idx, 0, 0, 0)
+    shape = SCRATCH[buf][1][1:]
+    if not idx: idx = tuple(slice(0, n) for n in shape)
+    cols = np.arange(int(np.prod(shape))).reshape(shape)[idx].reshape(-1)
+    if buf == "PS": return (buf, ps, idx, len(cols), 1, bits(np.unique(cols // 512)))
+    return (buf, ps, idx, len(cols), bits(np.arange(128)[ps]), bits(cols))
+
+
+def c(buf, a, b, s=1): return ap(buf, slice(a, b, s) if s > 1 else slice(a, b))
+def size(x): return {BF: 2, HF: 2, U16: 2, F32: 4, I32: 4}[SCRATCH[x[0]][2]]
+
+
+def build():
+    ops = []; tag = ["i"]
+
+    def add(alts, rd, wr, kind="c", extra=None):
+        ops.append({"alts": alts, "rd": [x for x in rd if isinstance(x, tuple) and x[0] in SCRATCH], "wr": [x for x in wr if x[0] in SCRATCH], "kind": kind, "x": extra, "tag": tag[0]})
+
+    def vc(n, k): return 70 + max(64, n * k) * 1.0
+    def half(o, i): return 0.5 if size(o) == 2 and size(i) == 2 else 1.0
+    def ts(o, i, s1, s2, op0, op1=None):
+        if op1 is None: f = lambda g, r: g.vector.tensor_scalar(r(o), r(i), r(s1), None, op0)
+        else: f = lambda g, r: g.vector.tensor_scalar(r(o), r(i), r(s1), r(s2), op0, op1)
+        add({"v": (f, vc(o[3], half(o, i)))}, [i, s1, s2], [o])
+    def tt(o, i0, i1, op):
+        k = 1 if "PS" in (i0[0], i1[0]) else 2
+        add({"v": (lambda g, r: g.vector.tensor_tensor(r(o), r(i0), r(i1), op), vc(o[3], k))}, [i0, i1], [o])
+    def cp(o, i): add({"v": (lambda g, r: g.vector.tensor_copy(r(o), r(i)), vc(o[3], half(o, i)))}, [i], [o])
+    def ms(o, v): add({"v": (lambda g, r: g.vector.memset(r(o), v), vc(o[3], size(o) / 4.0))}, [], [o])
+    def act(o, i, fn, bias=0.0, scale=1.0, acc=None):
+        add({"s": (lambda g, r: g.scalar.activation(r(o), r(i), fn, bias=r(bias), scale=scale, accum_out=None if acc is None else r(acc)), vc(o[3], 1) + 20)},
+            [i, bias], [o] + ([acc] if acc else []))
+    def ev(o, i, add_=0.0, mul=1.0, eng="vs"):
+        alts = {}
+        if "v" in eng: alts["v"] = (lambda g, r: g.vector.tensor_scalar(r(o), r(i), mul, add_, A.mult, A.add), vc(o[3], half(o, i)))
+        if "s" in eng: alts["s"] = (lambda g, r: g.scalar.activation(r(o), r(i), F.Identity, bias=add_, scale=mul), vc(o[3], 1) + 20)
+        add(alts, [i], [o])
+    def gat(o, w, off, add_=0.0, eng="vs"):
+        alts = {}
+        if "v" in eng:
+            if add_: alts["v"] = (lambda g, r: g.vector.tensor_scalar(r(o), r(w).indirect(r(off)), add_, None, A.add), vc(o[3], G_CYC))
+            else: alts["v"] = (lambda g, r: g.vector.tensor_copy(r(o), r(w).indirect(r(off))), vc(o[3], G_CYC))
+        if "s" in eng: alts["s"] = (lambda g, r: g.scalar.activation(r(o), r(w).indirect(r(off)), F.Identity, bias=add_), vc(o[3], G_CYC) + 20)
+        add(alts, [w, off], [o])
+    def gtt(o, w, off, i1, op):
+        add({"v": (lambda g, r: g.vector.tensor_tensor(r(o), r(w).indirect(r(off)), r(i1), op), vc(o[3], G_CYC))}, [w, off, i1], [o])
+    def sca(w, off, i):
+        add({"v": (lambda g, r: g.vector.tensor_copy(r(w).indirect(r(off)), r(i)), vc(i[3], S_CYC))}, [off, i, w], [w])
+    def mm(lst, start=True, stop=True):
+        def f(g, r):
+            for j, (o, l, x) in enumerate(lst): ins = g.tensor.matmul(r(o), r(l), r(x), start and j == 0, stop and j == len(lst) - 1)
+            return ins
+        add({"p": (f, 40 + sum(max(64, x[3]) * 0.5 * (4 if size(x) == 4 else 1) for o, l, x in lst))}, [y for o, l, x in lst for y in (l, x)], [o for o, l, x in lst])
+    def iota(o, pat, base, cm):
+        fl = SCRATCH[o[0]][2] != I32
+        if fl: f = lambda g, r: g.iota(r(o), pat, base, cm, allow_small_or_imprecise_dtypes=True)
+        else: f = lambda g, r: g.iota(r(o), pat, base, cm)
+        add({"q": (f, 150 + 2.0 * o[3])}, [], [o])
+    def sel(o, i, pat, op, base, cm):
+        add({"q": (lambda g, r: g.affine_select(r(o), r(i), pat, op, 0.0, base, cm), 190 + 2.0 * o[3])}, [i], [o])
+    def dma(o, i, q="y", nbytes=None):
+        x = i if i[0] in SCRATCH else o
+        nb = nbytes or x[3] * size(x) * 128
+        fs = {"y": lambda g, r: g.sync.dma_start(r(o), r(i)), "s": lambda g, r: g.scalar.dma_start(r(o), r(i)), "q": lambda g, r: g.dma_start(r(o), r(i))}
+        add({e: (fs[e], 1000 if e == "q" else 120) for e in q}, [i], [o], "dma", 1900 + nb / 180.0)
+    def ps(bank, a, b, s=1): return c("PS", 512 * bank + a, 512 * bank + b, s)
+    def idm(w): j = IDW.index(w); return c("ID", 128 * j, 128 * j + 128)
+    def sh(buf, r): return c(buf, 15 - r, 143 - r)
+    def col(j): return c("COL", j, j + 1)
+    def compact(out, m, buf, a, n):
+        return [(out, sh(m, r), c(buf, a + r, a + 16 * n, 16)) for r in range(16)]
+    def rows(f, a, b): return ap("R", slice(a, b), p=slice(f, 128, 16))
+    PM, PM16, W16, W2K, M0, M1, LOLD, LNEW, THR, V128 = range(10)
+
+    for h in range(2): dma(ap("EI", h, slice(0, 192)), ap("en0", slice(0, 3072), p=slice(h, 16, 2)), "ys"[h])
+    dma(c("Y0N", 0, 3072), ap("y0", slice(0, 3072), p=slice(0, 128)), "y")
+    dma(c("XT", XO, XO + 512), ap("x0", slice(0, 512), p=slice(0, 128)), "s")
+    dma(ap("SI"), ap("snd", slice(0, 24), p=slice(0, 128)), "s")
+    dma(ap("BI"), ap("bl0", slice(0, 512), p=slice(0, 128)), "y")
+    ms(ap("ONE"), 1.0)
+    iota(c("CI", 0, 1), [[1, 1]], 0, 1)
+    sel(ap("TRI"), c("ONE", 0, 128), [[-16, 8], [0, 16]], A.is_ge, 0, 1)
+    sel(ap("ONES"), ap("TRI"), [[16, 8], [0, 16]], A.is_ge, 15, -1)
+    sel(idm(1.0), c("ONE", 0, 128), [[-1, 128]], A.is_equal, 0, 1)
+    sel(ap("TRI"), ap("ONES"), [[1, 128]], A.is_gt, 0, -1)
+    ts(c("CI", 1, 2), c("CI", 0, 1), 15, None, A.bitwise_and)
+    cp(col(PM), c("CI", 1, 2))
+    ts(col(PM16), col(PM), 16.0, None, A.mult)
+    ts(col(M0), col(PM), 0.0, None, A.is_equal); ts(col(M1), col(PM), 1.0, None, A.is_equal)
+    ts(col(W16), col(M1), 16.0, col(M0), A.mult, A.add); ts(col(W2K), col(W16), 128.0, None, A.mult)
+    ms(ap("S"), 0.0); cp(c("S", 15, 143, 16), c("ONES", 0, 128, 16))
+    ts(ap("PK"), ap("S"), col(W16), None, A.mult); ts(ap("PK8"), ap("S"), col(W2K), None, A.mult); ts(ap("PKA"), ap("ONES"), col(W16), None, A.mult)
+    for w in IDW[1:]: ev(idm(w), idm(1.0), 0.0, w)
+    ev(ap("IF"), idm(1.0))
+    tt(ap("TM"), ap("TRI"), ap("ONES"), A.subtract); ts(c("JK", 0, 128), idm(1.0), -4096.0, None, A.mult); tt(ap("TM"), ap("TM"), c("JK", 0, 128), A.min)
+    tt(c("JK", 128, 256), ap("TRI"), idm(1.0), A.subtract); ev(ap("TF"), c("JK", 128, 256), 0.0, 16384.0)
+    iota(c("T2", 504, 512), [[256, 4], [RH, 2]], 3072, 0); ts(col(10), col(PM), -16384.0, None, A.mult); ts(ap("BC"), c("T2", 504, 512), col(10), None, A.add)
+    ts(c("BC", 6, 7), c("BC", 6, 7), -1.0, None, A.add); ts(c("BC", 7, 8), c("BC", 7, 8), -1.0 - RH, None, A.add)
+    iota(ap("IO1"), [[1, 256]], 1, 0)
+    ms(c("R", 0, 3088), 0.0)
+    for a in range(0, 3088, 512): ev(c("R", RH + a, RH + min(a + 512, 3088)), c("ONE", 0, min(512, 3088 - a)), 0.0, 0.0, "s")
+    ms(ap("ZE"), 0.0)
+    for j, e in enumerate((-2048.0, 0.3125, 0.53125, 0.65625)): ms(c("ETA", 128 * j, 128 * j + 128), e)
+    ms(c("WB", CST, CST + 16), 192.0); ms(c("WB", CST2, CST2 + 16), 192.0); ms(c("WP", 1528, 1536), -9.0); ms(c("BL", 1536, 1792), 0.0)
+    iota(c("IO", 0, 256), [[16, 256]], 0, 0); ts(ap("VC"), c("IO", 0, 256), col(PM), None, A.add)
+    iota(ap("VD"), [[0, 112], [1, 16]], 0, 0); iota(c("HZ", 0, 1792), [[1, 112], [0, 16]], 0, 0)
+    dma(ap("VD", slice(0, 1792), p=slice(1, 128, 16)), ap("HZ", slice(0, 1792), p=slice(1, 128, 16)), "y", 30000)
+    iota(c("T1", 0, 272), [[0, 17], [1, 16]], -8, 0); iota(c("T2", 0, 384), [[0, 3], [1, 8], [0, 16]], -4, 0)
+    ts(c("T1", 0, 272), c("T1", 0, 272), col(M0), 1.0 / 128, A.mult, A.mult); ts(c("T2", 0, 272), c("T2", 0, 272), col(M1), 1.0 / 128, A.mult, A.mult)
+    tt(ap("BT"), c("T1", 0, 272), c("T2", 0, 272), A.add)
+    iota(ap("IO"), [[1, 512]], 0, 0)
+    ev(c("ALT", 0, 256), ap("VC"), 8192.0 - LOO); ev(c("ALT", 256, 512), ap("VC"), YBO - LOO - 8192.0); ev(ap("VM"), c("VC", 0, 80), 256.0 - 4095)
+    iota(ap("S16"), [[256, 4], [1, 16]], 0, 0); ts(ap("ULAST"), ap("S16"), col(PM16), None, A.add)
+    e3 = lambda b, a, z: ap(b, slice(0, 2), slice(a, z))
+    for dgt, (s1, op) in enumerate(((15, A.bitwise_and), (4, A.logical_shift_right))):
+        ts(ap("ED"), ap("EI"), s1, None, op); cp(ap("DG", slice(2 * dgt, 2 * dgt + 2), slice(0, 192)), ap("ED"))
+        for h in range(2): dma(rows(dgt, RH * h + 1, RH * h + 3073), ap("DG", 2 * dgt + h, slice(0, 192)), "ys"[h])
+    cp(e3("E0", 0, 192), ap("EI")); cp(e3("EU0", 0, 192), ap("EI"))
+    for d in range(1, 4):
+        o, i = c("TW", 8 * d - 8, 8 * d), c("SI", 8 * d - 8, 8 * d)
+        add({"v": (lambda g, r, o=o, i=i, d=d: g.vector.tensor_scalar(r(o), r(i), 1.0 + (0 if (r("rank") + d) % 4 > r("rank") else RH), None, A.add), 140)}, [i], [o])
+    gat(ap("GT"), c("R", 0, RH + 3088), ap("TW"))
+    mm(compact(ps(6, 0, 24), "PK", "GT", 0, 24))
+    cp(ap("OWU"), ps(6, 0, 24)); ev(ap("OWN"), ps(6, 0, 24))
+    mm([(ps(7, 0, 192), sh("S", r), c("Y0N", 192 * r, 192 * r + 192)) for r in range(16)])
+    ts(c("LV0", 0, 192), ps(7, 0, 192), 176.0, None, A.is_ge)
+    mm([(ps(7, 0, 192), ap("ONES"), c("LV0", 0, 192))])
+    act(c("JK", 0, 192), ps(7, 0, 192), F.Identity, acc=col(LOLD))
+    ev(ap("ONF"), ap("ONES"), 0.0, -1.0); ms(ap("PQ"), 0.0); tt(col(13), col(M0), col(M1), A.subtract); tt(col(14), col(M0), col(M1), A.add)
+    ts(c("PQ", 0, 128, 16), c("ONES", 0, 128, 16), col(13), None, A.mult); ts(c("PQ", 1, 128, 16), c("ONES", 0, 128, 16), col(14), None, A.mult)
+    ts(col(12), col(M1), -16.0, -143.0, A.mult, A.add)
+
+    def cells_ahead(t):
+        C = 512 + 256 * t; X = c("XT", XO, XO + C)
+        mm(compact(ps(0, 0, C // 16), "S", "XT", XO, C // 16)); ev(c("SX", 0, C // 16), ps(0, 0, C // 16), float(-THETA[t]))
+        ts(c("XT", XO - C, XO), X, float(DELTA[t]), 63.0, A.add, A.min)
+        o = c("XT", XO + C, XO + 2 * C); dl = float(-DELTA[t])
+        add({"v": (lambda g, r: g.vector.tensor_scalar(r(o), r(X), dl, 0.0, A.add, A.max), vc(C, 0.5)),
+             "s": (lambda g, r: g.scalar.activation(r(o), r(X), F.Relu, bias=dl), vc(C, 1) + 20)}, [X], [o])
+    cells_ahead(0)
+    for r in range(16): ev(c("WB", r, 3072, 16), c("Y0N", 192 * r, 192 * r + 192), 192.0)
+    cp(ap("TI"), c("Y0N", 0, 1024)); ts(ap("TI"), ap("TI"), 7, None, A.bitwise_and); ts(ap("DR"), ap("TI"), -3.0, None, A.add)
+    tag[0] = "h"
+    ts(ap("OLU"), ap("BI"), 1.0, None, A.add)
+    for j in range(8):
+        gat(c("YF", 1024 * (j % 4), 1024 * (j % 4) + 1024), c("R", 0, 3088), c("OLU", 64 * j, 64 * j + 64))
+        mm(compact(ps(4 + j // 4, 64 * (j % 4), 64 * (j % 4) + 64), "PK", "YF", 1024 * (j % 4), 64))
+        if j % 4 == 3: tt(c("T1", 64 * j - 192, 64 * j + 64), ps(4 + j // 4, 0, 256), c("IO", 64 * j - 192, 64 * j + 64), A.not_equal)
+    ts(ap("T1"), ap("T1"), float(RH), 1.0, A.mult, A.add); tt(c("BL", 0, 512), ap("T1"), ap("BI"), A.add)
+    late = [lambda: iota(c("R", 3088, 4112), [[0, 1024]], 0, 0), lambda: iota(c("R", RH + 3088, RH + 4112), [[0, 1024]], 0, 0)]
+
+    reg = [0, 0]
+    for t in range(4):
+        C = 512 + 256 * t; Kc = C // 16; K = 192 + 16 * t; Ks = K // 2; base = 512 + 256 * t
+        E, En, EU, EUn, LV, LVn = ("E%d" % (t % 2), "E%d" % (1 - t % 2), "EU%d" % (t % 2), "EU%d" % (1 - t % 2), "LV%d" % (t % 2), "LV%d" % (1 - t % 2))
+        ysrc = 0 if t % 2 == 0 else YBO
+        ydst = (lambda a, b: c("WB", YBO + a, YBO + b), lambda a, b: c("WB", a, b), lambda a, b: c("WB", YBO + a, YBO + b), lambda a, b: c("YF", a, b))[t]
+        win = c("WB", 0, CST2) if t % 2 == 0 else c("WB", LOO, YBO + 16 * K)
+        k_ = lambda b: c(b, 0, Kc)
+        tag[0] = "w"
+        mm([(ps(7, 0, 1), ap("IF"), col(LOLD))] + ([(ps(7, 0, 1), ap("IF"), col(11)), (ps(7, 0, 1), ap("ONF"), col(LNEW))] if t else []))
+        ts(c("CI", 2, 3), ps(7, 0, 1), 1.0 / 32, -15.5 / 32, A.mult, A.add); ts(col(THR), c("CI", 2, 3), -32.0, ps(7, 0, 1), A.mult, A.add)
+        ts(k_("CA"), k_("SX"), col(THR), None, A.is_ge)
+        mm([(ps(1, 0, Kc), ap("ONES"), k_("CA"))]); mm([(ps(2, 0, Kc), ap("TM"), k_("CA"))])
+        add({"v": (lambda g, r, o=k_("CU"), i=ps(1, 0, Kc), z=k_("ZE"): g.vector.tensor_tensor_scan(r(o), r(i), r(z), 0.0, A.add, A.add), 150)}, [ps(1, 0, Kc), k_("ZE")], [k_("CU")])
+        tt(k_("PL"), ps(2, 0, Kc), k_("CU"), A.add)
+        ts(k_("ND"), k_("PL"), 256.0 - 4095, float(C), A.is_ge, A.mult)
+        tt(k_("B1"), k_("VC"), k_("ND"), A.add); cp(k_("UHI"), k_("B1"))
+        gat(c("WB", HIO, HIO + C), c("XT", XO - C, XO + C), k_("UHI"))
+        tt(k_("B2"), k_("VC"), k_("ND"), A.subtract); ts(k_("ULO"), k_("B2"), float(C), None, A.add)
+        gat(c("WB", LOO, LOO + C), c("XT", XO, XO + 2 * C), k_("ULO"))
+        SN, LN = "SN%d" % (t % 2), "LN%d" % t
+        h3 = lambda b, j: ap(b, slice(0, 3), slice(128 * j, 128 * j + 128))
+        for d in range(3):
+            for j, o in enumerate((HIO, LOO)): gat(ap(SN, d, slice(128 * j, 128 * j + 128)), c("WB", o, o + C), c("OWU", 8 * d, 8 * d + 8), 9.0 * j)
+        add({"q": (None, 600)}, [ap(SN)], [], "send", t)
+        add({}, [], [ap(LN)], "arrive", t)
+        if t == 0:
+            for f in late: f()
+        ts(k_("UBT"), k_("PL"), 4095.0, 256.0, A.add, A.min)
+        gat(c("BTG", 0, C), ap("BT"), k_("UBT"))
+        ev(c("HH", 0, C), c("WB", HIO, HIO + C), 96.0, 0.5, "v")
+        for a in range(0, C, 512):
+            z = min(C, a + 512); o = ps(a // 512, 0, z - a)
+            mm([(o, idm(1.0), c("WB", HIO + a, HIO + z)), (o, idm(-1.0), c("WB", LOO + a, LOO + z)), (o, idm(1.0), c("BTG", a, z))])
+        for a in range(0, C, 512):
+            z = min(C, a + 512); ev(c("WP", a, z), c("PS", a, z), -9.0)
+        ev(c("HH", 1536, 1920), h3(LN, 0), 96.0, 0.5, "v"); ev(c("WB", HIO + 1536, HIO + 1920), h3(LN, 0)); ev(c("WB", LOO + 1536, LOO + 1920), h3(LN, 1), -9.0)
+        tt(c("WP", 1536, 1920), h3(LN, 0), h3(LN, 1), A.subtract)
+        tag[0] = "l"
+        tt(k_("B3"), k_("PL"), k_("ND"), A.add); tt(k_("B4"), k_("B3"), k_("VM"), A.min); ts(k_("USC"), k_("B4"), 4095.0, None, A.add)
+        ev(c("DLD", 0, 256), c("VD", 1536, 1792))
+        for a in range(0, C, 256): sca(c("DLD", 0, 256 + C), c("USC", a // 16, a // 16 + 16), c("VD", a, a + 256))
+        mm(compact(ps(7, 0, 16), "PK", "DLD", 0, 16))
+        mm([(ps(7, 16, 32), sh("PK", r), c("DLD", 16 * r, 16 * r + 16)) for r in range(16)])
+        mm([(ps(7, 32, 34), ap("PKA"), c("DLD", 128, 130))])
+        cp(ap("DL2"), ps(7, 0, 16)); ts(ap("DLF"), ps(7, 16, 32), 1535.0, None, A.min); ev(col(V128), ps(7, 32, 33)); ev(col(15), ps(7, 32, 33), 0.5, -1.0)
+        ts(c("NXT", 256 * t, 256 * t + 256), c("IO", 0, 256), c("CU", Kc - 1, Kc), None, A.is_ge)
+        gat(c("WB", LOO + C, LOO + C + 256), c("WB", HIO, HIO + 1920), ap("DL2"))
+        gat(ap("OLD"), ap("BL"), ap("DL2")); cp(c("OLU", 0, 256), ap("OLD"))
+        gat(ap("LIW"), ap("WP"), ap("DL2"), 201.0)
+        gat(ap("GW"), c("WP", 0, 1536), ap("OWU"), eng="v")
+        if t == 3:
+            act(c("BLF", 0, C), c("BL", 0, C), F.Sign, 0.5 - RH); ev(c("BLF", 0, C), c("BLF", 0, C), -1.0 - RH / 2, -RH / 2.0)
+            tt(c("BLF", 0, C), c("BLF", 0, C), c("BL", 0, C), A.add); ms(c("BLF", 1536, 1792), -1.0)
+            gat(ap("OLD"), ap("BLF"), ap("DL2"))
+
+        def cut(a, z, n):
+            e = [a + 2 * ((z - a) * j // (2 * n)) for j in range(n)] + [z]
+            return list(zip(e[:-1], e[1:]))
+        part = [(0, LAST[0]), (LAST[0], K - FIRST[t]), (K - FIRST[t], K)]
+        def upto(a, z, n): return cut(a, z, -(-(z - a) // n))
+        def phase_a(s):
+            tag[0] = "a%d" % s
+            k0, k1 = part[s]; Ks = k1 - k0; db = 4 + s % 2; dec = ps(3, 0, 2 * Ks)
+            for (a, z) in ([(192, k1 - 16)] if k1 > 208 else []) + ([(k1 - 16, k1)] if k1 > 192 else []) + upto(k0, min(k1, 192), GP[0]):
+                a16, z16 = 16 * a, 16 * z; n = 1536 if a >= 192 else 1920
+                gtt(c("UH", a16, z16), c("HH", 0, n), ap(EU, 0, slice(a, z)), c("WB", ysrc + a16, ysrc + z16), A.subtract)
+                gtt(c("HZ", a16, z16), c("HH", 0, n), ap(EU, 1, slice(a, z)), c("UH", a16, z16), A.add)
+                gat(c("WZ", a16, z16), c("WP", 0, n), ap(EU, 1, slice(a, z)), eng="v")
+                gat(c("WA", a16, z16), c("WP", 0, n), ap(EU, 0, slice(a, z)), eng="v")
+                act(c("AB", 3840 * 3 + a16, 3840 * 3 + z16), c("HZ", a16, z16), F.Abs, 0.0, 2.0)
+                for (x, y) in upto(a, z, 32):
+                    a16, z16 = 16 * x, 16 * y
+                    for terms, j in ((("WZ",), 2), (("WA",), 1), (("WZ", "WA"), 0)):
+                        o = ps(reg[0] % NA[0], 0, z16 - a16); reg[0] += 1
+                        mm([(o, idm(2.0), c("HZ", a16, z16))] + [(o, idm(-1.0), c(b, a16, z16)) for b in terms])
+                        act(c("AB", 3840 * j + a16, 3840 * j + z16), o, F.Abs, -9.0 * len(terms))
+            for h in (1, 0):
+                o = ps(3, Ks * h, Ks * h + Ks)
+                mm([(o, idm(32768.0), c(LV, k0, k1))] + compact(o, "PK8", ("WA", "WZ")[h], 16 * k0, Ks))
+            tag[0] = "f%d" % s
+            FL, TOP, TT = c("FL", 2 * k0, 2 * k1), c("TOP", 2 * k0, 2 * k1), c("TT", k0, k1)
+            ts(FL, dec, 1.0 / 128, 1536 + 8.5 / 128, A.mult, A.add); ev(c("FF", 2 * k0, 2 * k1), dec, 72.0 + 64 + base - 2048 + 128 * 1536)
+            tt(c("MX", 0, Ks), c("FL", 2 * k0, 2 * k0 + Ks), c("FL", 2 * k0 + Ks, 2 * k1), A.max); ts(TT, c("MX", 0, Ks), 1716.0, None, A.is_gt)
+            act(TOP, e3(E, k0, k1), F.Sign, col(15))
+            for j in (3, 2, 1, 0):
+                o = ps(db, Ks * j, Ks * j + Ks)
+                mm([(o, idm(1.0), c("ETA", 128 * j, 128 * j + Ks))] + ([(o, idm(2048.0), c(LV, k0, k1))] if j == 0 else []) + compact(o, "S", "AB", 3840 * j + 16 * k0, Ks))
+        def decide(s):
+            tag[0] = "d%d" % s
+            k0, k1 = part[s]; Ks = k1 - k0; db = 4 + s % 2; dec = ps(db, 0, 2 * Ks)
+            FL, TOP, TT = c("FL", 2 * k0, 2 * k1), c("TOP", 2 * k0, 2 * k1), c("TT", k0, k1)
+            ev(c("SS", 0, 3 * Ks), ps(db, 0, 3 * Ks))
+            S_ = lambda j: c("SS", Ks * j, Ks * j + Ks); P_ = lambda j: ps(db, Ks * j, Ks * j + Ks); M_ = lambda j: c("MM", Ks * j, Ks * j + Ks)
+            tt(M_(2), P_(3), S_(2), A.min); tt(M_(3), P_(3), S_(1), A.min); tt(M_(0), P_(1), S_(0), A.min); tt(M_(1), P_(2), S_(0), A.min)
+            tt(e3("PT", k0, k1), c("MM", 2 * Ks, 4 * Ks), c("MM", 0, 2 * Ks), A.is_lt)
+            sg = 1.0 if t % 2 == 0 else -1.0
+            for h in range(2):
+                mm([(ps(db, Ks * h, Ks * h + Ks), l, x) for l, x in ((ap("IF"), ap(E, h, slice(k0, k1))), (idm(8192.0 * sg), TT), (idm(1920.0), ap("PT", h, slice(k0, k1))))])
+            cs = LOO - 8192.0 if t % 2 == 0 else 8192.0; mo = A.max if t % 2 == 0 else A.min
+            tt(c("IA", 0, Ks), ps(db, 0, Ks), c("ALT", 256 * (t % 2) + k0, 256 * (t % 2) + k1), mo); ts(ap("IX", 0, slice(k0, k1)), c("IA", 0, Ks), cs, None, A.add)
+            ts(ap("IX", 1, slice(k0, k1)), ps(db, Ks, 2 * Ks), cs, float(CST if t % 2 == 0 else CST2 - LOO), A.add, mo)
+            mm([(dec, idm(-128.0), FL), (dec, idm(64.0), TOP), (dec, ap("IF"), c("FF", 2 * k0, 2 * k1))]
+               + [(ps(db, Ks * h, Ks * h + Ks), idm(2048.0), ap("PT", h, slice(k0, k1))) for h in range(2)])
+            tt(e3(En, k0, k1), dec, e3(E, k0, k1), A.max)
+            if t < 3: cp(e3(EUn, k0, k1), e3(En, k0, k1))
+        def phase_b(s):
+            tag[0] = "b%d" % s
+            k0, k1 = part[s]; Ks = k1 - k0; db = 4 + s % 2; D = lambda j, x, y: c("HZ", x, y) if j == 0 else c("AB", 3840 * (j + 1) + x, 3840 * (j + 1) + y)
+            for n, (a, z) in enumerate(upto(k0, k1, 32 if s else BP[0])):
+                a16, z16 = 16 * a, 16 * z
+                gat(D(0, a16, z16), win, ap("IX", 0, slice(a, z)))
+                how = BMODE[s][n]; bb = [7, 6, 2][:5 - NA[0]]
+                o = ps(bb[reg[1] % len(bb)], 0, z16 - a16); reg[1] += 1
+                if how == 2:
+                    o2 = o; o = ps(bb[reg[1] % len(bb)], 0, z16 - a16); reg[1] += 1
+                    gat(D(1, a16, z16), win, ap("IX", 1, slice(a, z)))
+                    mm([(o2, idm(1.0), D(0, a16, z16)), (o2, idm(-1.0), D(1, a16, z16))]); act(D(2, a16, z16), o2, F.Abs)
+                else: gtt(D(1, a16, z16), win, ap("IX", 1, slice(a, z)), D(0, a16, z16), A.subtract)
+                if how == 1: act(D(2, a16, z16), D(1, a16, z16), F.Abs)
+                if how: mm([(o, idm(0.5), c("WB", ysrc + a16, ysrc + z16)), (o, idm(0.5), D(2, a16, z16))])
+                else:
+                    ts(D(2, a16, z16), D(1, a16, z16), 0.0, None, A.max)
+                    mm([(o, idm(0.5), c("WB", ysrc + a16, ysrc + z16)), (o, idm(-0.5), D(1, a16, z16)), (o, idm(1.0), D(2, a16, z16))])
+                ev(ydst(a16, z16), o, 95.75)
+        def alive(s):
+            k0, k1 = part[s]; Ks = k1 - k0
+            y = ydst(0, 16); mm(compact(ps(3, 0, Ks), "S", y[0], y[2][0].start + 16 * k0, Ks))
+            ts(c(LVn, k0, k1), ps(3, 0, Ks), 3248.0, None, A.is_ge)
+        def cells_on():
+            tag[0] = "c"
+            Cn = C + 256
+            for a in range(0, Cn, 512):
+                z = min(Cn, a + 512); bk = a // 512; o = ps(bk, 0, z - a); lst = [(o, idm(1.0), c("WB", LOO + a, LOO + z))]
+                if a >= 512: lst.append((o, idm(-128.0), c("NXT", a - 512, z - 512)))
+                if t < 3:
+                    u = a
+                    while u < z:
+                        s0 = (u + 331 * t) % 1024; n = min(z - u, 1024 - s0); lst.append((ps(bk, u - a, u - a + n), idm(1.0), c("DR", s0, s0 + n))); u += n
+                mm(lst)
+            for a in range(0, Cn, 1024):
+                z = min(Cn, a + 1024); ts(c("XT", XO + a, XO + z), c("PS", a, z), 0.0, 63.0, A.max, A.min)
+            if t < 3: cells_ahead(t + 1)
+            else: dma(ap("yx", slice(0, 1536), p=slice(0, 128)), c("XT", XO, XO + 1536), "y")
+        def to_rows(f, src, new, q):
+            for h in range(2):
+                if new:
+                    for u in range(t): dma(rows(f, RH * h + 3073 + 256 * u, RH * h + 3329 + 256 * u), src(h, 192 + 16 * u, 208 + 16 * u), q)
+                else: dma(rows(f, RH * h + 1, RH * h + 3073), src(h, 0, 192), q if len(q) == 1 else q[h])
+        pt = lambda h, a, z: ap("PT", h, slice(a, z)); lv = lambda h, a, z: c(LVn, a, z)
+        phase_a(2); decide(2); to_rows(1, pt, True, "y"); phase_a(1); phase_b(2); decide(1); phase_a(0); alive(2); to_rows(0, lv, True, "y"); cells_on()
+        phase_b(1); alive(1); decide(0); to_rows(1, pt, False, "y")
+        tag[0] = "t"
+        if t < 3:
+            mm([(ps(0, 0, 256), ap("ONES"), ap("LIW")), (ps(0, 0, 256), idm(-8192.0), c("NXT", 256 * t, 256 * t + 256))])
+            ts(ap("LI"), ps(0, 0, 256), 3248.0, None, A.is_ge); act(ap("JK"), ap("LI"), F.Identity, acc=col(11))
+            mm(compact(ps(1, 0, 24), "PK8", "GW", 0, 24))
+            ts(ap("F2"), ps(1, 0, 24), 1.0 / 128, 1536 + 8.5 / 128, A.mult, A.add); ev(c("FF", 480, 504), ps(1, 0, 24), 72.0)
+            ts(ap("P2"), ap("OWN"), col(V128), (base - 2048) / 128 + 1536.0, A.is_ge, A.add)
+            gat(ap("GT"), c("R", 0, RH + 3088), ap("TW"))
+            mm(compact(ps(2, 0, 24), "PK", "GT", 0, 24)); ts(ap("M2"), ps(2, 0, 24), 16.0, None, A.is_ge)
+            mm([(ps(1, 0, 24), idm(-128.0), ap("F2")), (ps(1, 0, 24), idm(128.0), ap("P2")), (ps(1, 0, 24), ap("IF"), c("FF", 480, 504)), (ps(1, 0, 24), idm(2048.0), ap("M2"))])
+            tt(ap("TWF"), ps(1, 0, 24), ap("OWN"), A.max); cp(ap("OWN"), ap("TWF")); cp(ap("OWU"), ap("TWF"))
+        else:
+            for h in range(2):
+                dma(ap("ye", slice(0, 3072), p=slice(h, 16, 2)), ap(En, h, slice(0, 192)), "y")
+                for u in range(3): dma(ap("ye", slice(3072 + 256 * u, 3328 + 256 * u), p=slice(h, 16, 2)), ap(En, h, slice(192 + 16 * u, 208 + 16 * u)), "y")
+        phase_b(0); alive(0); to_rows(0, lv, False, "y")
+        if t < 3: mm([(ps(7, 0, K), ap("ONES"), c(LVn, 0, K))]); act(c("JK", 0, K), ps(7, 0, K), F.Identity, acc=col(LOLD))
+        else:
+            for r in range(16): ev(c("AB", 4096 + 192 * r, 4288 + 192 * r), c("YF", r, 3072, 16), -192.0)
+            gat(c("AB", 7168, 7936), c("YF", 3072, 3840), c("ULAST", 0, 48), -192.0)
+            dma(ap("yy", slice(0, 3840), p=slice(0, 128)), c("AB", 4096, 7936), "y")
+        tag[0] = "s"
+        for j in range(4):
+            gat(c("AB", 1024 * j, 1024 * j + 1024), c("R", 0, RH + 4112), c("OLU", 64 * j, 64 * j + 64))
+            if t < 3:
+                o = ps(4, 64 * j, 64 * j + 64)
+                mm([(o, idm(128.0), c("LI", 64 * j, 64 * j + 64))] + [(o, ap("PQ"), c("AB", 1024 * j + r, 1024 * j + 1024, 16)) for r in range(16)])
+        if t < 3: act(ap("JK"), ps(4, 0, 256), F.Relu, col(12), acc=col(LNEW))
+        for j in range(4):
+            o = ps(5, 64 * j, 64 * j + 64)
+            mm([(o, idm(1.0), c("NXT", 256 * t + 64 * j, 256 * t + 64 * j + 64))] + compact(o, "PK", "AB", 1024 * j, 64))
+        ts(c("SM", 0, 256), ps(5, 0, 256), 1.0, None, A.is_equal); ts(c("SM", 256, 512), ps(5, 0, 256), 17.0, None, A.is_equal)
+        mm([(ps(6, 0, 512), ap("ONES"), ap("SM"))])
+        act(ap("NM"), ps(6, 0, 512), F.Relu, -15.0)
+        if t < 3:
+            mm([(ps(6, 0, 256), idm(1.0), ap("LI")), (ps(6, 0, 256), idm(-1.0), c("NM", 0, 256)), (ps(6, 0, 256), idm(-1.0), c("NM", 256, 512))])
+            act(ap("ML"), ps(6, 0, 256), F.Relu)
+        mm([(ps(3, 0, 512), idm(-16384.0), ap("ONE"))] + [(ps(3, 256 * h, 256 * h + 256), ap("IF"), ap("OLD")) for h in range(2)], stop=False)
+        mm([(ps(3, 0, 512), idm(16384.0), ap("SM"))], start=False)
+        mm([(ps(0, 0, 512), ap("TF"), ap("SM"))] + [(ps(0, 256 * h, 256 * h + 256), l, x) for h in range(2)
+                                                    for l, x in ((idm(1.0), ap("IO1")), (idm(-16384.0), c("NM", 0, 256)), (idm(-16384.0), c("NM", 256, 512)))])
+        bl = "BL" if t < 3 else "BLF"
+        for h, o in enumerate((ap("TVF"), c(bl, C, C + 256))):
+            hp = lambda b: ps(b, 256 * h, 256 * h + 256); t2 = c("T2", 256 * h, 256 * h + 256); bc = c("BC", 2 * t + h, 2 * t + h + 1)
+            if t < 3: act(t2, hp(0), F.Relu, bc)
+            else: ts(t2, hp(0), bc, -1.0, A.add, A.max)
+            tt(o, hp(3), t2, A.max)
+        sca(ap(bl), ap("DL2"), ap("TVF"))
+        mm([(ps(5, 0, 16), sh("PK", r), c("NM", 256 * j + 16 * r, 256 * j + 16 * r + 16)) for j in range(2) for r in range(16)])
+        s16 = lambda j: c("S16", 16 * j, 16 * j + 16)
+        ts(s16(0), ps(5, 0, 16), 1.0, 1535.0, A.is_ge, A.mult); tt(s16(1), s16(0), ap("DLF"), A.max); cp(ap("DLM"), s16(1))
+        gat(ydst(16 * K, 16 * K + 256), c("WP", 0, 1536), ap("DLM"), 201.0)
+        ts(s16(2), ps(5, 0, 16), 1.0, None, A.is_lt); ts(s16(3), c("IO", 0, 16), col(PM16), float(base), A.add, A.add)
+        tt(ap(En, 0, slice(K, K + 16)), s16(2), ap("DLF"), A.mult); tt(ap(En, 1, slice(K, K + 16)), s16(2), s16(3), A.mult)
+        if t < 3:
+            cp(e3(EUn, K, K + 16), e3(En, K, K + 16))
+            mm([(ps(4, 0, 16), sh("PK", r), c("ML", 16 * r, 16 * r + 16)) for r in range(16)]); ts(c(LVn, K, K + 16), ps(4, 0, 16), 1.0, None, A.is_ge)
+        else:
+            gat(c("AB", 7936, 8192), c("YF", 3072, 4096), c("ULAST", 48, 64), -192.0)
+            dma(ap("yy", slice(3840, 4096), p=slice(0, 128)), c("AB", 7936, 8192), "s")
+            for h in range(2): dma(ap("ye", slice(3840, 4096), p=slice(h, 16, 2)), ap(En, h, slice(240, 256)), "ys"[h])
+            dma(ap("yl", slice(0, 1536), p=slice(0, 128)), c("BLF", 0, 1536), "y")
+    return ops
+
+
+def depend(ops):
+    seen = {}
+    for n, o in enumerate(ops):
+        deps = set()
+        acc = [(x, False) for x in o["rd"]] + [(x, True) for x in o["wr"]]
+        for x, w in acc:
+            for m, pm, cm, mw in seen.get(x[0], []):
+                clash = w or mw or (x[0] == "PS" and (len(o["alts"]) > 1 or o["alts"].keys() != ops[m]["alts"].keys()))
+                if clash and m != n and pm & x[4] and cm & x[5]: deps.add(m)
+        for x, w in acc:
+            lst = seen.setdefault(x[0], [])
+            if w: lst[:] = [e for e in lst if (e[1] & ~x[4]) or (e[2] & ~x[5])]
+            lst.append((n, x[4], x[5], w))
+        if o["kind"] == "arrive": deps = {n - 1}
+        o["deps"] = deps
+
+
+def arrange(ops, lat=120.0, far=3500.0, bias=8000.0, look=3.0, ahead=400.0, noise=0.0, seed=0, bonus={}):
+    n = len(ops); kids = [[] for o in ops]
+    for i, o in enumerate(ops):
+        for d in o["deps"]: kids[d].append(i)
+    def span(o):
+        if o["kind"] == "arrive": return far
+        return min(v[1] for v in o["alts"].values()) + (o["x"] if o["kind"] == "dma" else 0) + lat
+    pr = [0.0] * n
+    for i in range(n - 1, -1, -1):
+        same = any(ops[k]["tag"] == ops[i]["tag"] for k in kids[i])
+        pr[i] = span(ops[i]) + max([pr[k] for k in kids[i]] + [0.0]) + (0.0 if same else bonus.get(ops[i]["tag"], 0.0))
+    pr = [float(x) for x in np.array(pr) + noise * np.random.default_rng(seed).random(n)]
+    left = [len(o["deps"]) for o in ops]; est = [0.0] * n; ready = [i for i in range(n) if not left[i]]
+    free = {e: 0.0 for e in "vspqy"}; order = []; busy = {e: 0.0 for e in "vspqy"}
+    def finish(i, tm):
+        ops[i]["end"] = tm
+        for k in kids[i]:
+            est[k] = max(est[k], tm + lat); left[k] -= 1
+            if not left[k]:
+                if ops[k]["kind"] == "arrive": ops[k]["e"] = None; finish(k, est[k] + far)
+                else: ready.append(k)
+    while ready:
+        best = None
+        for e in free:
+            cand = [i for i in ready if e in ops[i]["alts"]]
+            if not cand: continue
+            t0 = max(free[e], min(est[i] for i in cand))
+            key = lambda j: (pr[j] - (bias if e == "v" and len(ops[j]["alts"]) > 1 else 0) - look * max(0.0, est[j] - t0), -j)
+            i = max([i for i in cand if est[i] <= t0 + ahead], key=key)
+            if best is None or t0 < best[0]: best = (t0, e, i)
+        t0, e, i = best
+        st = max(free[e], est[i]); cost = ops[i]["alts"][e][1]; free[e] = st + cost; busy[e] += cost
+        ops[i]["e"] = e; ops[i]["st"] = st; ready.remove(i); order.append(i)
+        finish(i, st + cost + (ops[i]["x"] if ops[i]["kind"] == "dma" else 0))
+    return order, busy
+
+
+def settle(ops, rounds=6, lat=120.0, far=3500.0, bias=1.3):
+    n = len(ops); kids = [[] for o in ops]
+    for i, o in enumerate(ops):
+        for d in o["deps"]: kids[d].append(i)
+    tail = [far if o["kind"] == "arrive" else o["x"] if o["kind"] == "dma" else 0.0 for o in ops]
+    def lay(key, back):
+        lines = {e: ([], []) for e in "vspqy"}; st = [0.0] * n; en = [0.0] * n; eng = [None] * n
+        for i in sorted(range(n), key=key):
+            o = ops[i]; t0 = max([en[d] + lat for d in (kids[i] if back else o["deps"])] + [0.0]) + (tail[i] if back else 0.0); best = None
+            for e, v in o["alts"].items():
+                a, z = lines[e]; j = int(np.searchsorted(z, t0, side="right")) if z else 0; x = t0
+                while j < len(a) and a[j] < x + v[1]: x = max(x, z[j]); j += 1
+                sc = x + v[1] * (bias if e == "v" else 1.0)
+                if best is None or sc < best[0]: best = (sc, x, e, j)
+            if best is None: st[i] = en[i] = t0
+            else:
+                x, e, j = best[1:]; lines[e][0].insert(j, x); lines[e][1].insert(j, x + o["alts"][e][1]); st[i] = x; en[i] = x + o["alts"][e][1]; eng[i] = e
+            if not back: en[i] += tail[i]
+        return st, en, eng
+    en = [o["end"] for o in ops]; top = None
+    for k in range(rounds):
+        sb, eb, x = lay(lambda i: (-en[i], -i), True)
+        st, en, eng = lay(lambda i: (-eb[i], i), False)
+        if top is None or max(en) < top[0]: top = (max(en), st, en, eng)
+    busy = {e: 0.0 for e in "vspqy"}
+    for o, s, z, e in zip(ops, top[1], top[2], top[3]):
+        o["st"] = s; o["end"] = z; o["e"] = e
+        if e: busy[e] += o["alts"][e][1]
+    return sorted([i for i in range(n) if ops[i]["e"]], key=lambda i: (ops[i]["st"], i)), busy
+
+
+def plan():
+    ops = build(); depend(ops); arrange(ops); order, busy = settle(ops)
+    count = {}; known = {e: {} for e in "vspqy"}; nd = 0; steps = []
+    for i in order:
+        o = ops[i]; e = o["e"]; kn = known[e]; need = {}
+        for d in sorted(o["deps"]):
+            od = ops[d]
+            if od["kind"] == "arrive": sig, ck = ("ar%d" % od["x"], 12), {}
+            else: sig, ck = od["sig"], od["ck"]
+            if e == "p" and od.get("e") == "p" and not any(x[0] != "PS" for x in od["wr"]): continue
+            if kn.get(sig[0], 0) < sig[1]: need[sig[0]] = (max(sig[1], need.get(sig[0], (0,))[0]), ck if sig[1] >= need.get(sig[0], (0,))[0] else need[sig[0]][1])
+        for s in list(need):
+            if any(s2 != s and need[s2][1].get(s, 0) >= need[s][0] for s2 in need): need.pop(s)
+        for s, (v, ck) in need.items():
+            kn[s] = v
+            for s2, v2 in ck.items(): kn[s2] = max(kn.get(s2, 0), v2)
+        if o["kind"] == "dma": o["sig"] = ("d%d" % nd, 16); nd += 1
+        elif o["kind"] == "send": o["sig"] = ("ls%d" % o["x"], 12)
+        else: count[e] = count.get(e, 0) + 1; o["sig"] = (e, count[e])
+        o["ck"] = dict(kn)
+        steps.append((o, [(s, v[0]) for s, v in need.items()]))
+    last = dict(count)
+    for j in range(nd): last["d%d" % j] = 16
+    for t in range(4): last["ls%d" % t] = 12; last["ar%d" % t] = 12
+    seen = {}
+    for kn in known.values():
+        for s, v in kn.items(): seen[s] = max(seen.get(s, 0), v)
+    return steps, [(s, v) for s, v in last.items() if seen.get(s, 0) < v], ops, busy
+
+
+PLAN = []
+
+
+def rank_program(g, core, T, topo):
+    rank = T.rank_of(core)
+    if rank is None:
+        return
+    if not PLAN: PLAN.append(plan())
+    steps, last = PLAN[0][:2]
+    queue = {"v": g.vector, "s": g.scalar, "p": g.tensor, "q": g, "y": g.sync}
+
+    def r(x):
+        if isinstance(x, str): return rank
+        if not isinstance(x, tuple): return x
+        return T[x[0]][(x[1],) + x[2]]
+
+    for o, waits in steps:
+        for s, v in waits: queue[o["e"]].wait_ge(T.sem[s], v)
+        if o["kind"] == "send":
+            t = o["x"]; peers = [(d, T.cores[(rank + d) % 4]) for d in (1, 2, 3)]
+            used = []; tr = []
+            for d, peer in sorted(peers, key=lambda x: topo.die(x[1]) == topo.die(core)):
+                en = topo.engines(core, peer); en = [e for e in en[0::2] + en[1::2] if e not in used][:4]; used += en
+                rid, pid = topo.addr(peer)[:2]
+                tr.append(RemoteDMATransfer(dst_ids=[DstId(rid=rid, pnc=pid)], dma_engine_mask=sum(1 << e for e in en), remote_sem=T.sem["ar%d" % t],
+                                            src=T["SN%d" % (t % 2)][:, d - 1], dst=T["LN%d" % t][:, 3 - d]))
+            g.remote_dma_fused(tr, local_sem=T.sem["ls%d" % t])
+        else:
+            o["alts"][o["e"]][0](g, r).then_inc(T.sem[o["sig"][0]], 16 if o["kind"] == "dma" else 1)
+    for s, v in last: g.sync.wait_ge(T.sem[s], v)

@@ -7,36 +7,34 @@ F = ActivationFunctionType
 THETA, DELTA = (470, 540, 620, 560), (8, 6, 9, 7)
 BF, HF, F32, I32, U16 = "bfloat16", "float16", "float32", "int32", "uint16"
 CST, LOO, HIO, CST2, YBO, WBW = 3584, 3600, 5520, 7440, 7456, 11296
-XO = 1280
-RH = 8192
+RO, RW_ = 192, 4032
+FO = 1500
+NMAT = 34
 SB = {
-    "Y0N": ([3072], BF), "WB": ([WBW], BF), "YF": ([4096], BF), "HH": ([1920], BF), "WP": ([1920], F32), "XT": ([XO + 2560], BF),
-    "UH": ([3840], HF), "WA": ([3840], HF), "WZ": ([3840], HF), "HZ": ([3840], BF), "AB": ([4 * 3840], BF),
-    "R": ([RH + 4112], BF), "BL": ([1792], F32), "BLF": ([1792], F32), "VD": ([1792], BF), "DR": ([1024], BF),
-    "DLD": ([1536], BF), "BTG": ([1280], BF), "NXT": ([1024], BF), "TI": ([1024], I32), "BC": ([8], F32), "IO1": ([256], BF),
-    "EI": ([2, 192], I32), "ED": ([2, 192], I32), "DG": ([4, 192], BF), "BI": ([512], I32), "SI": ([24], I32),
-    "E0": ([2, 256], F32), "E1": ([2, 256], F32), "EU0": ([2, 256], U16), "EU1": ([2, 256], U16),
-    "LV0": ([256], BF), "LV1": ([256], BF), "PT": ([2, 256], BF), "IX": ([2, 256], U16),
-    "SS": ([360], F32), "MM": ([480], F32), "FL": ([480], HF), "FF": ([504], F32), "MX": ([120], HF), "TT": ([256], BF), "TOP": ([480], BF),
-    "IA": ([120], F32), "JK": ([256], BF), "SX": ([80], F32), "CA": ([80], BF), "CU": ([80], F32), "PL": ([80], F32), "ND": ([80], F32),
-    "B1": ([80], F32), "B2": ([80], F32), "B3": ([80], F32), "B4": ([80], F32), "UHI": ([80], U16), "ULO": ([80], U16), "UBT": ([80], U16), "USC": ([80], U16),
-    "COL": ([32], F32), "CI": ([8], I32), "DL2": ([16], U16), "DLF": ([16], F32), "DLM": ([16], U16), "S16": ([64], F32), "ULAST": ([64], U16),
-    "OLD": ([256], F32), "OLU": ([512], U16), "LIW": ([256], BF), "LI": ([256], BF), "SM": ([512], BF), "NM": ([512], BF),
-    "ML": ([256], BF), "T1": ([512], F32), "T2": ([512], F32), "TVF": ([256], F32),
-    "TW": ([24], U16), "TWF": ([24], F32), "OWN": ([24], F32), "OWU": ([24], U16), "GT": ([384], BF), "GW": ([384], HF), "F2": ([24], HF), "P2": ([24], HF), "M2": ([24], BF),
-    "ONE": ([512], BF), "ONES": ([128], BF), "TRI": ([128], BF), "S": ([144], BF), "PK": ([144], BF), "PK8": ([144], BF), "PKA": ([128], BF),
-    "TM": ([128], BF), "TF": ([128], BF), "ID": ([15 * 128], BF), "IF": ([128], F32), "ONF": ([128], F32), "PQ": ([128], BF), "ETA": ([512], BF), "BT": ([272], BF),
-    "VC": ([256], F32), "ALT": ([512], F32), "VM": ([80], F32), "IO": ([512], F32), "ZE": ([80], F32),
+    "Y0N": ([3072], BF), "WB": ([WBW], BF), "YF": ([4096], BF), "HH": ([1920], BF), "WP": ([1920], F32), "XT": ([1536], BF), "P2": ([1280], BF),
+    "UH": ([3840], HF), "WA": ([3840], HF), "WZ": ([3840], HF), "HZ": ([3840], BF), "AB": ([4 * 3840], BF), "D": ([3 * 3840], BF), "SG": ([4096], BF),
+    "R": ([RW_], BF), "BL": ([1536], F32), "DR": ([1024], BF), "FR": ([1024], BF), "BTG": ([1280], BF), "NXT": ([1024], BF), "BC": ([4], F32), "IO1": ([512], BF),
+    "EI": ([2, 192], I32), "BI": ([512], I32), "SI": ([24], I32), "NSW": ([192], F32), "SWF": ([192], F32), "EB": ([192], BF), "FC": ([2, 256], HF),
+    "E0": ([2, 256], HF), "E1": ([2, 256], HF), "EF": ([2, 256], F32), "EU0": ([2, 256], U16), "EU1": ([2, 256], U16),
+    "LV0": ([256], BF), "LV1": ([256], BF), "EQ": ([3, 256], BF), "TR": ([2, 256], BF), "IX": ([2, 256], U16),
+    "SS": ([4, 128], F32), "FL": ([2, 256], HF), "FF": ([2, 240], F32), "TT": ([256], BF), "IA": ([128], F32),
+    "JK": ([16, 80], BF), "SX": ([80], F32), "NSX": ([80], F32), "CA": ([80], BF), "CU": ([80], F32), "PL": ([96], F32), "UBT": ([80], U16),
+    "COL": ([32], F32), "QB": ([2], BF), "CI": ([8], I32), "OH": ([16], F32), "ACC": ([16], F32), "KI": ([16], U16), "NB": ([16], F32), "KT": ([96], BF), "KD": ([256], BF), "MK": ([256], BF),
+    "DM": ([16], F32), "DL2": ([16], U16), "VR": ([16], HF), "DLM": ([16], U16), "NC": ([32], BF), "S16": ([64], F32), "NR": ([64], HF), "ULAST": ([64], U16),
+    "OLD": ([256], F32), "OLU": ([256], U16), "LIW": ([272], BF), "LI": ([256], BF), "SM": ([3, 256], BF), "NM": ([2, 256], BF), "T2": ([512], F32), "TVF": ([256], F32),
+    "TW": ([24], U16), "TA": ([24], F32), "TB": ([24], F32), "OWN": ([24], F32), "OWU": ([24], U16), "GT": ([384], BF),
+    "ONE": ([512], BF), "MAT": ([NMAT * 128], BF), "MF": ([4 * 128], F32), "SEL": ([11 * 144], BF), "ETA": ([3, 256], BF),
+    "BT": ([272], BF), "BD": ([2, 256], BF), "DT": ([4 * 272], BF), "VC": ([256], F32), "ALT": ([512], F32), "IO": ([16], F32), "IOM": ([256], F32), "ZE": ([80], F32),
     "SN0": ([3, 256], BF), "SN1": ([3, 256], BF), "LN0": ([3, 256], BF), "LN1": ([3, 256], BF), "LN2": ([3, 256], BF), "LN3": ([3, 256], BF),
 }
 SCRATCH = {k: ("sbuf", [128] + v[0], v[1]) for k, v in SB.items()}
 SCRATCH["PS"] = ("psum", [128, 4096], F32)
-NDMA = 84
+NDMA = 120
 SEMAPHORES = ["v", "s", "p", "q"] + ["ar%d" % t for t in range(4)] + ["ls%d" % t for t in range(4)] + ["d%d" % i for i in range(NDMA)]
-IDW = (1.0, -1.0, 2.0, 0.5, -0.5, 128.0, -128.0, 64.0, 32768.0, 2048.0, 1920.0, 8192.0, -8192.0, 16384.0, -16384.0)
-G_CYC, S_CYC = 1.5, 3.8
-BMODE = [[1] * 4, [1] * 4, [1] * 4]
-NA, LAST, GP, BP, FIRST = [3], [64], [48], [32], [64, 72, 80, 80]
+SELS = ("S", "PKW", "PKR", "PKT", "P0", "P16", "RW", "S2", "SC", "S4", "SN")
+P = {"g": 1.4, "s": 3.0, "ov": 15.0, "gp": 32, "aw": 32, "abank": [0, 1, 2], "bbank": [5, 6, 7], "bw": [16, 32, 32], "last": 64, "mid": [64, 64, 64, 64],
+     "bmode": [1, 1, 1], "relu": [0, 0, 0], "lat": 230.0, "far": 3000.0, "dma": 1300.0, "bias": 2.0, "war": 0, "direct": 1}
+CY, XB, YB = 0.83, 3, 4
 
 
 def bits(idx):
@@ -65,7 +63,7 @@ def build():
     def add(alts, rd, wr, kind="c", extra=None):
         ops.append({"alts": alts, "rd": [x for x in rd if isinstance(x, tuple) and x[0] in SCRATCH], "wr": [x for x in wr if x[0] in SCRATCH], "kind": kind, "x": extra, "tag": tag[0]})
 
-    def vc(n, k): return 70 + max(64, n * k) * 1.0
+    def vc(n, k): return P["ov"] + max(64, n * k) * CY
     def half(o, i): return 0.5 if size(o) == 2 and size(i) == 2 else 1.0
     def ts(o, i, s1, s2, op0, op1=None):
         if op1 is None: f = lambda g, r: g.vector.tensor_scalar(r(o), r(i), r(s1), None, op0)
@@ -75,424 +73,434 @@ def build():
         k = 1 if "PS" in (i0[0], i1[0]) else 2
         add({"v": (lambda g, r: g.vector.tensor_tensor(r(o), r(i0), r(i1), op), vc(o[3], k))}, [i0, i1], [o])
     def cp(o, i): add({"v": (lambda g, r: g.vector.tensor_copy(r(o), r(i)), vc(o[3], half(o, i)))}, [i], [o])
-    def ms(o, v): add({"v": (lambda g, r: g.vector.memset(r(o), v), vc(o[3], size(o) / 4.0))}, [], [o])
+    def scan(o, i): z = c("ZE", 0, o[3]); add({"v": (lambda g, r: g.vector.tensor_tensor_scan(r(o), r(i), r(z), 0.0, A.add, A.add), vc(o[3], 1))}, [i, z], [o])
+    def fill(o, v, eng="vq"):
+        alts = {}
+        if "v" in eng: alts["v"] = (lambda g, r: g.vector.memset(r(o), v), vc(o[3], size(o) / 4.0))
+        if "q" in eng and v == int(v):
+            alts["q"] = (lambda g, r: g.iota(r(o), [[0, o[3]]], int(v), 0, allow_small_or_imprecise_dtypes=True), 150 + 2 * CY * o[3])
+        add(alts, [], [o])
     def act(o, i, fn, bias=0.0, scale=1.0, acc=None):
-        add({"s": (lambda g, r: g.scalar.activation(r(o), r(i), fn, bias=r(bias), scale=scale, accum_out=None if acc is None else r(acc)), vc(o[3], 1) + 20)},
+        add({"s": (lambda g, r: g.scalar.activation(r(o), r(i), fn, bias=r(bias), scale=scale, accum_out=None if acc is None else r(acc)), vc(o[3], 1) + (20 if acc else 0))},
             [i, bias], [o] + ([acc] if acc else []))
     def ev(o, i, add_=0.0, mul=1.0, eng="vs"):
         alts = {}
         if "v" in eng: alts["v"] = (lambda g, r: g.vector.tensor_scalar(r(o), r(i), mul, add_, A.mult, A.add), vc(o[3], half(o, i)))
-        if "s" in eng: alts["s"] = (lambda g, r: g.scalar.activation(r(o), r(i), F.Identity, bias=add_, scale=mul), vc(o[3], 1) + 20)
+        if "s" in eng: alts["s"] = (lambda g, r: g.scalar.activation(r(o), r(i), F.Identity, bias=add_, scale=mul), vc(o[3], 1))
         add(alts, [i], [o])
+    def relu(o, i, bias):
+        add({"v": (lambda g, r: g.vector.tensor_scalar(r(o), r(i), bias, 0.0, A.add, A.max), vc(o[3], half(o, i))),
+             "s": (lambda g, r: g.scalar.activation(r(o), r(i), F.Relu, bias=bias), vc(o[3], 1))}, [i], [o])
+    def gc_(n, e): return (50 if e == "v" else 65) + n * P["g"] * CY
     def gat(o, w, off, add_=0.0, eng="vs"):
         alts = {}
         if "v" in eng:
-            if add_: alts["v"] = (lambda g, r: g.vector.tensor_scalar(r(o), r(w).indirect(r(off)), add_, None, A.add), vc(o[3], G_CYC))
-            else: alts["v"] = (lambda g, r: g.vector.tensor_copy(r(o), r(w).indirect(r(off))), vc(o[3], G_CYC))
-        if "s" in eng: alts["s"] = (lambda g, r: g.scalar.activation(r(o), r(w).indirect(r(off)), F.Identity, bias=add_), vc(o[3], G_CYC) + 20)
+            if add_: alts["v"] = (lambda g, r: g.vector.tensor_scalar(r(o), r(w).indirect(r(off)), add_, None, A.add), gc_(o[3], "v"))
+            else: alts["v"] = (lambda g, r: g.vector.tensor_copy(r(o), r(w).indirect(r(off))), gc_(o[3], "v"))
+        if "s" in eng: alts["s"] = (lambda g, r: g.scalar.activation(r(o), r(w).indirect(r(off)), F.Identity, bias=add_), gc_(o[3], "s"))
         add(alts, [w, off], [o])
     def gtt(o, w, off, i1, op):
-        add({"v": (lambda g, r: g.vector.tensor_tensor(r(o), r(w).indirect(r(off)), r(i1), op), vc(o[3], G_CYC))}, [w, off, i1], [o])
+        add({"v": (lambda g, r: g.vector.tensor_tensor(r(o), r(w).indirect(r(off)), r(i1), op), gc_(o[3], "v"))}, [w, off, i1], [o])
     def sca(w, off, i):
-        add({"v": (lambda g, r: g.vector.tensor_copy(r(w).indirect(r(off)), r(i)), vc(i[3], S_CYC))}, [off, i, w], [w])
+        add({"v": (lambda g, r: g.vector.tensor_copy(r(w).indirect(r(off)), r(i)), 50 + i[3] * P["s"] * CY)}, [off, i, w], [w])
     def mm(lst, start=True, stop=True):
         def f(g, r):
             for j, (o, l, x) in enumerate(lst): ins = g.tensor.matmul(r(o), r(l), r(x), start and j == 0, stop and j == len(lst) - 1)
             return ins
-        add({"p": (f, 40 + sum(max(64, x[3]) * 0.5 * (4 if size(x) == 4 else 1) for o, l, x in lst))}, [y for o, l, x in lst for y in (l, x)], [o for o, l, x in lst])
+        add({"p": (f, sum(max(64, x[3]) * 0.42 * (4 if size(x) == 4 else 1) for o, l, x in lst))}, [y for o, l, x in lst for y in (l, x)], [o for o, l, x in lst])
     def iota(o, pat, base, cm):
         fl = SCRATCH[o[0]][2] != I32
         if fl: f = lambda g, r: g.iota(r(o), pat, base, cm, allow_small_or_imprecise_dtypes=True)
         else: f = lambda g, r: g.iota(r(o), pat, base, cm)
-        add({"q": (f, 150 + 2.0 * o[3])}, [], [o])
+        add({"q": (f, 150 + 2 * CY * o[3])}, [], [o])
     def sel(o, i, pat, op, base, cm):
-        add({"q": (lambda g, r: g.affine_select(r(o), r(i), pat, op, 0.0, base, cm), 190 + 2.0 * o[3])}, [i], [o])
+        add({"q": (lambda g, r: g.affine_select(r(o), r(i), pat, op, 0.0, base, cm), 170 + 2 * CY * o[3])}, [i], [o])
     def dma(o, i, q="y", nbytes=None):
         x = i if i[0] in SCRATCH else o
         nb = nbytes or x[3] * size(x) * 128
-        fs = {"y": lambda g, r: g.sync.dma_start(r(o), r(i)), "s": lambda g, r: g.scalar.dma_start(r(o), r(i)), "q": lambda g, r: g.dma_start(r(o), r(i))}
-        add({e: (fs[e], 1000 if e == "q" else 120) for e in q}, [i], [o], "dma", 1900 + nb / 180.0)
+        fs = {"y": lambda g, r: g.sync.dma_start(r(o), r(i)), "s": lambda g, r: g.scalar.dma_start(r(o), r(i))}
+        add({e: (fs[e], 100) for e in q}, [i], [o], "dma", P["dma"] + nb / 190.0)
     def ps(bank, a, b, s=1): return c("PS", 512 * bank + a, 512 * bank + b, s)
-    def idm(w): j = IDW.index(w); return c("ID", 128 * j, 128 * j + 128)
-    def sh(buf, r): return c(buf, 15 - r, 143 - r)
+    mats = {}; fmats = {}
+    def mat(kind, w=1.0):
+        if (kind, w) not in mats:
+            j = len(mats); mats[kind, w] = c("MAT", 128 * j, 128 * j + 128)
+            if w != 1.0:
+                keep = tag[0]; tag[0] = "i"; ev(mats[kind, w], mat(kind), 0.0, w); tag[0] = keep
+        return mats[kind, w]
+    def fmat(kind, w):
+        if (kind, w) not in fmats:
+            j = len(fmats); fmats[kind, w] = c("MF", 128 * j, 128 * j + 128)
+            keep = tag[0]; tag[0] = "i"; ev(fmats[kind, w], mat(kind), 0.0, w); tag[0] = keep
+        return fmats[kind, w]
+    def idm(w): return mat("I", float(w))
+    def sh(name, r): j = 144 * SELS.index(name); return c("SEL", j + 15 - r, j + 143 - r)
     def col(j): return c("COL", j, j + 1)
     def compact(out, m, buf, a, n):
         return [(out, sh(m, r), c(buf, a + r, a + 16 * n, 16)) for r in range(16)]
-    def rows(f, a, b): return ap("R", slice(a, b), p=slice(f, 128, 16))
-    PM, PM16, W16, W2K, M0, M1, LOLD, LNEW, THR, V128 = range(10)
+    def across(out, m, buf, a, n=16):
+        return [(out, sh(m, r), c(buf, a + n * r, a + n * r + n)) for r in range(16)]
+    def e3(b, a, z, n=2): return ap(b, slice(0, n), slice(a, z))
+    PM, PM16, WA_, WB_, WC_, WD_, WE_, THR, LIA, LOST, CB_, LQ, LO_, HI_, WF_, WG_, WH_, LA = range(18)
+    def oh(j): return c("OH", j, j + 1)
+    LW = P["last"]; MW = 192 - LW; B0 = 16 * MW
+    runs = [(B0, 3072, 0, LW), (0, B0, LW, 192)] + [(3072 + 256 * u, 3328 + 256 * u, 192 + 16 * u, 208 + 16 * u) for u in range(4)]
 
-    for h in range(2): dma(ap("EI", h, slice(0, 192)), ap("en0", slice(0, 3072), p=slice(h, 16, 2)), "ys"[h])
-    dma(c("Y0N", 0, 3072), ap("y0", slice(0, 3072), p=slice(0, 128)), "y")
-    dma(c("XT", XO, XO + 512), ap("x0", slice(0, 512), p=slice(0, 128)), "s")
+    for j in range(4): dma(c("Y0N", 768 * j, 768 * j + 768), ap("y0", slice(768 * j, 768 * j + 768), p=slice(0, 128)), "ys"[j % 2])
+    for h in range(2):
+        for a, z, k0, k1 in runs[:2]: dma(ap("EI", h, slice(k0, k1)), ap("en0", slice(a, z), p=slice(h, 16, 2)), "ys"[h])
+    dma(c("XT", 0, 512), ap("x0", slice(0, 512), p=slice(0, 128)), "s")
     dma(ap("SI"), ap("snd", slice(0, 24), p=slice(0, 128)), "s")
     dma(ap("BI"), ap("bl0", slice(0, 512), p=slice(0, 128)), "y")
-    ms(ap("ONE"), 1.0)
+    fill(ap("ONE"), 1.0, "v")
     iota(c("CI", 0, 1), [[1, 1]], 0, 1)
-    sel(ap("TRI"), c("ONE", 0, 128), [[-16, 8], [0, 16]], A.is_ge, 0, 1)
-    sel(ap("ONES"), ap("TRI"), [[16, 8], [0, 16]], A.is_ge, 15, -1)
-    sel(idm(1.0), c("ONE", 0, 128), [[-1, 128]], A.is_equal, 0, 1)
-    sel(ap("TRI"), ap("ONES"), [[1, 128]], A.is_gt, 0, -1)
-    ts(c("CI", 1, 2), c("CI", 0, 1), 15, None, A.bitwise_and)
-    cp(col(PM), c("CI", 1, 2))
+    ONES, TRI, TM, TF, HOLE = mat("O"), mat("T"), mat("M"), mat("F"), mat("H")
+    sel(TRI, c("ONE", 0, 128), [[-16, 8], [0, 16]], A.is_ge, 0, 1)
+    sel(ONES, TRI, [[16, 8], [0, 16]], A.is_ge, 15, -1)
+    sel(idm(1), c("ONE", 0, 128), [[-1, 128]], A.is_equal, 0, 1)
+    sel(TRI, ONES, [[1, 128]], A.is_gt, 0, -1)
+    ts(c("CI", 1, 2), c("CI", 0, 1), 15, None, A.bitwise_and); cp(col(PM), c("CI", 1, 2))
+    iota(ap("IO"), [[1, 16]], 0, 0)
+    ts(ap("OH"), ap("IO"), col(PM), None, A.is_equal)
+    fill(ap("SEL"), 0.0, "v")
+    def mksel(name, w1, w2=None):
+        j = 144 * SELS.index(name); o = c("SEL", j + 15, j + 143, 16); i = (ONES[0], ONES[1], (slice(ONES[2][0].start, ONES[2][0].stop, 16),), 8, ONES[4], ONES[5])
+        if w2 is None: ts(o, i, w1, None, A.mult)
+        else: ts(o, i, w1, w2, A.mult, A.mult)
+    mksel("S", 1.0); mksel("P0", oh(0)); mksel("P16", oh(0), 16.0)
+    ts(col(WA_), oh(1), 16.0, oh(0), A.mult, A.add); mksel("PKW", col(WA_), 256.0)
+    ts(col(WB_), col(PM), 2.0, None, A.is_lt); mksel("PKT", col(WB_))
+    ts(col(WC_), oh(2), 1024.0, col(WB_), A.mult, A.add); ts(col(WD_), oh(3), 2048.0, col(WC_), A.mult, A.add); mksel("PKR", col(WD_))
+    ts(col(WE_), col(PM), -256.0, None, A.add); mksel("RW", col(WE_))
+    if any(P["relu"]): mksel("S4", 4.0); mksel("SN", -2.0)
+    if P["direct"]:
+        mksel("S2", 2.0); ts(col(WF_), oh(0), -6400.0, None, A.mult); ts(col(WG_), oh(1), -95.0, col(WF_), A.mult, A.add); mksel("SC", col(WG_))
+        ts(col(WH_), col(PM), 3.0, None, A.not_equal); ts(HOLE, idm(1), col(WH_), None, A.mult)
+        ts(col(LO_), oh(3), 9999.0, -10000.0, A.mult, A.add); ts(col(HI_), oh(3), -9999.0, 10000.0, A.mult, A.add)
+    tt(TM, TRI, ONES, A.subtract); tt(TM, TM, idm(-4096), A.min)
+    tt(TF, TRI, idm(1), A.subtract)
     ts(col(PM16), col(PM), 16.0, None, A.mult)
-    ts(col(M0), col(PM), 0.0, None, A.is_equal); ts(col(M1), col(PM), 1.0, None, A.is_equal)
-    ts(col(W16), col(M1), 16.0, col(M0), A.mult, A.add); ts(col(W2K), col(W16), 128.0, None, A.mult)
-    ms(ap("S"), 0.0); cp(c("S", 15, 143, 16), c("ONES", 0, 128, 16))
-    ts(ap("PK"), ap("S"), col(W16), None, A.mult); ts(ap("PK8"), ap("S"), col(W2K), None, A.mult); ts(ap("PKA"), ap("ONES"), col(W16), None, A.mult)
-    for w in IDW[1:]: ev(idm(w), idm(1.0), 0.0, w)
-    ev(ap("IF"), idm(1.0))
-    tt(ap("TM"), ap("TRI"), ap("ONES"), A.subtract); ts(c("JK", 0, 128), idm(1.0), -4096.0, None, A.mult); tt(ap("TM"), ap("TM"), c("JK", 0, 128), A.min)
-    tt(c("JK", 128, 256), ap("TRI"), idm(1.0), A.subtract); ev(ap("TF"), c("JK", 128, 256), 0.0, 16384.0)
-    iota(c("T2", 504, 512), [[256, 4], [RH, 2]], 3072, 0); ts(col(10), col(PM), -16384.0, None, A.mult); ts(ap("BC"), c("T2", 504, 512), col(10), None, A.add)
-    ts(c("BC", 6, 7), c("BC", 6, 7), -1.0, None, A.add); ts(c("BC", 7, 8), c("BC", 7, 8), -1.0 - RH, None, A.add)
-    iota(ap("IO1"), [[1, 256]], 1, 0)
-    ms(c("R", 0, 3088), 0.0)
-    for a in range(0, 3088, 512): ev(c("R", RH + a, RH + min(a + 512, 3088)), c("ONE", 0, min(512, 3088 - a)), 0.0, 0.0, "s")
-    ms(ap("ZE"), 0.0)
-    for j, e in enumerate((-2048.0, 0.3125, 0.53125, 0.65625)): ms(c("ETA", 128 * j, 128 * j + 128), e)
-    ms(c("WB", CST, CST + 16), 192.0); ms(c("WB", CST2, CST2 + 16), 192.0); ms(c("WP", 1528, 1536), -9.0); ms(c("BL", 1536, 1792), 0.0)
-    iota(c("IO", 0, 256), [[16, 256]], 0, 0); ts(ap("VC"), c("IO", 0, 256), col(PM), None, A.add)
-    iota(ap("VD"), [[0, 112], [1, 16]], 0, 0); iota(c("HZ", 0, 1792), [[1, 112], [0, 16]], 0, 0)
-    dma(ap("VD", slice(0, 1792), p=slice(1, 128, 16)), ap("HZ", slice(0, 1792), p=slice(1, 128, 16)), "y", 30000)
-    iota(c("T1", 0, 272), [[0, 17], [1, 16]], -8, 0); iota(c("T2", 0, 384), [[0, 3], [1, 8], [0, 16]], -4, 0)
-    ts(c("T1", 0, 272), c("T1", 0, 272), col(M0), 1.0 / 128, A.mult, A.mult); ts(c("T2", 0, 272), c("T2", 0, 272), col(M1), 1.0 / 128, A.mult, A.mult)
-    tt(ap("BT"), c("T1", 0, 272), c("T2", 0, 272), A.add)
-    iota(ap("IO"), [[1, 512]], 0, 0)
-    ev(c("ALT", 0, 256), ap("VC"), 8192.0 - LOO); ev(c("ALT", 256, 512), ap("VC"), YBO - LOO - 8192.0); ev(ap("VM"), c("VC", 0, 80), 256.0 - 4095)
-    iota(ap("S16"), [[256, 4], [1, 16]], 0, 0); ts(ap("ULAST"), ap("S16"), col(PM16), None, A.add)
-    e3 = lambda b, a, z: ap(b, slice(0, 2), slice(a, z))
-    for dgt, (s1, op) in enumerate(((15, A.bitwise_and), (4, A.logical_shift_right))):
-        ts(ap("ED"), ap("EI"), s1, None, op); cp(ap("DG", slice(2 * dgt, 2 * dgt + 2), slice(0, 192)), ap("ED"))
-        for h in range(2): dma(rows(dgt, RH * h + 1, RH * h + 3073), ap("DG", 2 * dgt + h, slice(0, 192)), "ys"[h])
-    cp(e3("E0", 0, 192), ap("EI")); cp(e3("EU0", 0, 192), ap("EI"))
-    for d in range(1, 4):
-        o, i = c("TW", 8 * d - 8, 8 * d), c("SI", 8 * d - 8, 8 * d)
-        add({"v": (lambda g, r, o=o, i=i, d=d: g.vector.tensor_scalar(r(o), r(i), 1.0 + (0 if (r("rank") + d) % 4 > r("rank") else RH), None, A.add), 140)}, [i], [o])
-    gat(ap("GT"), c("R", 0, RH + 3088), ap("TW"))
-    mm(compact(ps(6, 0, 24), "PK", "GT", 0, 24))
-    cp(ap("OWU"), ps(6, 0, 24)); ev(ap("OWN"), ps(6, 0, 24))
-    mm([(ps(7, 0, 192), sh("S", r), c("Y0N", 192 * r, 192 * r + 192)) for r in range(16)])
-    ts(c("LV0", 0, 192), ps(7, 0, 192), 176.0, None, A.is_ge)
-    mm([(ps(7, 0, 192), ap("ONES"), c("LV0", 0, 192))])
-    act(c("JK", 0, 192), ps(7, 0, 192), F.Identity, acc=col(LOLD))
-    ev(ap("ONF"), ap("ONES"), 0.0, -1.0); ms(ap("PQ"), 0.0); tt(col(13), col(M0), col(M1), A.subtract); tt(col(14), col(M0), col(M1), A.add)
-    ts(c("PQ", 0, 128, 16), c("ONES", 0, 128, 16), col(13), None, A.mult); ts(c("PQ", 1, 128, 16), c("ONES", 0, 128, 16), col(14), None, A.mult)
-    ts(col(12), col(M1), -16.0, -143.0, A.mult, A.add)
+    iota(c("T2", 0, 4), [[256, 4]], 3071, 0); ts(col(CB_), col(PM), -16384.0, None, A.mult); ts(ap("BC"), c("T2", 0, 4), col(CB_), None, A.add)
+    iota(ap("IO1"), [[0, 2], [1, 256]], 1, 0); iota(ap("IOM"), [[1, 256]], -4095, 0); iota(ap("KT"), [[1, 96]], 0, 0)
+    for a in range(0, RW_, 1008): fill(c("R", a, a + 1008), 0.0)
+    fill(ap("ZE"), 0.0); fill(ap("PL"), 0.0); fill(c("LIW", 256, 272), 192.0)
+    fill(ap("ETA", 2, slice(0, 256)), 0.75)
+    for j in range(2): fill(ap("ETA", j, slice(192, 256)), 0.25 * (j + 1))
+    fill(c("WB", CST, CST + 16), 192.0); fill(c("WB", CST2, CST2 + 16), 192.0)
+    for a in (512, 1024): fill(c("WP", a, a + 512), -12.0); fill(c("BL", a, a + 512), -1.0); fill(c("WB", HIO + a, HIO + a + 512), 0.0)
+    for t in range(4): fill(c("DT", 272 * t, 272 * t + 256), 128.0 + DELTA[t]); fill(c("DT", 272 * t + 256, 272 * t + 272), 128.0)
+    iota(c("T2", 256, 512), [[16, 256]], 0, 0); ts(ap("VC"), c("T2", 256, 512), col(PM), None, A.add)
+    ev(c("ALT", 0, 256), ap("VC"), 4096.0 - LOO); ev(c("ALT", 256, 512), ap("VC"), YBO - LOO - 4096.0); ev(ap("NB"), c("VC", 0, 16), -0.5, -1.0)
+    fill(ap("BT"), 0.0); iota(ap("BD", 0, slice(0, 256)), [[0, 16], [1, 16]], -8, 0); iota(ap("BD", 1, slice(0, 256)), [[1, 16], [0, 16]], -8, 0)
+    for h in range(2): dma(ap("BT", slice(0, 256), p=slice(h, 128, 16)), ap("BD", h, slice(0, 256), p=slice(h, 128, 16)), "y", 4096)
+    iota(ap("S16"), [[256, 4], [1, 16]], 0, 0); ts(ap("ULAST"), ap("S16"), col(PM16), None, A.add); ts(ap("NR"), ap("S16"), col(PM16), 512.0, A.add, A.add)
+    def to_row(f, src, which):
+        for a, z, k0, k1 in which: dma(ap("R", slice(RO + a, RO + z), p=slice(f, 128, 16)), src(k0, k1), "y")
+    ei = lambda h: ap("EI", h, slice(0, 192)); e0 = lambda h: ap("E0", h, slice(0, 192))
+    ts(ap("NSW"), ei(0), 1536.0, 4096.0, A.is_lt, A.mult); tt(c("T2", 0, 192), ei(1), ap("NSW"), A.add); tt(e0(0), ei(0), c("T2", 0, 192), A.min)
+    ev(ap("EB"), e0(0), -256.0, eng="v"); to_row(0, lambda a, z: c("EB", a, z), runs[:2])
+    tt(ap("SWF"), ei(0), ap("NSW"), A.subtract); tt(e0(1), ei(1), ap("SWF"), A.max); cp(e3("EU0", 0, 192), e3("E0", 0, 192))
+    ev(ap("ETA", 0, slice(0, 192)), ap("NSW"), 0.5, -1.0 / 16384); ev(ap("ETA", 1, slice(0, 192)), ap("NSW"), 0.25, 1.0 / 16384)
+    ev(ap("FC"), ap("ONE"), 0.0, 5.0 - FO, "v"); ts(ap("EB"), e0(1), 1536.0, 16.0, A.is_ge, A.mult); ts(ap("FC", 1, slice(0, 192)), ap("EB"), 5.0 - FO, None, A.add)
+    ts(ap("TW"), ap("SI"), float(RO), None, A.add)
+    gat(ap("GT"), ap("R"), ap("TW"))
+    mm(compact(ps(6, 0, 24), "PKT", "GT", 0, 24))
+    ts(ap("OWU"), ps(6, 0, 24), 256.0, None, A.add); ev(ap("OWN"), ps(6, 0, 24), 256.0)
+    lst = across(ps(7, LW, 192), "S", "Y0N", 0, MW)
+    for j in range(4): mm(lst[4 * j:4 * j + 4], j == 0, j == 3)
+    mm(across(ps(7, 0, LW), "S", "Y0N", B0, LW))
+    act(c("LV0", 0, 192), ps(7, 0, 192), F.Sign, -175.5, acc=col(LA))
 
     def cells_ahead(t):
-        C = 512 + 256 * t; X = c("XT", XO, XO + C)
-        mm(compact(ps(0, 0, C // 16), "S", "XT", XO, C // 16)); ev(c("SX", 0, C // 16), ps(0, 0, C // 16), float(-THETA[t]))
-        ts(c("XT", XO - C, XO), X, float(DELTA[t]), 63.0, A.add, A.min)
-        o = c("XT", XO + C, XO + 2 * C); dl = float(-DELTA[t])
-        add({"v": (lambda g, r: g.vector.tensor_scalar(r(o), r(X), dl, 0.0, A.add, A.max), vc(C, 0.5)),
-             "s": (lambda g, r: g.scalar.activation(r(o), r(X), F.Relu, bias=dl), vc(C, 1) + 20)}, [X], [o])
-    cells_ahead(0)
-    for r in range(16): ev(c("WB", r, 3072, 16), c("Y0N", 192 * r, 192 * r + 192), 192.0)
-    cp(ap("TI"), c("Y0N", 0, 1024)); ts(ap("TI"), ap("TI"), 7, None, A.bitwise_and); ts(ap("DR"), ap("TI"), -3.0, None, A.add)
-    tag[0] = "h"
-    ts(ap("OLU"), ap("BI"), 1.0, None, A.add)
-    for j in range(8):
-        gat(c("YF", 1024 * (j % 4), 1024 * (j % 4) + 1024), c("R", 0, 3088), c("OLU", 64 * j, 64 * j + 64))
-        mm(compact(ps(4 + j // 4, 64 * (j % 4), 64 * (j % 4) + 64), "PK", "YF", 1024 * (j % 4), 64))
-        if j % 4 == 3: tt(c("T1", 64 * j - 192, 64 * j + 64), ps(4 + j // 4, 0, 256), c("IO", 64 * j - 192, 64 * j + 64), A.not_equal)
-    ts(ap("T1"), ap("T1"), float(RH), 1.0, A.mult, A.add); tt(c("BL", 0, 512), ap("T1"), ap("BI"), A.add)
-    late = [lambda: iota(c("R", 3088, 4112), [[0, 1024]], 0, 0), lambda: iota(c("R", RH + 3088, RH + 4112), [[0, 1024]], 0, 0)]
-
+        C = 512 + 256 * t
+        mm(compact(ps(0, 0, C // 16), "S", "XT", 0, C // 16)); ev(c("SX", 0, C // 16), ps(0, 0, C // 16), THETA[t] + 6144.0, -1.0)
+        for d in range(3): gat(ap("SN%d" % (t % 2), d, slice(0, 128)), c("XT", 0, C), c("OWU", 8 * d, 8 * d + 8))
+    def count_ahead(t):
+        o = ps(7, 0, 1); Kc = 32 + 16 * t
+        mm([(o, fmat("O", 0.5), col(LA + s)) for s in range(3 if t else 1)] + ([(o, fmat("O", 1.0 / 32), col(LIA))] if t else []))
+        ts(c("CI", 2, 3), o, 1.0 / 32, None, A.mult); ts(col(THR), c("CI", 2, 3), -32.0, o, A.mult, A.add)
+        ts(col(LQ), col(THR), 6128.5, None, A.add); ts(c("NSX", 0, Kc), c("SX", 0, Kc), col(THR), None, A.add)
+    cells_ahead(0); count_ahead(0)
+    for a, z, k0, k1 in runs[:2]:
+        for r in range(16): ev(c("WB", 16 * k0 + r, 16 * k1, 16), c("Y0N", a + (k1 - k0) * r, a + (k1 - k0) * (r + 1)), 192.0)
+    ev(ap("FR"), c("Y0N", 0, 1024), 1532.5)
+    for a in (0, 512): mm([(ps(1 + a // 512, 0, 512), idm(1), c("Y0N", a, a + 512)), (ps(1 + a // 512, 0, 512), idm(-1), c("FR", a, a + 512))])
+    ev(ap("DR"), c("PS", 512, 1536), 1533.0)
+    cp(c("BL", 0, 512), ap("BI"))
     reg = [0, 0]
-    for t in range(4):
-        C = 512 + 256 * t; Kc = C // 16; K = 192 + 16 * t; Ks = K // 2; base = 512 + 256 * t
-        E, En, EU, EUn, LV, LVn = ("E%d" % (t % 2), "E%d" % (1 - t % 2), "EU%d" % (t % 2), "EU%d" % (1 - t % 2), "LV%d" % (t % 2), "LV%d" % (1 - t % 2))
-        ysrc = 0 if t % 2 == 0 else YBO
-        ydst = (lambda a, b: c("WB", YBO + a, YBO + b), lambda a, b: c("WB", a, b), lambda a, b: c("WB", YBO + a, YBO + b), lambda a, b: c("YF", a, b))[t]
-        win = c("WB", 0, CST2) if t % 2 == 0 else c("WB", LOO, YBO + 16 * K)
-        k_ = lambda b: c(b, 0, Kc)
+    sm = lambda j, a=0, z=256: ap("SM", j, slice(a, z)); nm = lambda j: ap("NM", j, slice(0, 256))
+    hp = lambda b, h: ps(b, 256 * h, 256 * h + 256)
+    def kept(bank, kind, w, a=0, z=256):
+        return [(ps(bank, a, z), mat(kind, w), sm(0, a, z))] + [(ps(bank, 256 * h + a, 256 * h + z), mat(kind, (-w, w)[h]), sm(j, a, z)) for h in range(2) for j in (1, 2)]
+    def names(t):
+        return ("E%d" % (t % 2), "E%d" % (1 - t % 2) if t < 3 else "EF", "EU%d" % (t % 2), "EU%d" % (1 - t % 2), "LV%d" % (t % 2), "LV%d" % (1 - t % 2),
+                (lambda a, b: c("WB", YBO + a, YBO + b), lambda a, b: c("WB", a, b), lambda a, b: c("WB", YBO + a, YBO + b), lambda a, b: c("YF", a, b))[t])
+
+    def who(t):
         tag[0] = "w"
-        mm([(ps(7, 0, 1), ap("IF"), col(LOLD))] + ([(ps(7, 0, 1), ap("IF"), col(11)), (ps(7, 0, 1), ap("ONF"), col(LNEW))] if t else []))
-        ts(c("CI", 2, 3), ps(7, 0, 1), 1.0 / 32, -15.5 / 32, A.mult, A.add); ts(col(THR), c("CI", 2, 3), -32.0, ps(7, 0, 1), A.mult, A.add)
-        ts(k_("CA"), k_("SX"), col(THR), None, A.is_ge)
-        mm([(ps(1, 0, Kc), ap("ONES"), k_("CA"))]); mm([(ps(2, 0, Kc), ap("TM"), k_("CA"))])
-        add({"v": (lambda g, r, o=k_("CU"), i=ps(1, 0, Kc), z=k_("ZE"): g.vector.tensor_tensor_scan(r(o), r(i), r(z), 0.0, A.add, A.add), 150)}, [ps(1, 0, Kc), k_("ZE")], [k_("CU")])
-        tt(k_("PL"), ps(2, 0, Kc), k_("CU"), A.add)
-        ts(k_("ND"), k_("PL"), 256.0 - 4095, float(C), A.is_ge, A.mult)
-        tt(k_("B1"), k_("VC"), k_("ND"), A.add); cp(k_("UHI"), k_("B1"))
-        gat(c("WB", HIO, HIO + C), c("XT", XO - C, XO + C), k_("UHI"))
-        tt(k_("B2"), k_("VC"), k_("ND"), A.subtract); ts(k_("ULO"), k_("B2"), float(C), None, A.add)
-        gat(c("WB", LOO, LOO + C), c("XT", XO, XO + 2 * C), k_("ULO"))
+        C = 512 + 256 * t; Kc = C // 16; k_ = lambda b: c(b, 0, Kc); lost = col(LOST) if t else c("ZE", 0, 1)
+        ts(c("QB", 0, 1), lost, -1.0, col(LQ), A.mult, A.add); cp(c("QB", 1, 2), lost)
+        ts(k_("CA"), k_("NSX"), c("QB", 0, 1), c("QB", 1, 2), A.subtract, A.is_le)
+        mm([(ps(5, 0, Kc), ONES, k_("CA")), (ps(5, 0, Kc), TM, k_("CA")), (ps(5, 1, Kc), mat("M", -1.0), c("CA", 0, Kc - 1))]); mm([(ps(5, 128, 128 + Kc), ONES, k_("CA"))])
+        scan(k_("PL"), ps(5, 0, Kc))
+        ts(k_("UBT"), k_("PL"), 4095.0, 256.0, A.add, A.min)
+        scan(k_("CU"), ps(5, 128, 128 + Kc))
         SN, LN = "SN%d" % (t % 2), "LN%d" % t
         h3 = lambda b, j: ap(b, slice(0, 3), slice(128 * j, 128 * j + 128))
-        for d in range(3):
-            for j, o in enumerate((HIO, LOO)): gat(ap(SN, d, slice(128 * j, 128 * j + 128)), c("WB", o, o + C), c("OWU", 8 * d, 8 * d + 8), 9.0 * j)
+        gtt(c("P2", 0, C), c("DT", 272 * t, 272 * t + 272), k_("UBT"), c("XT", 0, C), A.add)
+        for d in range(3): gat(ap(SN, d, slice(128, 256)), c("P2", 0, C), c("OWU", 8 * d, 8 * d + 8))
         add({"q": (None, 600)}, [ap(SN)], [], "send", t)
         add({}, [], [ap(LN)], "arrive", t)
-        if t == 0:
-            for f in late: f()
-        ts(k_("UBT"), k_("PL"), 4095.0, 256.0, A.add, A.min)
         gat(c("BTG", 0, C), ap("BT"), k_("UBT"))
-        ev(c("HH", 0, C), c("WB", HIO, HIO + C), 96.0, 0.5, "v")
-        for a in range(0, C, 512):
-            z = min(C, a + 512); o = ps(a // 512, 0, z - a)
-            mm([(o, idm(1.0), c("WB", HIO + a, HIO + z)), (o, idm(-1.0), c("WB", LOO + a, LOO + z)), (o, idm(1.0), c("BTG", a, z))])
-        for a in range(0, C, 512):
-            z = min(C, a + 512); ev(c("WP", a, z), c("PS", a, z), -9.0)
-        ev(c("HH", 1536, 1920), h3(LN, 0), 96.0, 0.5, "v"); ev(c("WB", HIO + 1536, HIO + 1920), h3(LN, 0)); ev(c("WB", LOO + 1536, LOO + 1920), h3(LN, 1), -9.0)
-        tt(c("WP", 1536, 1920), h3(LN, 0), h3(LN, 1), A.subtract)
-        tag[0] = "l"
-        tt(k_("B3"), k_("PL"), k_("ND"), A.add); tt(k_("B4"), k_("B3"), k_("VM"), A.min); ts(k_("USC"), k_("B4"), 4095.0, None, A.add)
-        ev(c("DLD", 0, 256), c("VD", 1536, 1792))
-        for a in range(0, C, 256): sca(c("DLD", 0, 256 + C), c("USC", a // 16, a // 16 + 16), c("VD", a, a + 256))
-        mm(compact(ps(7, 0, 16), "PK", "DLD", 0, 16))
-        mm([(ps(7, 16, 32), sh("PK", r), c("DLD", 16 * r, 16 * r + 16)) for r in range(16)])
-        mm([(ps(7, 32, 34), ap("PKA"), c("DLD", 128, 130))])
-        cp(ap("DL2"), ps(7, 0, 16)); ts(ap("DLF"), ps(7, 16, 32), 1535.0, None, A.min); ev(col(V128), ps(7, 32, 33)); ev(col(15), ps(7, 32, 33), 0.5, -1.0)
-        ts(c("NXT", 256 * t, 256 * t + 256), c("IO", 0, 256), c("CU", Kc - 1, Kc), None, A.is_ge)
-        gat(c("WB", LOO + C, LOO + C + 256), c("WB", HIO, HIO + 1920), ap("DL2"))
-        gat(ap("OLD"), ap("BL"), ap("DL2")); cp(c("OLU", 0, 256), ap("OLD"))
-        gat(ap("LIW"), ap("WP"), ap("DL2"), 201.0)
-        gat(ap("GW"), c("WP", 0, 1536), ap("OWU"), eng="v")
-        if t == 3:
-            act(c("BLF", 0, C), c("BL", 0, C), F.Sign, 0.5 - RH); ev(c("BLF", 0, C), c("BLF", 0, C), -1.0 - RH / 2, -RH / 2.0)
-            tt(c("BLF", 0, C), c("BLF", 0, C), c("BL", 0, C), A.add); ms(c("BLF", 1536, 1792), -1.0)
-            gat(ap("OLD"), ap("BLF"), ap("DL2"))
+        def tables(a, z, x, p2, b0, b1, dig):
+            ts(c("HH", a, z), p2, 191.0, 0.5, A.min, A.mult); ts(c("WB", HIO + a, HIO + z), p2, 191.0, -128.0, A.min, A.add)
+            o = ps(b0, 0, z - a); mm([(o, idm(2), x), (o, idm(-1), p2)]); relu(c("WB", LOO + a, LOO + z), o, 128.0)
+            o = ps(b1, 0, z - a)
+            mm([(o, idm(1), c("WB", HIO + a, HIO + z)), (o, idm(-1), c("WB", LOO + a, LOO + z))] + ([(o, idm(1.0 / 256), c("BTG", a, z))] if dig else []))
+            ev(c("WP", a, z), o, -12.0)
+        for j, a in enumerate(range(0, C, 512)):
+            z = min(C, a + 512); tables(a, z, c("XT", a, z), c("P2", a, z), (6, 0, 5)[j], (7, 1, 6)[j], True)
+        tables(1536, 1920, h3(LN, 0), h3(LN, 1), 7, 5, False)
 
+    def dividers(t):
+        tag[0] = "l"
+        C = 512 + 256 * t; Kc = C // 16
+        for j in range(16): act(ap("JK", j, slice(0, Kc)), c("CU", 0, Kc), F.Sign, c("NB", j, j + 1), acc=c("ACC", j, j + 1))
+        ts(ap("KI"), ap("ACC"), -0.5, Kc / 2.0, A.mult, A.add)
+        gtt(ap("MK"), ap("PL"), ap("KI"), ap("IOM"), A.is_equal)
+        gat(ap("KD"), ap("KT"), ap("KI"))
+        mm([(ps(YB, 0, 16), fmat("I", -8.0), ap("ACC"))] + compact(ps(YB, 0, 16), "RW", "MK", 0, 16))
+        tt(ap("DM"), ps(YB, 0, 16), c("VC", 8 * t, 8 * t + 16), A.min); ts(ap("DL2"), ap("DM"), 256.0 + C // 2, None, A.add)
+        mm(across(ps(YB, 16, 32), "RW", "MK", 0) + across(ps(YB, 16, 32), "P16", "KD", 0)); ev(ap("VR"), ps(YB, 16, 32), 256.0, eng="v")
+        ts(c("NXT", 256 * t, 256 * t + 256), c("IO1", 0, 256), c("CU", Kc - 1, Kc), None, A.is_gt)
+        gat(c("WB", LOO + C, LOO + C + 256), c("WB", HIO, HIO + 1536), ap("DL2"))
+        gat(ap("OLD"), ap("BL"), ap("DL2")); ts(ap("OLU"), ap("OLD"), float(RO), None, A.add)
+        gat(c("LIW", 0, 256), c("WP", 0, 1536), ap("DL2"), 204.0)
+        if t < 3: mm([(ps(YB, 0, 256), ONES, c("LIW", 0, 256))]); act(ap("LI"), ps(YB, 0, 256), F.Sign, -3247.5, acc=col(LIA))
+
+    def bridges(t):
+        C = 512 + 256 * t; K = 192 + 16 * t; base = C
+        E, En, EU, EUn, LV, LVn, ydst = names(t)
+        ysrc = 0 if t % 2 == 0 else YBO
+        win = c("WB", 0, CST2) if t % 2 == 0 else c("WB", LOO, YBO + 16 * K)
         def cut(a, z, n):
             e = [a + 2 * ((z - a) * j // (2 * n)) for j in range(n)] + [z]
             return list(zip(e[:-1], e[1:]))
-        part = [(0, LAST[0]), (LAST[0], K - FIRST[t]), (K - FIRST[t], K)]
+        part = [(0, LW), (LW, LW + P["mid"][t]), (LW + P["mid"][t], K)]
         def upto(a, z, n): return cut(a, z, -(-(z - a) // n))
+        def slot(j):
+            pool = P[("abank", "bbank")[j]]; b = pool[reg[j] % len(pool)]; reg[j] += 1
+            return 512 * b
+        def wide(o, n, terms): mm([(c("PS", o, o + n), idm(x), c(b, a, a + n)) for x, b, a in terms])
         def phase_a(s):
             tag[0] = "a%d" % s
-            k0, k1 = part[s]; Ks = k1 - k0; db = 4 + s % 2; dec = ps(3, 0, 2 * Ks)
-            for (a, z) in ([(192, k1 - 16)] if k1 > 208 else []) + ([(k1 - 16, k1)] if k1 > 192 else []) + upto(k0, min(k1, 192), GP[0]):
+            k0, k1 = part[s]; Ks = k1 - k0
+            for (a, z) in upto(k0, min(k1, 192), P["gp"]) + ([(192, k1 - 16)] if k1 > 208 else []) + ([(k1 - 16, k1)] if k1 > 192 else []):
                 a16, z16 = 16 * a, 16 * z; n = 1536 if a >= 192 else 1920
-                gtt(c("UH", a16, z16), c("HH", 0, n), ap(EU, 0, slice(a, z)), c("WB", ysrc + a16, ysrc + z16), A.subtract)
+                gtt(c("UH", a16, z16), c("HH", 0, 1536), ap(EU, 0, slice(a, z)), c("WB", ysrc + a16, ysrc + z16), A.subtract)
+                gat(c("WA", a16, z16), c("WP", 0, 1536), ap(EU, 0, slice(a, z)), eng="v")
                 gtt(c("HZ", a16, z16), c("HH", 0, n), ap(EU, 1, slice(a, z)), c("UH", a16, z16), A.add)
                 gat(c("WZ", a16, z16), c("WP", 0, n), ap(EU, 1, slice(a, z)), eng="v")
-                gat(c("WA", a16, z16), c("WP", 0, n), ap(EU, 0, slice(a, z)), eng="v")
-                act(c("AB", 3840 * 3 + a16, 3840 * 3 + z16), c("HZ", a16, z16), F.Abs, 0.0, 2.0)
-                for (x, y) in upto(a, z, 32):
-                    a16, z16 = 16 * x, 16 * y
-                    for terms, j in ((("WZ",), 2), (("WA",), 1), (("WZ", "WA"), 0)):
-                        o = ps(reg[0] % NA[0], 0, z16 - a16); reg[0] += 1
-                        mm([(o, idm(2.0), c("HZ", a16, z16))] + [(o, idm(-1.0), c(b, a16, z16)) for b in terms])
-                        act(c("AB", 3840 * j + a16, 3840 * j + z16), o, F.Abs, -9.0 * len(terms))
-            for h in (1, 0):
-                o = ps(3, Ks * h, Ks * h + Ks)
-                mm([(o, idm(32768.0), c(LV, k0, k1))] + compact(o, "PK8", ("WA", "WZ")[h], 16 * k0, Ks))
+                if P["relu"][s]: ts(c("AB", 3840 * 3 + a16, 3840 * 3 + z16), c("HZ", a16, z16), -64.0, None, A.max)
+                else: act(c("AB", 3840 * 3 + a16, 3840 * 3 + z16), c("HZ", a16, z16), F.Abs, 128.0, 2.0)
+                for (x, y) in upto(a, z, P["aw"]):
+                    a16, z16 = 16 * x, 16 * y; n = z16 - a16; hz, wz, wa = (2, "HZ", a16), (-1, "WZ", a16), (-1, "WA", a16)
+                    for j, terms in ((1, [hz, wa]), (2, [hz, wz]), (0, [hz, wa, wz])):
+                        o = slot(0); wide(o, n, terms); act(c("AB", 3840 * j + a16, 3840 * j + z16), c("PS", o, o + n), F.Abs, 140.0 - 12 * len(terms))
+            dec = ps(XB, 0, 2 * Ks)
+            for h in (0, 1): mm(compact(ps(XB, Ks * h, Ks * h + Ks), "PKW", ("WA", "WZ")[h], 16 * k0, Ks))
             tag[0] = "f%d" % s
-            FL, TOP, TT = c("FL", 2 * k0, 2 * k1), c("TOP", 2 * k0, 2 * k1), c("TT", k0, k1)
-            ts(FL, dec, 1.0 / 128, 1536 + 8.5 / 128, A.mult, A.add); ev(c("FF", 2 * k0, 2 * k1), dec, 72.0 + 64 + base - 2048 + 128 * 1536)
-            tt(c("MX", 0, Ks), c("FL", 2 * k0, 2 * k0 + Ks), c("FL", 2 * k0 + Ks, 2 * k1), A.max); ts(TT, c("MX", 0, Ks), 1716.0, None, A.is_gt)
-            act(TOP, e3(E, k0, k1), F.Sign, col(15))
-            for j in (3, 2, 1, 0):
-                o = ps(db, Ks * j, Ks * j + Ks)
-                mm([(o, idm(1.0), c("ETA", 128 * j, 128 * j + Ks))] + ([(o, idm(2048.0), c(LV, k0, k1))] if j == 0 else []) + compact(o, "S", "AB", 3840 * j + 16 * k0, Ks))
+            ts(e3("FL", k0, k1), dec, 1.0 / 256, FO - t + 8.5 / 256, A.mult, A.add); ev(e3("FF", k0, k1), dec, -120.0)
+            o = ps(XB, 2 * Ks, 3 * Ks)
+            mm([(o, idm(512), c(LV, k0, k1))] + [(o, idm(1), ap("FL", h, slice(k0, k1))) for h in range(2)])
+            act(c("TT", k0, k1), o, F.Sign, -(2.0 * (FO - t - 204) + 42.5 + 512))
+            mm([(dec, idm(-256), e3("FL", k0, k1)), (dec, idm(-256), e3("FC", k0, k1)), (dec, fmat("I", 1.0), e3("FF", k0, k1))], stop=False)
+            for j in (3, 1, 2, 0):
+                o = ps(YB, Ks * j, Ks * j + Ks); lst = [(o, idm(1), ap("ETA", j - 1, slice(k0, k1))) if j else (o, idm(1024), c(LV, k0, k1))]
+                if j == 3 and P["relu"][s]: lst += [(o, idm(2048), c("ONE", 0, Ks))] + compact(o, "S4", "AB", 3840 * 3 + 16 * k0, Ks) + compact(o, "SN", "HZ", 16 * k0, Ks)
+                else: lst += compact(o, "S", "AB", 3840 * j + 16 * k0, Ks)
+                mm(lst)
         def decide(s):
             tag[0] = "d%d" % s
-            k0, k1 = part[s]; Ks = k1 - k0; db = 4 + s % 2; dec = ps(db, 0, 2 * Ks)
-            FL, TOP, TT = c("FL", 2 * k0, 2 * k1), c("TOP", 2 * k0, 2 * k1), c("TT", k0, k1)
-            ev(c("SS", 0, 3 * Ks), ps(db, 0, 3 * Ks))
-            S_ = lambda j: c("SS", Ks * j, Ks * j + Ks); P_ = lambda j: ps(db, Ks * j, Ks * j + Ks); M_ = lambda j: c("MM", Ks * j, Ks * j + Ks)
-            tt(M_(2), P_(3), S_(2), A.min); tt(M_(3), P_(3), S_(1), A.min); tt(M_(0), P_(1), S_(0), A.min); tt(M_(1), P_(2), S_(0), A.min)
-            tt(e3("PT", k0, k1), c("MM", 2 * Ks, 4 * Ks), c("MM", 0, 2 * Ks), A.is_lt)
-            sg = 1.0 if t % 2 == 0 else -1.0
-            for h in range(2):
-                mm([(ps(db, Ks * h, Ks * h + Ks), l, x) for l, x in ((ap("IF"), ap(E, h, slice(k0, k1))), (idm(8192.0 * sg), TT), (idm(1920.0), ap("PT", h, slice(k0, k1))))])
-            cs = LOO - 8192.0 if t % 2 == 0 else 8192.0; mo = A.max if t % 2 == 0 else A.min
-            tt(c("IA", 0, Ks), ps(db, 0, Ks), c("ALT", 256 * (t % 2) + k0, 256 * (t % 2) + k1), mo); ts(ap("IX", 0, slice(k0, k1)), c("IA", 0, Ks), cs, None, A.add)
-            ts(ap("IX", 1, slice(k0, k1)), ps(db, Ks, 2 * Ks), cs, float(CST if t % 2 == 0 else CST2 - LOO), A.add, mo)
-            mm([(dec, idm(-128.0), FL), (dec, idm(64.0), TOP), (dec, ap("IF"), c("FF", 2 * k0, 2 * k1))]
-               + [(ps(db, Ks * h, Ks * h + Ks), idm(2048.0), ap("PT", h, slice(k0, k1))) for h in range(2)])
+            k0, k1 = part[s]; Ks = k1 - k0; dec = ps(XB, 0, 2 * Ks)
+            S_ = lambda j: ap("SS", j, slice(0, Ks)); P_ = lambda j: ps(YB, Ks * j, Ks * j + Ks); Q_ = lambda j: ap("EQ", j - 1, slice(k0, k1))
+            ev(S_(0), P_(0), -1024.0)
+            for j in (1, 2, 3): tt(S_(j), P_(j), S_(j - 1), A.min)
+            for j in (3, 1, 2): tt(Q_(j), P_(j), S_(3), A.is_equal)
+            sg = 1.0 if t % 2 == 0 else -1.0; pole = ((2, 3), (1, 3))
+            for h in (1, 0):
+                mm([(P_(h), l, x) for l, x in [(idm(1), ap(E, h, slice(k0, k1))), (idm(4096 * sg), c("TT", k0, k1))] + [(idm(1920), Q_(j)) for j in pole[h]]])
+            cs = LOO - 4096.0 if t % 2 == 0 else 4096.0; mo = A.max if t % 2 == 0 else A.min
+            ts(ap("IX", 1, slice(k0, k1)), P_(1), cs, float(CST if t % 2 == 0 else CST2 - LOO), A.add, mo)
+            tt(c("IA", 0, Ks), P_(0), c("ALT", 256 * (t % 2) + k0, 256 * (t % 2) + k1), mo); ts(ap("IX", 0, slice(k0, k1)), c("IA", 0, Ks), cs, None, A.add)
+            mm([(ps(XB, Ks * h, Ks * h + Ks), idm(2048), Q_(j)) for h in range(2) for j in pole[h]], start=False)
+            relu(e3("TR", k0, k1), dec, 1.0 - base)
             tt(e3(En, k0, k1), dec, e3(E, k0, k1), A.max)
             if t < 3: cp(e3(EUn, k0, k1), e3(En, k0, k1))
         def phase_b(s):
             tag[0] = "b%d" % s
-            k0, k1 = part[s]; Ks = k1 - k0; db = 4 + s % 2; D = lambda j, x, y: c("HZ", x, y) if j == 0 else c("AB", 3840 * (j + 1) + x, 3840 * (j + 1) + y)
-            for n, (a, z) in enumerate(upto(k0, k1, 32 if s else BP[0])):
-                a16, z16 = 16 * a, 16 * z
-                gat(D(0, a16, z16), win, ap("IX", 0, slice(a, z)))
-                how = BMODE[s][n]; bb = [7, 6, 2][:5 - NA[0]]
-                o = ps(bb[reg[1] % len(bb)], 0, z16 - a16); reg[1] += 1
+            k0, k1 = part[s]; how = P["bmode"][s]
+            for (a, z) in upto(k0, k1, P["bw"][s]):
+                a16, z16 = 16 * a, 16 * z; n = z16 - a16; D = lambda j: c("D", 3840 * j + a16, 3840 * j + z16); d_ = lambda w, j: (w, "D", 3840 * j + a16)
+                gat(D(0), win, ap("IX", 1, slice(a, z)))
                 if how == 2:
-                    o2 = o; o = ps(bb[reg[1] % len(bb)], 0, z16 - a16); reg[1] += 1
-                    gat(D(1, a16, z16), win, ap("IX", 1, slice(a, z)))
-                    mm([(o2, idm(1.0), D(0, a16, z16)), (o2, idm(-1.0), D(1, a16, z16))]); act(D(2, a16, z16), o2, F.Abs)
-                else: gtt(D(1, a16, z16), win, ap("IX", 1, slice(a, z)), D(0, a16, z16), A.subtract)
-                if how == 1: act(D(2, a16, z16), D(1, a16, z16), F.Abs)
-                if how: mm([(o, idm(0.5), c("WB", ysrc + a16, ysrc + z16)), (o, idm(0.5), D(2, a16, z16))])
-                else:
-                    ts(D(2, a16, z16), D(1, a16, z16), 0.0, None, A.max)
-                    mm([(o, idm(0.5), c("WB", ysrc + a16, ysrc + z16)), (o, idm(-0.5), D(1, a16, z16)), (o, idm(1.0), D(2, a16, z16))])
-                ev(ydst(a16, z16), o, 95.75)
+                    gat(D(1), win, ap("IX", 0, slice(a, z)))
+                    o = slot(1); wide(o, n, [d_(1, 0), d_(-1, 1)]); act(D(2), c("PS", o, o + n), F.Abs)
+                else: gtt(D(1), win, ap("IX", 0, slice(a, z)), D(0), A.subtract)
+                if how == 1: act(D(2), D(1), F.Abs)
+                o = slot(1); y = (0.5, "WB", ysrc + a16)
+                if how: wide(o, n, [y, d_(0.5, 2)])
+                else: ts(D(2), D(1), 0.0, None, A.max); wide(o, n, [y, d_(-0.5, 1), d_(1, 2)])
+                ev(ydst(a16, z16), c("PS", o, o + n), 95.75)
+        y_ = ydst(0, 16); yb, y0 = y_[0], y_[2][0].start
         def alive(s):
-            k0, k1 = part[s]; Ks = k1 - k0
-            y = ydst(0, 16); mm(compact(ps(3, 0, Ks), "S", y[0], y[2][0].start + 16 * k0, Ks))
-            ts(c(LVn, k0, k1), ps(3, 0, Ks), 3248.0, None, A.is_ge)
+            k0, k1 = part[s]; Ks = k1 - k0; o = slot(1); o = c("PS", o, o + Ks)
+            mm(compact(o, "S", yb, y0 + 16 * k0, Ks))
+            act(c(LVn, k0, k1), o, F.Sign, -3247.5, acc=col(LA + s) if t < 3 else None)
+        def live_row():
+            nb = LW // 32; per = 16 // nb
+            for j in range(nb):
+                bk = (XB, YB)[j]; x = c("R", RO + B0 + 512 * j, RO + B0 + 512 * j + 512)
+                mm([(ps(bk, 0, 512), sh("SC", 3), ap("ONE")), (ps(bk, 0, 512), HOLE, x)], stop=False)
+                mm([(ps(bk, LW * r, LW * r + LW), sh("S2", 3), c(yb, y0 + per * j + r, y0 + 16 * LW, 16)) for r in range(per)], start=False)
+                ts(x, ps(bk, 0, 512), col(LO_), col(HI_), A.max, A.min)
         def cells_on():
             tag[0] = "c"
             Cn = C + 256
+            if t == 3: return dma(ap("yx", slice(0, 1536), p=slice(0, 128)), c("WB", LOO, LOO + 1536), "y")
             for a in range(0, Cn, 512):
-                z = min(Cn, a + 512); bk = a // 512; o = ps(bk, 0, z - a); lst = [(o, idm(1.0), c("WB", LOO + a, LOO + z))]
-                if a >= 512: lst.append((o, idm(-128.0), c("NXT", a - 512, z - 512)))
-                if t < 3:
-                    u = a
-                    while u < z:
-                        s0 = (u + 331 * t) % 1024; n = min(z - u, 1024 - s0); lst.append((ps(bk, u - a, u - a + n), idm(1.0), c("DR", s0, s0 + n))); u += n
+                z = min(Cn, a + 512); bk = a // 512; o = ps(bk, 0, z - a); lst = [(o, idm(1), c("WB", LOO + a, LOO + z))]
+                if a >= 512: lst.append((o, idm(-128), c("NXT", a - 512, z - 512)))
+                u = a
+                while u < z:
+                    s0 = (u + 331 * t) % 1024; n = min(z - u, 1024 - s0); lst.append((ps(bk, u - a, u - a + n), idm(1), c("DR", s0, s0 + n))); u += n
                 mm(lst)
             for a in range(0, Cn, 1024):
-                z = min(Cn, a + 1024); ts(c("XT", XO + a, XO + z), c("PS", a, z), 0.0, 63.0, A.max, A.min)
-            if t < 3: cells_ahead(t + 1)
-            else: dma(ap("yx", slice(0, 1536), p=slice(0, 128)), c("XT", XO, XO + 1536), "y")
-        def to_rows(f, src, new, q):
-            for h in range(2):
-                if new:
-                    for u in range(t): dma(rows(f, RH * h + 3073 + 256 * u, RH * h + 3329 + 256 * u), src(h, 192 + 16 * u, 208 + 16 * u), q)
-                else: dma(rows(f, RH * h + 1, RH * h + 3073), src(h, 0, 192), q if len(q) == 1 else q[h])
-        pt = lambda h, a, z: ap("PT", h, slice(a, z)); lv = lambda h, a, z: c(LVn, a, z)
-        phase_a(2); decide(2); to_rows(1, pt, True, "y"); phase_a(1); phase_b(2); decide(1); phase_a(0); alive(2); to_rows(0, lv, True, "y"); cells_on()
-        phase_b(1); alive(1); decide(0); to_rows(1, pt, False, "y")
+                z = min(Cn, a + 1024); ts(c("XT", a, z), c("PS", a, z), 0.0, 63.0, A.max, A.min)
+        def to_rows(fs, which):
+            for f in fs: to_row(f, (lambda a, z: ap("TR", 0, slice(a, z)), lambda a, z: ap("TR", 1, slice(a, z)), lambda a, z: ap("EQ", 2, slice(a, z)), lambda a, z: c(LVn, a, z))[f], which)
+        phase_a(1); decide(1); phase_a(2); phase_b(1); decide(2); to_rows((0, 1, 2), runs[1:2 + t]); phase_a(0); alive(1); decide(0); to_rows((0, 1, 2), runs[:1])
+        phase_b(2); alive(2); to_rows((3,), runs[1:2 + t]); cells_on()
         tag[0] = "t"
         if t < 3:
-            mm([(ps(0, 0, 256), ap("ONES"), ap("LIW")), (ps(0, 0, 256), idm(-8192.0), c("NXT", 256 * t, 256 * t + 256))])
-            ts(ap("LI"), ps(0, 0, 256), 3248.0, None, A.is_ge); act(ap("JK"), ap("LI"), F.Identity, acc=col(11))
-            mm(compact(ps(1, 0, 24), "PK8", "GW", 0, 24))
-            ts(ap("F2"), ps(1, 0, 24), 1.0 / 128, 1536 + 8.5 / 128, A.mult, A.add); ev(c("FF", 480, 504), ps(1, 0, 24), 72.0)
-            ts(ap("P2"), ap("OWN"), col(V128), (base - 2048) / 128 + 1536.0, A.is_ge, A.add)
-            gat(ap("GT"), c("R", 0, RH + 3088), ap("TW"))
-            mm(compact(ps(2, 0, 24), "PK", "GT", 0, 24)); ts(ap("M2"), ps(2, 0, 24), 16.0, None, A.is_ge)
-            mm([(ps(1, 0, 24), idm(-128.0), ap("F2")), (ps(1, 0, 24), idm(128.0), ap("P2")), (ps(1, 0, 24), ap("IF"), c("FF", 480, 504)), (ps(1, 0, 24), idm(2048.0), ap("M2"))])
-            tt(ap("TWF"), ps(1, 0, 24), ap("OWN"), A.max); cp(ap("OWN"), ap("TWF")); cp(ap("OWU"), ap("TWF"))
+            gat(ap("GT"), ap("R"), ap("TW"))
+            o = ps(1, 0, 24); mm(compact(o, "PKT", "GT", 0, 24))
+            ts(ap("TA"), o, 0.5, base - 1.0, A.is_gt, A.mult); tt(ap("TB"), o, ap("TA"), A.add); tt(ap("OWN"), ap("TB"), ap("OWN"), A.max); cp(ap("OWU"), ap("OWN"))
+            cells_ahead(t + 1)
         else:
+            ef = lambda h: ap("EF", h, slice(0, 192))
+            tt(c("T2", 0, 192), ef(0), ap("NSW"), A.add); tt(ef(1), ef(1), c("T2", 0, 192), A.min); tt(ef(0), ef(0), ap("SWF"), A.max)
             for h in range(2):
-                dma(ap("ye", slice(0, 3072), p=slice(h, 16, 2)), ap(En, h, slice(0, 192)), "y")
-                for u in range(3): dma(ap("ye", slice(3072 + 256 * u, 3328 + 256 * u), p=slice(h, 16, 2)), ap(En, h, slice(192 + 16 * u, 208 + 16 * u)), "y")
-        phase_b(0); alive(0); to_rows(0, lv, False, "y")
-        if t < 3: mm([(ps(7, 0, K), ap("ONES"), c(LVn, 0, K))]); act(c("JK", 0, K), ps(7, 0, K), F.Identity, acc=col(LOLD))
+                for a, z, k0, k1 in runs[:5]: dma(ap("ye", slice(a, z), p=slice(h, 16, 2)), ap(En, h, slice(k0, k1)), "y")
+        phase_b(0)
+        if P["direct"]: live_row()
+        if t < 3 or not P["direct"]: alive(0)
+        if not P["direct"]: to_rows((3,), runs[:1])
+        if t < 3: count_ahead(t + 1)
         else:
-            for r in range(16): ev(c("AB", 4096 + 192 * r, 4288 + 192 * r), c("YF", r, 3072, 16), -192.0)
-            gat(c("AB", 7168, 7936), c("YF", 3072, 3840), c("ULAST", 0, 48), -192.0)
-            dma(ap("yy", slice(0, 3840), p=slice(0, 128)), c("AB", 4096, 7936), "y")
+            for a, z, k0, k1 in (runs[1], runs[0]):
+                for r in range(16): ev(c("Y0N", a + (k1 - k0) * r, a + (k1 - k0) * (r + 1)), c("YF", 16 * k0 + r, 16 * k1, 16), -192.0)
+                dma(ap("yy", slice(a, z), p=slice(0, 128)), c("Y0N", a, z), "y")
+            gat(c("FR", 0, 768), c("YF", 3072, 3840), c("ULAST", 0, 48), -192.0)
+            dma(ap("yy", slice(3072, 3840), p=slice(0, 128)), c("FR", 0, 768), "y")
+
+    def slots(t):
         tag[0] = "s"
+        mm([(ps(2, 0, 512), idm(-1), ap("ONE")), (hp(2, 0), idm(2048), c("NXT", 256 * t, 256 * t + 256))] + ([(hp(2, h), idm(1), ap("LI")) for h in range(2)] if t < 3 else []), stop=False)
         for j in range(4):
-            gat(c("AB", 1024 * j, 1024 * j + 1024), c("R", 0, RH + 4112), c("OLU", 64 * j, 64 * j + 64))
-            if t < 3:
-                o = ps(4, 64 * j, 64 * j + 64)
-                mm([(o, idm(128.0), c("LI", 64 * j, 64 * j + 64))] + [(o, ap("PQ"), c("AB", 1024 * j + r, 1024 * j + 1024, 16)) for r in range(16)])
-        if t < 3: act(ap("JK"), ps(4, 0, 256), F.Relu, col(12), acc=col(LNEW))
-        for j in range(4):
-            o = ps(5, 64 * j, 64 * j + 64)
-            mm([(o, idm(1.0), c("NXT", 256 * t + 64 * j, 256 * t + 64 * j + 64))] + compact(o, "PK", "AB", 1024 * j, 64))
-        ts(c("SM", 0, 256), ps(5, 0, 256), 1.0, None, A.is_equal); ts(c("SM", 256, 512), ps(5, 0, 256), 17.0, None, A.is_equal)
-        mm([(ps(6, 0, 512), ap("ONES"), ap("SM"))])
-        act(ap("NM"), ps(6, 0, 512), F.Relu, -15.0)
-        if t < 3:
-            mm([(ps(6, 0, 256), idm(1.0), ap("LI")), (ps(6, 0, 256), idm(-1.0), c("NM", 0, 256)), (ps(6, 0, 256), idm(-1.0), c("NM", 256, 512))])
-            act(ap("ML"), ps(6, 0, 256), F.Relu)
-        mm([(ps(3, 0, 512), idm(-16384.0), ap("ONE"))] + [(ps(3, 256 * h, 256 * h + 256), ap("IF"), ap("OLD")) for h in range(2)], stop=False)
-        mm([(ps(3, 0, 512), idm(16384.0), ap("SM"))], start=False)
-        mm([(ps(0, 0, 512), ap("TF"), ap("SM"))] + [(ps(0, 256 * h, 256 * h + 256), l, x) for h in range(2)
-                                                    for l, x in ((idm(1.0), ap("IO1")), (idm(-16384.0), c("NM", 0, 256)), (idm(-16384.0), c("NM", 256, 512)))])
-        bl = "BL" if t < 3 else "BLF"
-        for h, o in enumerate((ap("TVF"), c(bl, C, C + 256))):
-            hp = lambda b: ps(b, 256 * h, 256 * h + 256); t2 = c("T2", 256 * h, 256 * h + 256); bc = c("BC", 2 * t + h, 2 * t + h + 1)
-            if t < 3: act(t2, hp(0), F.Relu, bc)
-            else: ts(t2, hp(0), bc, -1.0, A.add, A.max)
-            tt(o, hp(3), t2, A.max)
-        sca(ap(bl), ap("DL2"), ap("TVF"))
-        mm([(ps(5, 0, 16), sh("PK", r), c("NM", 256 * j + 16 * r, 256 * j + 16 * r + 16)) for j in range(2) for r in range(16)])
-        s16 = lambda j: c("S16", 16 * j, 16 * j + 16)
-        ts(s16(0), ps(5, 0, 16), 1.0, 1535.0, A.is_ge, A.mult); tt(s16(1), s16(0), ap("DLF"), A.max); cp(ap("DLM"), s16(1))
-        gat(ydst(16 * K, 16 * K + 256), c("WP", 0, 1536), ap("DLM"), 201.0)
-        ts(s16(2), ps(5, 0, 16), 1.0, None, A.is_lt); ts(s16(3), c("IO", 0, 16), col(PM16), float(base), A.add, A.add)
-        tt(ap(En, 0, slice(K, K + 16)), s16(2), ap("DLF"), A.mult); tt(ap(En, 1, slice(K, K + 16)), s16(2), s16(3), A.mult)
-        if t < 3:
-            cp(e3(EUn, K, K + 16), e3(En, K, K + 16))
-            mm([(ps(4, 0, 16), sh("PK", r), c("ML", 16 * r, 16 * r + 16)) for r in range(16)]); ts(c(LVn, K, K + 16), ps(4, 0, 16), 1.0, None, A.is_ge)
+            gat(c("SG", 1024 * j, 1024 * j + 1024), ap("R"), c("OLU", 64 * j, 64 * j + 64))
+            o = ps(j // 2, 64 * (j % 2), 64 * (j % 2) + 64)
+            mm([(o, idm(-1), c("IO1", 64 * j, 64 * j + 64))] + compact(o, "PKR", "SG", 1024 * j, 64))
+        for u in range(2):
+            o = ps(u, 0, 128); a = 128 * u
+            ts(sm(0, a, a + 128), o, 0.0, None, A.is_gt); ts(sm(1, a, a + 128), o, 2048.0, None, A.is_equal); ts(sm(2, a, a + 128), o, 2560.0, None, A.is_ge)
+            mm(kept(2, "O", 128.0, a, a + 128), False, u == 1)
+        if t < 3: act(ap("T2"), ps(2, 0, 512), F.Relu, -2047.0, acc=col(LOST))
+
+    def books(t):
+        tag[0] = "k"
+        C = 512 + 256 * t; K = 192 + 16 * t
+        E, En, EU, EUn, LV, LVn, ydst = names(t)
+        relu(ap("NM"), ps(2, 0, 512), -1920.0)
+        mm([(ps(2, 0, 32), sh("P0", r), e3("NM", 16 * r, 16 * r + 16)) for r in range(16)]); ev(ap("NC"), ps(2, 0, 32))
+        q = lambda j: ps(2, 32 + 16 * j, 48 + 16 * j); nc = [c("NC", 0, 16), c("NC", 16, 32)]
+        for j, (x, w) in enumerate(((ap("VR"), -16), (c("NR", 16 * t, 16 * t + 16), -16), (c("NR", 0, 16), 16))): mm([(q(j), idm(1), x)] + [(q(j), idm(w), y) for y in nc])
+        if t < 3: mm(across(q(3), "P0", "LI", 0) + [(q(3), idm(-1), y) for y in nc])
+        ts(ap("DLM"), q(2), -512.0, 256.0, A.add, A.min)
+        gat(ydst(16 * K, 16 * K + 256), ap("LIW"), ap("DLM"))
+        ts(e3(En, K, K + 16), ps(2, 32, 64), 0.0, None, A.max)
+        if t < 3: ts(e3(EUn, K, K + 16), ps(2, 32, 64), 0.0, None, A.max); act(c(LVn, K, K + 16), q(3), F.Sign)
         else:
-            gat(c("AB", 7936, 8192), c("YF", 3072, 4096), c("ULAST", 48, 64), -192.0)
-            dma(ap("yy", slice(3840, 4096), p=slice(0, 128)), c("AB", 7936, 8192), "s")
+            gat(c("FR", 768, 1024), c("YF", 3072, 4096), c("ULAST", 48, 64), -192.0)
+            dma(ap("yy", slice(3840, 4096), p=slice(0, 128)), c("FR", 768, 1024), "s")
             for h in range(2): dma(ap("ye", slice(3840, 4096), p=slice(h, 16, 2)), ap(En, h, slice(240, 256)), "ys"[h])
-            dma(ap("yl", slice(0, 1536), p=slice(0, 128)), c("BLF", 0, 1536), "y")
+        mm([(ps(XB, 0, 512), idm(-16384), ap("ONE"))] + [(hp(XB, h), fmat("I", 1.0), ap("OLD")) for h in range(2)], stop=False)
+        mm(kept(XB, "I", 16384.0), start=False)
+        mm([(ps(YB, 0, 512), idm(1), ap("IO1"))] + kept(YB, "F", 16384.0), stop=False)
+        mm([(hp(YB, h), idm(-128), nm(j)) for h in range(2) for j in range(2)], start=False)
+        for h, o in enumerate((ap("TVF"), c("BL", C, C + 256))):
+            t2 = c("T2", 256 * h, 256 * h + 256)
+            ts(t2, hp(YB, h), c("BC", t, t + 1), -1.0, A.add, A.max)
+            tt(o, hp(XB, h), t2, A.max)
+            if h == 0: sca(ap("BL"), ap("DL2"), ap("TVF"))
+        if t == 3: dma(ap("yl", slice(0, 1536), p=slice(0, 128)), ap("BL"), "y")
+
+    who(0)
+    for t in range(4):
+        dividers(t); bridges(t); slots(t)
+        if t < 3: who(t + 1)
+        books(t)
     return ops
 
 
 def depend(ops):
     seen = {}
     for n, o in enumerate(ops):
-        deps = set()
+        deps = {}
         acc = [(x, False) for x in o["rd"]] + [(x, True) for x in o["wr"]]
         for x, w in acc:
             for m, pm, cm, mw in seen.get(x[0], []):
-                clash = w or mw or (x[0] == "PS" and (len(o["alts"]) > 1 or o["alts"].keys() != ops[m]["alts"].keys()))
-                if clash and m != n and pm & x[4] and cm & x[5]: deps.add(m)
+                if (w or mw or x[0] == "PS") and m != n and pm & x[4] and cm & x[5]:
+                    hard = (mw and not w) or ((w or mw) and not P["war"]) or ops[m]["kind"] != "c" or o["kind"] != "c"
+                    if "p" in o["alts"] and "p" in ops[m]["alts"]: hard = False
+                    deps[m] = deps.get(m, False) or hard
         for x, w in acc:
             lst = seen.setdefault(x[0], [])
             if w: lst[:] = [e for e in lst if (e[1] & ~x[4]) or (e[2] & ~x[5])]
             lst.append((n, x[4], x[5], w))
-        if o["kind"] == "arrive": deps = {n - 1}
+        if o["kind"] == "arrive": deps = {n - 1: True}
         o["deps"] = deps
 
 
-def arrange(ops, lat=120.0, far=3500.0, bias=8000.0, look=3.0, ahead=400.0, noise=0.0, seed=0, bonus={}):
-    n = len(ops); kids = [[] for o in ops]
+def settle(ops, rounds=8):
+    lat, far, bias = P["lat"], P["far"], P["bias"]
+    n = len(ops); kids = [{} for o in ops]
     for i, o in enumerate(ops):
-        for d in o["deps"]: kids[d].append(i)
-    def span(o):
-        if o["kind"] == "arrive": return far
-        return min(v[1] for v in o["alts"].values()) + (o["x"] if o["kind"] == "dma" else 0) + lat
-    pr = [0.0] * n
-    for i in range(n - 1, -1, -1):
-        same = any(ops[k]["tag"] == ops[i]["tag"] for k in kids[i])
-        pr[i] = span(ops[i]) + max([pr[k] for k in kids[i]] + [0.0]) + (0.0 if same else bonus.get(ops[i]["tag"], 0.0))
-    pr = [float(x) for x in np.array(pr) + noise * np.random.default_rng(seed).random(n)]
-    left = [len(o["deps"]) for o in ops]; est = [0.0] * n; ready = [i for i in range(n) if not left[i]]
-    free = {e: 0.0 for e in "vspqy"}; order = []; busy = {e: 0.0 for e in "vspqy"}
-    def finish(i, tm):
-        ops[i]["end"] = tm
-        for k in kids[i]:
-            est[k] = max(est[k], tm + lat); left[k] -= 1
-            if not left[k]:
-                if ops[k]["kind"] == "arrive": ops[k]["e"] = None; finish(k, est[k] + far)
-                else: ready.append(k)
-    while ready:
-        best = None
-        for e in free:
-            cand = [i for i in ready if e in ops[i]["alts"]]
-            if not cand: continue
-            t0 = max(free[e], min(est[i] for i in cand))
-            key = lambda j: (pr[j] - (bias if e == "v" and len(ops[j]["alts"]) > 1 else 0) - look * max(0.0, est[j] - t0), -j)
-            i = max([i for i in cand if est[i] <= t0 + ahead], key=key)
-            if best is None or t0 < best[0]: best = (t0, e, i)
-        t0, e, i = best
-        st = max(free[e], est[i]); cost = ops[i]["alts"][e][1]; free[e] = st + cost; busy[e] += cost
-        ops[i]["e"] = e; ops[i]["st"] = st; ready.remove(i); order.append(i)
-        finish(i, st + cost + (ops[i]["x"] if ops[i]["kind"] == "dma" else 0))
-    return order, busy
-
-
-def settle(ops, rounds=6, lat=120.0, far=3500.0, bias=1.3):
-    n = len(ops); kids = [[] for o in ops]
-    for i, o in enumerate(ops):
-        for d in o["deps"]: kids[d].append(i)
+        for d, hard in o["deps"].items(): kids[d][i] = hard
     tail = [far if o["kind"] == "arrive" else o["x"] if o["kind"] == "dma" else 0.0 for o in ops]
     def lay(key, back):
         lines = {e: ([], []) for e in "vspqy"}; st = [0.0] * n; en = [0.0] * n; eng = [None] * n
         for i in sorted(range(n), key=key):
-            o = ops[i]; t0 = max([en[d] + lat for d in (kids[i] if back else o["deps"])] + [0.0]) + (tail[i] if back else 0.0); best = None
+            o = ops[i]; near = kids[i] if back else o["deps"]; best = None
             for e, v in o["alts"].items():
+                t0 = max([en[d] + (lat if hard or eng[d] != e else 0.0) for d, hard in near.items()] + [0.0]) + (tail[i] if back else 0.0)
                 a, z = lines[e]; j = int(np.searchsorted(z, t0, side="right")) if z else 0; x = t0
                 while j < len(a) and a[j] < x + v[1]: x = max(x, z[j]); j += 1
                 sc = x + v[1] * (bias if e == "v" else 1.0)
                 if best is None or sc < best[0]: best = (sc, x, e, j)
-            if best is None: st[i] = en[i] = t0
+            if best is None: st[i] = en[i] = max([en[d] + lat for d in near] + [0.0]) + (tail[i] if back else 0.0)
             else:
                 x, e, j = best[1:]; lines[e][0].insert(j, x); lines[e][1].insert(j, x + o["alts"][e][1]); st[i] = x; en[i] = x + o["alts"][e][1]; eng[i] = e
             if not back: en[i] += tail[i]
         return st, en, eng
-    en = [o["end"] for o in ops]; top = None
+    pr = [0.0] * n
+    for i in range(n - 1, -1, -1):
+        pr[i] = min([v[1] for v in ops[i]["alts"].values()] + [0.0] * (not ops[i]["alts"])) + tail[i] + lat + max([pr[k] for k in kids[i]] + [0.0])
+    st, en, eng = lay(lambda i: (-pr[i], i), False); top = (max(en), st, en, eng)
     for k in range(rounds):
         sb, eb, x = lay(lambda i: (-en[i], -i), True)
         st, en, eng = lay(lambda i: (-eb[i], i), False)
-        if top is None or max(en) < top[0]: top = (max(en), st, en, eng)
+        if max(en) < top[0]: top = (max(en), st, en, eng)
     busy = {e: 0.0 for e in "vspqy"}
     for o, s, z, e in zip(ops, top[1], top[2], top[3]):
         o["st"] = s; o["end"] = z; o["e"] = e
@@ -501,15 +509,15 @@ def settle(ops, rounds=6, lat=120.0, far=3500.0, bias=1.3):
 
 
 def plan():
-    ops = build(); depend(ops); arrange(ops); order, busy = settle(ops)
+    ops = build(); depend(ops); order, busy = settle(ops)
     count = {}; known = {e: {} for e in "vspqy"}; nd = 0; steps = []
     for i in order:
         o = ops[i]; e = o["e"]; kn = known[e]; need = {}
-        for d in sorted(o["deps"]):
+        for d, hard in sorted(o["deps"].items()):
             od = ops[d]
             if od["kind"] == "arrive": sig, ck = ("ar%d" % od["x"], 12), {}
             else: sig, ck = od["sig"], od["ck"]
-            if e == "p" and od.get("e") == "p" and not any(x[0] != "PS" for x in od["wr"]): continue
+            if od["e"] == e and not hard: continue
             if kn.get(sig[0], 0) < sig[1]: need[sig[0]] = (max(sig[1], need.get(sig[0], (0,))[0]), ck if sig[1] >= need.get(sig[0], (0,))[0] else need[sig[0]][1])
         for s in list(need):
             if any(s2 != s and need[s2][1].get(s, 0) >= need[s][0] for s2 in need): need.pop(s)
@@ -542,7 +550,6 @@ def rank_program(g, core, T, topo):
     queue = {"v": g.vector, "s": g.scalar, "p": g.tensor, "q": g, "y": g.sync}
 
     def r(x):
-        if isinstance(x, str): return rank
         if not isinstance(x, tuple): return x
         return T[x[0]][(x[1],) + x[2]]
 

@@ -12,12 +12,12 @@ FO = 1500
 NMAT = 34
 SB = {
     "Y0N": ([3072], BF), "WB": ([WBW], BF), "YF": ([4096], BF), "HH": ([1920], BF), "WP": ([1920], F32), "XT": ([1536], BF), "P2": ([1280], BF),
-    "UH": ([3840], HF), "WA": ([3840], HF), "WZ": ([3840], HF), "HZ": ([3840], BF), "AB": ([4 * 3840], BF), "D": ([3 * 3840], BF), "SG": ([4096], BF),
+    "UH": ([3840], HF), "WA": ([3840], HF), "WZ": ([3840], HF), "HZ": ([3840], BF), "AB": ([4 * 3840], BF), "D": ([3 * 3840], BF),
     "R": ([RW_], BF), "BL": ([1536], F32), "DR": ([1024], BF), "FR": ([1024], BF), "BTG": ([1280], BF), "NXT": ([1024], BF), "BC": ([4], F32), "IO1": ([512], BF),
     "EI": ([2, 192], I32), "BI": ([512], I32), "SI": ([24], I32), "NSW": ([192], F32), "SWF": ([192], F32), "EB": ([192], BF), "FC": ([2, 256], HF),
     "E0": ([2, 256], HF), "E1": ([2, 256], HF), "EF": ([2, 256], F32), "EU0": ([2, 256], U16), "EU1": ([2, 256], U16),
-    "LV0": ([256], BF), "LV1": ([256], BF), "EQ": ([3, 256], BF), "TR": ([2, 256], BF), "IX": ([2, 256], U16),
-    "SS": ([4, 128], F32), "FL": ([2, 256], HF), "FF": ([2, 240], F32), "TT": ([256], BF), "IA": ([128], F32),
+    "LV0": ([256], BF), "LV1": ([256], BF), "EQ": ([2, 384], BF), "EC": ([256], BF), "TR": ([2, 256], BF), "IX": ([2, 256], U16),
+    "SS": ([3, 128], F32), "FL": ([2, 256], HF), "FF": ([2, 256], F32), "TT": ([2, 128], BF), "IA": ([128], F32), "I3": ([384], BF), "S24": ([24], BF),
     "JK": ([16, 80], BF), "SX": ([80], F32), "NSX": ([80], F32), "CA": ([80], BF), "CU": ([80], F32), "PL": ([96], F32), "UBT": ([80], U16),
     "COL": ([32], F32), "QB": ([2], BF), "CI": ([8], I32), "OH": ([16], F32), "ACC": ([16], F32), "KI": ([16], U16), "NB": ([16], F32), "KT": ([96], BF), "KD": ([256], BF), "MK": ([256], BF),
     "DM": ([16], F32), "DL2": ([16], U16), "VR": ([16], HF), "DLM": ([16], U16), "NC": ([32], BF), "S16": ([64], F32), "NR": ([64], HF), "ULAST": ([64], U16),
@@ -32,8 +32,8 @@ SCRATCH["PS"] = ("psum", [128, 4096], F32)
 NDMA = 120
 SEMAPHORES = ["v", "s", "p", "q"] + ["ar%d" % t for t in range(4)] + ["ls%d" % t for t in range(4)] + ["d%d" % i for i in range(NDMA)]
 SELS = ("S", "PKW", "PKR", "PKT", "P0", "P16", "RW", "S2", "SC", "S4", "SN")
-P = {"g": 1.4, "s": 3.0, "ov": 15.0, "gp": 32, "aw": 32, "abank": [0, 1, 2], "bbank": [5, 6, 7], "bw": [16, 32, 32], "last": 64, "mid": [64, 64, 64, 64],
-     "bmode": [1, 1, 1], "relu": [0, 0, 0], "lat": 230.0, "far": 3000.0, "dma": 1300.0, "bias": 2.0, "war": 0, "direct": 1}
+P = {"g": 1.4, "s": 3.0, "ov": 15.0, "gp": 32, "aw": 32, "abank": [0, 1], "bbank": [5, 6, 7], "bw": [32, 32, 16], "last": 32,
+     "bmode": [1, 1, 1], "relu": [0, 0, 0], "lat": 230.0, "far": 3000.0, "dma": 1300.0, "bias": 2.0, "war": 0, "direct": 1, "xb": [3, 2], "shake": 0.0, "rounds": 8, "temp": 500.0, "due": 1, "slack": 500.0, "tilt": 0.1}
 CY, XB, YB = 0.83, 3, 4
 
 
@@ -103,11 +103,14 @@ def build():
         add({"v": (lambda g, r: g.vector.tensor_tensor(r(o), r(w).indirect(r(off)), r(i1), op), gc_(o[3], "v"))}, [w, off, i1], [o])
     def sca(w, off, i):
         add({"v": (lambda g, r: g.vector.tensor_copy(r(w).indirect(r(off)), r(i)), 50 + i[3] * P["s"] * CY)}, [off, i, w], [w])
-    def mm(lst, start=True, stop=True):
+    def mm(lst, start=True, stop=True, each=False):
         def f(g, r):
-            for j, (o, l, x) in enumerate(lst): ins = g.tensor.matmul(r(o), r(l), r(x), start and j == 0, stop and j == len(lst) - 1)
+            for j, (o, l, x) in enumerate(lst): ins = g.tensor.matmul(r(o), r(l), r(x), each or (start and j == 0), each or (stop and j == len(lst) - 1))
             return ins
-        add({"p": (f, sum(max(64, x[3]) * 0.42 * (4 if size(x) == 4 else 1) for o, l, x in lst))}, [y for o, l, x in lst for y in (l, x)], [o for o, l, x in lst])
+        add({"p": (f, sum(max(min(64, l[3]), x[3]) * 0.42 * (4 if size(x) == 4 else 1) for o, l, x in lst))}, [y for o, l, x in lst for y in (l, x)], [o for o, l, x in lst])
+    def pt(bank, a, b, n, s=1): return ap("PS", slice(512 * bank + a, 512 * bank + b, s), p=slice(0, n))
+    def top(m, n): a = m[2][0].start; return ap(m[0], slice(a, a + n), p=slice(0, n))
+    def s8(name): j = 144 * SELS.index(name); return c("SEL", j + 15, j + 143, 16)
     def iota(o, pat, base, cm):
         fl = SCRATCH[o[0]][2] != I32
         if fl: f = lambda g, r: g.iota(r(o), pat, base, cm, allow_small_or_imprecise_dtypes=True)
@@ -143,12 +146,12 @@ def build():
     def e3(b, a, z, n=2): return ap(b, slice(0, n), slice(a, z))
     PM, PM16, WA_, WB_, WC_, WD_, WE_, THR, LIA, LOST, CB_, LQ, LO_, HI_, WF_, WG_, WH_, LA = range(18)
     def oh(j): return c("OH", j, j + 1)
-    LW = P["last"]; MW = 192 - LW; B0 = 16 * MW
-    runs = [(B0, 3072, 0, LW), (0, B0, LW, 192)] + [(3072 + 256 * u, 3328 + 256 * u, 192 + 16 * u, 208 + 16 * u) for u in range(4)]
+    LW = P["last"]; MW = 128 - LW; B0 = 16 * MW
+    runs = [(B0, 2048, MW, 128), (0, B0, 0, MW), (2048, 3072, 128, 192)] + [(3072 + 256 * u, 3328 + 256 * u, 192 + 16 * u, 208 + 16 * u) for u in range(4)]
 
     for j in range(4): dma(c("Y0N", 768 * j, 768 * j + 768), ap("y0", slice(768 * j, 768 * j + 768), p=slice(0, 128)), "ys"[j % 2])
     for h in range(2):
-        for a, z, k0, k1 in runs[:2]: dma(ap("EI", h, slice(k0, k1)), ap("en0", slice(a, z), p=slice(h, 16, 2)), "ys"[h])
+        for a, z, k0, k1 in runs[:3]: dma(ap("EI", h, slice(k0, k1)), ap("en0", slice(a, z), p=slice(h, 16, 2)), "ys"[h])
     dma(c("XT", 0, 512), ap("x0", slice(0, 512), p=slice(0, 128)), "s")
     dma(ap("SI"), ap("snd", slice(0, 24), p=slice(0, 128)), "s")
     dma(ap("BI"), ap("bl0", slice(0, 512), p=slice(0, 128)), "y")
@@ -168,6 +171,7 @@ def build():
         if w2 is None: ts(o, i, w1, None, A.mult)
         else: ts(o, i, w1, w2, A.mult, A.mult)
     mksel("S", 1.0); mksel("P0", oh(0)); mksel("P16", oh(0), 16.0)
+    for j in range(3): ev(c("I3", 128 * j, 128 * j + 128), idm(1), 0.0, -1024.0); ev(c("S24", 8 * j, 8 * j + 8), s8("S"), 0.0, -1.0)
     ts(col(WA_), oh(1), 16.0, oh(0), A.mult, A.add); mksel("PKW", col(WA_), 256.0)
     ts(col(WB_), col(PM), 2.0, None, A.is_lt); mksel("PKT", col(WB_))
     ts(col(WC_), oh(2), 1024.0, col(WB_), A.mult, A.add); ts(col(WD_), oh(3), 2048.0, col(WC_), A.mult, A.add); mksel("PKR", col(WD_))
@@ -198,7 +202,7 @@ def build():
         for a, z, k0, k1 in which: dma(ap("R", slice(RO + a, RO + z), p=slice(f, 128, 16)), src(k0, k1), "y")
     ei = lambda h: ap("EI", h, slice(0, 192)); e0 = lambda h: ap("E0", h, slice(0, 192))
     ts(ap("NSW"), ei(0), 1536.0, 4096.0, A.is_lt, A.mult); tt(c("T2", 0, 192), ei(1), ap("NSW"), A.add); tt(e0(0), ei(0), c("T2", 0, 192), A.min)
-    ev(ap("EB"), e0(0), -256.0, eng="v"); to_row(0, lambda a, z: c("EB", a, z), runs[:2])
+    ev(ap("EB"), e0(0), -256.0, eng="v"); to_row(0, lambda a, z: c("EB", a, z), runs[:3])
     tt(ap("SWF"), ei(0), ap("NSW"), A.subtract); tt(e0(1), ei(1), ap("SWF"), A.max); cp(e3("EU0", 0, 192), e3("E0", 0, 192))
     ev(ap("ETA", 0, slice(0, 192)), ap("NSW"), 0.5, -1.0 / 16384); ev(ap("ETA", 1, slice(0, 192)), ap("NSW"), 0.25, 1.0 / 16384)
     ev(ap("FC"), ap("ONE"), 0.0, 5.0 - FO, "v"); ts(ap("EB"), e0(1), 1536.0, 16.0, A.is_ge, A.mult); ts(ap("FC", 1, slice(0, 192)), ap("EB"), 5.0 - FO, None, A.add)
@@ -206,22 +210,21 @@ def build():
     gat(ap("GT"), ap("R"), ap("TW"))
     mm(compact(ps(6, 0, 24), "PKT", "GT", 0, 24))
     ts(ap("OWU"), ps(6, 0, 24), 256.0, None, A.add); ev(ap("OWN"), ps(6, 0, 24), 256.0)
-    lst = across(ps(7, LW, 192), "S", "Y0N", 0, MW)
-    for j in range(4): mm(lst[4 * j:4 * j + 4], j == 0, j == 3)
-    mm(across(ps(7, 0, LW), "S", "Y0N", B0, LW))
+    for a, z, k0, k1 in (runs[1], runs[0], runs[2]): mm(across(ps(7, k0, k1), "S", "Y0N", a, k1 - k0))
     act(c("LV0", 0, 192), ps(7, 0, 192), F.Sign, -175.5, acc=col(LA))
 
     def cells_ahead(t):
         C = 512 + 256 * t
         mm(compact(ps(0, 0, C // 16), "S", "XT", 0, C // 16)); ev(c("SX", 0, C // 16), ps(0, 0, C // 16), THETA[t] + 6144.0, -1.0)
-        for d in range(3): gat(ap("SN%d" % (t % 2), d, slice(0, 128)), c("XT", 0, C), c("OWU", 8 * d, 8 * d + 8))
+    def twins_ahead(t):
+        for d in range(3): gat(ap("SN%d" % (t % 2), d, slice(0, 128)), c("XT", 0, 512 + 256 * t), c("OWU", 8 * d, 8 * d + 8))
     def count_ahead(t):
         o = ps(7, 0, 1); Kc = 32 + 16 * t
         mm([(o, fmat("O", 0.5), col(LA + s)) for s in range(3 if t else 1)] + ([(o, fmat("O", 1.0 / 32), col(LIA))] if t else []))
         ts(c("CI", 2, 3), o, 1.0 / 32, None, A.mult); ts(col(THR), c("CI", 2, 3), -32.0, o, A.mult, A.add)
         ts(col(LQ), col(THR), 6128.5, None, A.add); ts(c("NSX", 0, Kc), c("SX", 0, Kc), col(THR), None, A.add)
-    cells_ahead(0); count_ahead(0)
-    for a, z, k0, k1 in runs[:2]:
+    cells_ahead(0); twins_ahead(0); count_ahead(0)
+    for a, z, k0, k1 in (runs[2], runs[1], runs[0]):
         for r in range(16): ev(c("WB", 16 * k0 + r, 16 * k1, 16), c("Y0N", a + (k1 - k0) * r, a + (k1 - k0) * (r + 1)), 192.0)
     ev(ap("FR"), c("Y0N", 0, 1024), 1532.5)
     for a in (0, 512): mm([(ps(1 + a // 512, 0, 512), idm(1), c("Y0N", a, a + 512)), (ps(1 + a // 512, 0, 512), idm(-1), c("FR", a, a + 512))])
@@ -286,7 +289,7 @@ def build():
         def cut(a, z, n):
             e = [a + 2 * ((z - a) * j // (2 * n)) for j in range(n)] + [z]
             return list(zip(e[:-1], e[1:]))
-        part = [(0, LW), (LW, LW + P["mid"][t]), (LW + P["mid"][t], K)]
+        part = [(128, K), (0, 128)]; span = [(128, K), (0, MW), (MW, 128)]
         def upto(a, z, n): return cut(a, z, -(-(z - a) // n))
         def slot(j):
             pool = P[("abank", "bbank")[j]]; b = pool[reg[j] % len(pool)]; reg[j] += 1
@@ -307,39 +310,45 @@ def build():
                     a16, z16 = 16 * x, 16 * y; n = z16 - a16; hz, wz, wa = (2, "HZ", a16), (-1, "WZ", a16), (-1, "WA", a16)
                     for j, terms in ((1, [hz, wa]), (2, [hz, wz]), (0, [hz, wa, wz])):
                         o = slot(0); wide(o, n, terms); act(c("AB", 3840 * j + a16, 3840 * j + z16), c("PS", o, o + n), F.Abs, 140.0 - 12 * len(terms))
-            dec = ps(XB, 0, 2 * Ks)
-            for h in (0, 1): mm(compact(ps(XB, Ks * h, Ks * h + Ks), "PKW", ("WA", "WZ")[h], 16 * k0, Ks))
+            XB = P["xb"][s]
+            for h in (0, 1): mm([(pt(XB, 128 * h + r, 128 * h + 128, Ks, 16), c(("WA", "WZ")[h], 16 * k0 + r, 16 * k1, 16), s8("PKW")) for r in range(16)], each=True)
             tag[0] = "f%d" % s
-            ts(e3("FL", k0, k1), dec, 1.0 / 256, FO - t + 8.5 / 256, A.mult, A.add); ev(e3("FF", k0, k1), dec, -120.0)
-            o = ps(XB, 2 * Ks, 3 * Ks)
-            mm([(o, idm(512), c(LV, k0, k1))] + [(o, idm(1), ap("FL", h, slice(k0, k1))) for h in range(2)])
-            act(c("TT", k0, k1), o, F.Sign, -(2.0 * (FO - t - 204) + 42.5 + 512))
-            mm([(dec, idm(-256), e3("FL", k0, k1)), (dec, idm(-256), e3("FC", k0, k1)), (dec, fmat("I", 1.0), e3("FF", k0, k1))], stop=False)
-            for j in (3, 1, 2, 0):
-                o = ps(YB, Ks * j, Ks * j + Ks); lst = [(o, idm(1), ap("ETA", j - 1, slice(k0, k1))) if j else (o, idm(1024), c(LV, k0, k1))]
-                if j == 3 and P["relu"][s]: lst += [(o, idm(2048), c("ONE", 0, Ks))] + compact(o, "S4", "AB", 3840 * 3 + 16 * k0, Ks) + compact(o, "SN", "HZ", 16 * k0, Ks)
-                else: lst += compact(o, "S", "AB", 3840 * j + 16 * k0, Ks)
-                mm(lst)
+            tn = lambda b, j, n=1: ap(b, s, slice(128 * j, 128 * (j + n)), p=slice(0, Ks)); dec = ps(XB, 0, 2 * Ks)
+            ts(tn("FL", 0, 2), pt(XB, 0, 256, Ks), 1.0 / 256, FO - t + 8.5 / 256, A.mult, A.add)
+            o = pt(XB, 256, 384, Ks)
+            mm([(o, c(LV, k0, k1), idm(512))] + [(o, top(idm(1), Ks), tn("FL", h)) for h in range(2)])
+            act(tn("TT", 0), o, F.Sign, -(2.0 * (FO - t - 204) + 42.5 + 512))
+            ev(tn("FF", 0, 2), pt(XB, 0, 256, Ks), -120.0)
+            mm([(dec, idm(-256), e3("FC", k0, k1))] + [(ps(XB, Ks * h, Ks * h + Ks), tn(b, h), top(m, Ks)) for h in range(2) for b, m in (("FL", idm(-256)), ("FF", fmat("I", 1.0)))], stop=False)
+            mm([(pt(YB, 0, 384, Ks), c(LV, k0, k1), ap("I3"))] + [(pt(YB, 128 * j, 128 * j + 128, Ks), ap("ETA", j, slice(k0, k1)), idm(1)) for j in range(3)], stop=False)
+            turned = lambda j, b, a, m: [(pt(YB, 128 * j + r, 128 * j + 128, Ks, 16), c(b, a + 16 * k0 + r, a + 16 * k1, 16), s8(m)) for r in range(16)]
+            if P["relu"][s]: mm([(pt(YB, 256, 384, Ks), c("ONE", 0, Ks), mat("O", 128.0))] + turned(2, "AB", 3840 * 3, "S4") + turned(2, "HZ", 0, "SN"), False, False)
+            else: mm(turned(2, "AB", 3840 * 3, "S"), False, False)
+            for j in (1, 2): mm(turned(j - 1, "AB", 3840 * j, "S"), False, False)
+            mm([(pt(YB, r, 384, Ks, 16), c("AB", 16 * k0 + r, 16 * k1, 16), ap("S24")) for r in range(16)], start=False)
         def decide(s):
             tag[0] = "d%d" % s
-            k0, k1 = part[s]; Ks = k1 - k0; dec = ps(XB, 0, 2 * Ks)
-            S_ = lambda j: ap("SS", j, slice(0, Ks)); P_ = lambda j: ps(YB, Ks * j, Ks * j + Ks); Q_ = lambda j: ap("EQ", j - 1, slice(k0, k1))
-            ev(S_(0), P_(0), -1024.0)
-            for j in (1, 2, 3): tt(S_(j), P_(j), S_(j - 1), A.min)
-            for j in (3, 1, 2): tt(Q_(j), P_(j), S_(3), A.is_equal)
+            k0, k1 = part[s]; Ks = k1 - k0; XB = P["xb"][s]; dec = ps(XB, 0, 2 * Ks)
+            tn = lambda b, j, n=1: ap(b, s, slice(128 * j, 128 * (j + n)), p=slice(0, Ks))
+            S_ = lambda j: ap("SS", j - 1, slice(0, 128), p=slice(0, Ks)); T_ = lambda j: pt(YB, 128 * j - 128, 128 * j, Ks); Q_ = lambda j: tn("EQ", j - 1); P_ = lambda j: ps(YB, Ks * j, Ks * j + Ks)
+            ts(S_(1), T_(1), -1024.0, None, A.min)
+            for j in (2, 3): tt(S_(j), T_(j), S_(j - 1), A.min)
+            for j in (3, 1, 2): tt(Q_(j), T_(j), S_(3), A.is_equal)
             sg = 1.0 if t % 2 == 0 else -1.0; pole = ((2, 3), (1, 3))
             for h in (1, 0):
-                mm([(P_(h), l, x) for l, x in [(idm(1), ap(E, h, slice(k0, k1))), (idm(4096 * sg), c("TT", k0, k1))] + [(idm(1920), Q_(j)) for j in pole[h]]])
+                mm([(P_(h), l, x) for l, x in [(idm(1), ap(E, h, slice(k0, k1))), (tn("TT", 0), top(idm(4096 * sg), Ks))] + [(Q_(j), top(idm(1920), Ks)) for j in pole[h]]])
+            mm([(P_(2), Q_(3), top(idm(1), Ks))])
             cs = LOO - 4096.0 if t % 2 == 0 else 4096.0; mo = A.max if t % 2 == 0 else A.min
             ts(ap("IX", 1, slice(k0, k1)), P_(1), cs, float(CST if t % 2 == 0 else CST2 - LOO), A.add, mo)
             tt(c("IA", 0, Ks), P_(0), c("ALT", 256 * (t % 2) + k0, 256 * (t % 2) + k1), mo); ts(ap("IX", 0, slice(k0, k1)), c("IA", 0, Ks), cs, None, A.add)
-            mm([(ps(XB, Ks * h, Ks * h + Ks), idm(2048), Q_(j)) for h in range(2) for j in pole[h]], start=False)
+            ev(c("EC", k0, k1), P_(2))
+            mm([(ps(XB, Ks * h, Ks * h + Ks), Q_(j), top(idm(2048), Ks)) for h in range(2) for j in pole[h]], start=False)
             relu(e3("TR", k0, k1), dec, 1.0 - base)
             tt(e3(En, k0, k1), dec, e3(E, k0, k1), A.max)
             if t < 3: cp(e3(EUn, k0, k1), e3(En, k0, k1))
         def phase_b(s):
             tag[0] = "b%d" % s
-            k0, k1 = part[s]; how = P["bmode"][s]
+            k0, k1 = span[s]; how = P["bmode"][s]
             for (a, z) in upto(k0, k1, P["bw"][s]):
                 a16, z16 = 16 * a, 16 * z; n = z16 - a16; D = lambda j: c("D", 3840 * j + a16, 3840 * j + z16); d_ = lambda w, j: (w, "D", 3840 * j + a16)
                 gat(D(0), win, ap("IX", 1, slice(a, z)))
@@ -354,7 +363,7 @@ def build():
                 ev(ydst(a16, z16), c("PS", o, o + n), 95.75)
         y_ = ydst(0, 16); yb, y0 = y_[0], y_[2][0].start
         def alive(s):
-            k0, k1 = part[s]; Ks = k1 - k0; o = slot(1); o = c("PS", o, o + Ks)
+            k0, k1 = span[s]; Ks = k1 - k0; o = slot(1); o = c("PS", o, o + Ks)
             mm(compact(o, "S", yb, y0 + 16 * k0, Ks))
             act(c(LVn, k0, k1), o, F.Sign, -3247.5, acc=col(LA + s) if t < 3 else None)
         def live_row():
@@ -362,7 +371,7 @@ def build():
             for j in range(nb):
                 bk = (XB, YB)[j]; x = c("R", RO + B0 + 512 * j, RO + B0 + 512 * j + 512)
                 mm([(ps(bk, 0, 512), sh("SC", 3), ap("ONE")), (ps(bk, 0, 512), HOLE, x)], stop=False)
-                mm([(ps(bk, LW * r, LW * r + LW), sh("S2", 3), c(yb, y0 + per * j + r, y0 + 16 * LW, 16)) for r in range(per)], start=False)
+                mm([(ps(bk, LW * r, LW * r + LW), sh("S2", 3), c(yb, y0 + B0 + per * j + r, y0 + 2048, 16)) for r in range(per)], start=False)
                 ts(x, ps(bk, 0, 512), col(LO_), col(HI_), A.max, A.min)
         def cells_on():
             tag[0] = "c"
@@ -378,27 +387,30 @@ def build():
             for a in range(0, Cn, 1024):
                 z = min(Cn, a + 1024); ts(c("XT", a, z), c("PS", a, z), 0.0, 63.0, A.max, A.min)
         def to_rows(fs, which):
-            for f in fs: to_row(f, (lambda a, z: ap("TR", 0, slice(a, z)), lambda a, z: ap("TR", 1, slice(a, z)), lambda a, z: ap("EQ", 2, slice(a, z)), lambda a, z: c(LVn, a, z))[f], which)
-        phase_a(1); decide(1); phase_a(2); phase_b(1); decide(2); to_rows((0, 1, 2), runs[1:2 + t]); phase_a(0); alive(1); decide(0); to_rows((0, 1, 2), runs[:1])
-        phase_b(2); alive(2); to_rows((3,), runs[1:2 + t]); cells_on()
+            for f in fs: to_row(f, (lambda a, z: ap("TR", 0, slice(a, z)), lambda a, z: ap("TR", 1, slice(a, z)), lambda a, z: c("EC", a, z), lambda a, z: c(LVn, a, z))[f], which)
+        phase_a(0); decide(0); to_rows((0, 1, 2), runs[2:3 + t]); phase_a(1); phase_b(0); alive(0); to_rows((3,), runs[2:3 + t]); decide(1); to_rows((0, 1, 2), runs[:2])
+        cells_on()
+        if t < 3: cells_ahead(t + 1)
+        phase_b(1); alive(1); to_rows((3,), runs[1:2])
         tag[0] = "t"
-        if t < 3:
-            gat(ap("GT"), ap("R"), ap("TW"))
-            o = ps(1, 0, 24); mm(compact(o, "PKT", "GT", 0, 24))
-            ts(ap("TA"), o, 0.5, base - 1.0, A.is_gt, A.mult); tt(ap("TB"), o, ap("TA"), A.add); tt(ap("OWN"), ap("TB"), ap("OWN"), A.max); cp(ap("OWU"), ap("OWN"))
-            cells_ahead(t + 1)
-        else:
+        if t == 3:
             ef = lambda h: ap("EF", h, slice(0, 192))
             tt(c("T2", 0, 192), ef(0), ap("NSW"), A.add); tt(ef(1), ef(1), c("T2", 0, 192), A.min); tt(ef(0), ef(0), ap("SWF"), A.max)
             for h in range(2):
-                for a, z, k0, k1 in runs[:5]: dma(ap("ye", slice(a, z), p=slice(h, 16, 2)), ap(En, h, slice(k0, k1)), "y")
-        phase_b(0)
+                for a, z, k0, k1 in runs[:6]: dma(ap("ye", slice(a, z), p=slice(h, 16, 2)), ap(En, h, slice(k0, k1)), "y")
+        phase_b(2)
+        if t < 3 or not P["direct"]: alive(2)
         if P["direct"]: live_row()
-        if t < 3 or not P["direct"]: alive(0)
         if not P["direct"]: to_rows((3,), runs[:1])
-        if t < 3: count_ahead(t + 1)
+        if t < 3:
+            count_ahead(t + 1)
+            tag[0] = "t"
+            gat(ap("GT"), ap("R"), ap("TW"))
+            o = ps(YB, 0, 24); mm(compact(o, "PKT", "GT", 0, 24))
+            ts(ap("TA"), o, 0.5, base - 1.0, A.is_gt, A.mult); tt(ap("TB"), o, ap("TA"), A.add); tt(ap("OWN"), ap("TB"), ap("OWN"), A.max); cp(ap("OWU"), ap("OWN"))
+            twins_ahead(t + 1)
         else:
-            for a, z, k0, k1 in (runs[1], runs[0]):
+            for a, z, k0, k1 in (runs[2], runs[1], runs[0]):
                 for r in range(16): ev(c("Y0N", a + (k1 - k0) * r, a + (k1 - k0) * (r + 1)), c("YF", 16 * k0 + r, 16 * k1, 16), -192.0)
                 dma(ap("yy", slice(a, z), p=slice(0, 128)), c("Y0N", a, z), "y")
             gat(c("FR", 0, 768), c("YF", 3072, 3840), c("ULAST", 0, 48), -192.0)
@@ -408,13 +420,13 @@ def build():
         tag[0] = "s"
         mm([(ps(2, 0, 512), idm(-1), ap("ONE")), (hp(2, 0), idm(2048), c("NXT", 256 * t, 256 * t + 256))] + ([(hp(2, h), idm(1), ap("LI")) for h in range(2)] if t < 3 else []), stop=False)
         for j in range(4):
-            gat(c("SG", 1024 * j, 1024 * j + 1024), ap("R"), c("OLU", 64 * j, 64 * j + 64))
-            o = ps(j // 2, 64 * (j % 2), 64 * (j % 2) + 64)
-            mm([(o, idm(-1), c("IO1", 64 * j, 64 * j + 64))] + compact(o, "PKR", "SG", 1024 * j, 64))
-        for u in range(2):
-            o = ps(u, 0, 128); a = 128 * u
-            ts(sm(0, a, a + 128), o, 0.0, None, A.is_gt); ts(sm(1, a, a + 128), o, 2048.0, None, A.is_equal); ts(sm(2, a, a + 128), o, 2560.0, None, A.is_ge)
-            mm(kept(2, "O", 128.0, a, a + 128), False, u == 1)
+            gat(c("D", 1024 * j, 1024 * j + 1024), ap("R"), c("OLU", 64 * j, 64 * j + 64))
+            o = ps((0, 0, 1, 5)[j], 64 * (j == 1), 64 * (j == 1) + 64)
+            mm([(o, idm(-1), c("IO1", 64 * j, 64 * j + 64))] + compact(o, "PKR", "D", 1024 * j, 64))
+        for bk, a, z in ((0, 0, 128), (1, 128, 192), (5, 192, 256)):
+            o = ps(bk, 0, z - a)
+            ts(sm(0, a, z), o, 0.0, None, A.is_gt); ts(sm(1, a, z), o, 2048.0, None, A.is_equal); ts(sm(2, a, z), o, 2560.0, None, A.is_ge)
+            mm(kept(2, "O", 128.0, a, z), False, z == 256)
         if t < 3: act(ap("T2"), ps(2, 0, 512), F.Relu, -2047.0, acc=col(LOST))
 
     def books(t):
@@ -478,7 +490,7 @@ def settle(ops, rounds=8):
     for i, o in enumerate(ops):
         for d, hard in o["deps"].items(): kids[d][i] = hard
     tail = [far if o["kind"] == "arrive" else o["x"] if o["kind"] == "dma" else 0.0 for o in ops]
-    def lay(key, back):
+    def lay(key, back, due=None):
         lines = {e: ([], []) for e in "vspqy"}; st = [0.0] * n; en = [0.0] * n; eng = [None] * n
         for i in sorted(range(n), key=key):
             o = ops[i]; near = kids[i] if back else o["deps"]; best = None
@@ -486,7 +498,8 @@ def settle(ops, rounds=8):
                 t0 = max([en[d] + (lat if hard or eng[d] != e else 0.0) for d, hard in near.items()] + [0.0]) + (tail[i] if back else 0.0)
                 a, z = lines[e]; j = int(np.searchsorted(z, t0, side="right")) if z else 0; x = t0
                 while j < len(a) and a[j] < x + v[1]: x = max(x, z[j]); j += 1
-                sc = x + v[1] * (bias if e == "v" else 1.0)
+                if due is None: sc = x + v[1] * (bias if e == "v" else 1.0)
+                else: sc = max(x + v[1], due[i] - P["slack"]) + {"v": P["tilt"] * v[1], "q": 1e-3 * v[1]}.get(e, 0.0)
                 if best is None or sc < best[0]: best = (sc, x, e, j)
             if best is None: st[i] = en[i] = max([en[d] + lat for d in near] + [0.0]) + (tail[i] if back else 0.0)
             else:
@@ -497,9 +510,15 @@ def settle(ops, rounds=8):
     for i in range(n - 1, -1, -1):
         pr[i] = min([v[1] for v in ops[i]["alts"].values()] + [0.0] * (not ops[i]["alts"])) + tail[i] + lat + max([pr[k] for k in kids[i]] + [0.0])
     st, en, eng = lay(lambda i: (-pr[i], i), False); top = (max(en), st, en, eng)
-    for k in range(rounds):
-        sb, eb, x = lay(lambda i: (-en[i], -i), True)
-        st, en, eng = lay(lambda i: (-eb[i], i), False)
+    rng = np.random.default_rng(1)
+    for k in range(P["rounds"]):
+        on = P["due"] and k >= 2
+        if k >= 4 and P["shake"] and max(en) > top[0] + P["temp"]: st, en = top[1:3]
+        sb, eb, x = lay(lambda i: (-en[i], -i), True, [max(en) - a for a in st] if on else None)
+        if k >= 4 and P["shake"]:
+            nz = rng.random(n) * P["shake"]
+            for i in range(n - 1, -1, -1): eb[i] = max([eb[i] + float(nz[i])] + [eb[j] for j in kids[i]])
+        st, en, eng = lay(lambda i: (-eb[i], i), False, [max(eb) - a + b for a, b in zip(sb, tail)] if on else None)
         if max(en) < top[0]: top = (max(en), st, en, eng)
     busy = {e: 0.0 for e in "vspqy"}
     for o, s, z, e in zip(ops, top[1], top[2], top[3]):

@@ -9,31 +9,32 @@ BF, HF, F32, I32, U16 = "bfloat16", "float16", "float32", "int32", "uint16"
 CST, LOO, HIO, CST2, YBO, WBW = 3584, 3600, 5520, 7440, 7456, 11296
 RO, RW_ = 192, 4032
 FO = 1500
-NMAT = 34
+NMAT = 33
 SB = {
-    "Y0N": ([3072], BF), "WB": ([WBW], BF), "YF": ([4096], BF), "HH": ([1920], BF), "WP": ([1920], F32), "XT": ([1536], BF), "P2": ([1280], BF),
-    "UH": ([3840], HF), "WA": ([3840], HF), "WZ": ([3840], HF), "HZ": ([3840], BF), "AB": ([4 * 3840], BF), "D": ([3 * 3840], BF),
+    "Y0N": ([3072], BF), "WB": ([WBW], BF), "YF": ([4096], BF), "HH": ([1920], BF), "WP": ([1920], F32), "XT": ([1536], BF), "P2": ([1280], BF), "DT": ([4 * 272], BF),
+    "UH": ([3840], HF), "WA": ([3840], HF), "WZ": ([3840], BF), "HZ": ([3840], BF), "AB": ([4 * 3840], BF), "D": ([3 * 3840], BF),
     "R": ([RW_], BF), "BL": ([1536], F32), "DR": ([1024], BF), "FR": ([1024], BF), "BTG": ([1280], BF), "NXT": ([1024], BF), "BC": ([4], F32), "IO1": ([512], BF),
-    "EI": ([2, 192], I32), "BI": ([512], I32), "SI": ([24], I32), "NSW": ([192], F32), "SWF": ([192], F32), "EB": ([192], BF), "FC": ([2, 256], HF),
+    "EI": ([2, 192], I32), "BI": ([512], I32), "SI": ([24], I32), "NSW": ([192], F32), "SWF": ([192], F32), "EB": ([192], BF), "FK": ([2, 256], BF),
     "E0": ([2, 256], HF), "E1": ([2, 256], HF), "EF": ([2, 256], F32), "EU0": ([2, 256], U16), "EU1": ([2, 256], U16),
     "LV0": ([256], BF), "LV1": ([256], BF), "EQ": ([2, 384], BF), "EC": ([256], BF), "TR": ([2, 256], BF), "IX": ([2, 256], U16),
-    "SS": ([3, 128], F32), "FL": ([2, 256], HF), "FF": ([2, 256], F32), "TT": ([2, 128], BF), "IA": ([128], F32), "I3": ([384], BF), "S24": ([24], BF),
+    "SS": ([3, 128], F32), "FL": ([2, 512], HF), "Z32": ([32], BF), "JI": ([16], I32), "BJ": ([2, 128], I32), "FF": ([2, 256], F32), "TT": ([2, 128], BF), "IA": ([128], F32), "I3": ([384], BF), "S24": ([24], BF),
     "JK": ([16, 80], BF), "SX": ([80], F32), "NSX": ([80], F32), "CA": ([80], BF), "CU": ([80], F32), "PL": ([96], F32), "UBT": ([80], U16),
-    "COL": ([32], F32), "QB": ([2], BF), "CI": ([8], I32), "OH": ([16], F32), "ACC": ([16], F32), "KI": ([16], U16), "NB": ([16], F32), "KT": ([96], BF), "KD": ([256], BF), "MK": ([256], BF),
+    "COL": ([40], F32), "QB": ([2], BF), "CI": ([8], I32), "OH": ([16], F32), "ACC": ([16], F32), "KI": ([16], U16), "NB": ([16], F32), "KT": ([96], BF), "KD": ([256], BF), "MK": ([256], BF),
     "DM": ([16], F32), "DL2": ([16], U16), "VR": ([16], HF), "DLM": ([16], U16), "NC": ([32], BF), "S16": ([64], F32), "NR": ([64], HF), "ULAST": ([64], U16),
-    "OLD": ([256], F32), "OLU": ([256], U16), "LIW": ([272], BF), "LI": ([256], BF), "SM": ([3, 256], BF), "NM": ([2, 256], BF), "T2": ([512], F32), "TVF": ([256], F32),
+    "OLD": ([256], F32), "OLU": ([256], U16), "O16": ([256], HF), "LP": ([1280], BF), "K2": ([512], HF), "LIW": ([272], BF), "LI": ([256], BF), "SM": ([3, 256], BF), "NM": ([2, 256], BF), "T2": ([512], F32), "TVF": ([256], F32),
     "TW": ([24], U16), "TA": ([24], F32), "TB": ([24], F32), "OWN": ([24], F32), "OWU": ([24], U16), "GT": ([384], BF),
-    "ONE": ([512], BF), "MAT": ([NMAT * 128], BF), "MF": ([4 * 128], F32), "SEL": ([11 * 144], BF), "ETA": ([3, 256], BF),
-    "BT": ([272], BF), "BD": ([2, 256], BF), "DT": ([4 * 272], BF), "VC": ([256], F32), "ALT": ([512], F32), "IO": ([16], F32), "IOM": ([256], F32), "ZE": ([80], F32),
-    "SN0": ([3, 256], BF), "SN1": ([3, 256], BF), "LN0": ([3, 256], BF), "LN1": ([3, 256], BF), "LN2": ([3, 256], BF), "LN3": ([3, 256], BF),
+    "ONE": ([512], BF), "MAT": ([NMAT * 128], BF), "MF": ([4 * 128], F32), "SEL": ([8 * 144], BF), "ETA": ([3, 256], BF),
+    "BT": ([272], BF), "VC": ([256], F32), "ALT": ([512], F32), "IO": ([16], F32), "IOM": ([256], F32), "ZE": ([80], F32),
+    "SN": ([4, 384], BF), "LN": ([8, 384], BF), "FA": ([2, 384], BF), "C3": ([384], BF), "W16": ([32], BF), "LC": ([16], BF),
 }
 SCRATCH = {k: ("sbuf", [128] + v[0], v[1]) for k, v in SB.items()}
 SCRATCH["PS"] = ("psum", [128, 4096], F32)
-NDMA = 120
-SEMAPHORES = ["v", "s", "p", "q"] + ["ar%d" % t for t in range(4)] + ["ls%d" % t for t in range(4)] + ["d%d" % i for i in range(NDMA)]
-SELS = ("S", "PKW", "PKR", "PKT", "P0", "P16", "RW", "S2", "SC", "S4", "SN")
-P = {"g": 1.4, "s": 3.0, "ov": 15.0, "gp": 32, "aw": 32, "abank": [0, 1], "bbank": [5, 6, 7], "bw": [32, 32, 16], "last": 32,
-     "bmode": [1, 1, 1], "relu": [0, 0, 0], "lat": 230.0, "far": 3000.0, "dma": 1300.0, "bias": 2.0, "war": 0, "direct": 1, "xb": [3, 2], "shake": 0.0, "rounds": 8, "temp": 500.0, "due": 1, "slack": 500.0, "tilt": 0.1}
+NDMA = 128
+SEMAPHORES = ["v", "s", "p", "q"] + ["ar%d" % t for t in range(8)] + ["ls%d" % t for t in range(8)] + ["d%d" % i for i in range(NDMA)]
+SELS = ("S", "PKW", "PKR", "P0", "P16", "RW", "S2", "SC")
+P = {"g": 1.4, "s": 3.0, "ov": 20.0, "pe": 0.42, "nz": 300.0, "gp": [32, 32], "aw": [32, 32], "zw": [32, 32, 32], "abank": [[0, 1, 2, 6, 7], [0, 1]], "bbank": [[5, 6, 7], [5, 6, 7], [5, 6, 7]], "newfirst": 2, "xat": 10, "lf": [1, 1, 0, 0], "lvfirst": 0, "chain": [0, 1], "ncdma": 1, "bw": [16, 16, 16], "last": 32,
+     "bmode": [1, 1, 1], "relu": [0, 0, 0], "lat": 240.0, "far": 3000.0, "dma": 1300.0, "bias": 2.0, "war": 0, "direct": 1, "xb": [3, 2], "rounds": 8, "tries": 1100, "part": 0.03, "every": 10, "due": 1, "slack": 800.0, "tilt": 0.1}
+GUESSES = ({"ov": 45.0, "lat": 170.0, "g": 1.1}, {"ov": 15.0, "lat": 230.0, "g": 1.4, "pe": 0.47}, {"ov": 45.0, "lat": 200.0, "g": 1.8, "s": 5.0, "dma": 1600.0, "far": 3500.0})
 CY, XB, YB = 0.83, 3, 4
 
 
@@ -92,12 +93,13 @@ def build():
         add({"v": (lambda g, r: g.vector.tensor_scalar(r(o), r(i), bias, 0.0, A.add, A.max), vc(o[3], half(o, i))),
              "s": (lambda g, r: g.scalar.activation(r(o), r(i), F.Relu, bias=bias), vc(o[3], 1))}, [i], [o])
     def gc_(n, e): return (50 if e == "v" else 65) + n * P["g"] * CY
-    def gat(o, w, off, add_=0.0, eng="vs"):
+    def total(o, i): add({"v": (lambda g, r: g.vector.tensor_reduce(r(o), r(i), AxisListType.X, A.add), vc(i[3], 1))}, [i], [o])
+    def gat(o, w, off, add_=0.0, eng="vs", mul=1.0):
         alts = {}
         if "v" in eng:
-            if add_: alts["v"] = (lambda g, r: g.vector.tensor_scalar(r(o), r(w).indirect(r(off)), add_, None, A.add), gc_(o[3], "v"))
+            if add_: alts["v"] = (lambda g, r: g.vector.tensor_scalar(r(o), r(w).indirect(r(off)), mul, add_, A.mult, A.add), gc_(o[3], "v"))
             else: alts["v"] = (lambda g, r: g.vector.tensor_copy(r(o), r(w).indirect(r(off))), gc_(o[3], "v"))
-        if "s" in eng: alts["s"] = (lambda g, r: g.scalar.activation(r(o), r(w).indirect(r(off)), F.Identity, bias=add_), gc_(o[3], "s"))
+        if "s" in eng: alts["s"] = (lambda g, r: g.scalar.activation(r(o), r(w).indirect(r(off)), F.Identity, bias=add_, scale=mul), gc_(o[3], "s"))
         add(alts, [w, off], [o])
     def gtt(o, w, off, i1, op):
         add({"v": (lambda g, r: g.vector.tensor_tensor(r(o), r(w).indirect(r(off)), r(i1), op), gc_(o[3], "v"))}, [w, off, i1], [o])
@@ -107,7 +109,7 @@ def build():
         def f(g, r):
             for j, (o, l, x) in enumerate(lst): ins = g.tensor.matmul(r(o), r(l), r(x), each or (start and j == 0), each or (stop and j == len(lst) - 1))
             return ins
-        add({"p": (f, sum(max(min(64, l[3]), x[3]) * 0.42 * (4 if size(x) == 4 else 1) for o, l, x in lst))}, [y for o, l, x in lst for y in (l, x)], [o for o, l, x in lst])
+        add({"p": (f, sum(max(min(64, l[3]), x[3]) * P["pe"] * (4 if size(x) == 4 else 1) for o, l, x in lst))}, [y for o, l, x in lst for y in (l, x)], [o for o, l, x in lst])
     def pt(bank, a, b, n, s=1): return ap("PS", slice(512 * bank + a, 512 * bank + b, s), p=slice(0, n))
     def top(m, n): a = m[2][0].start; return ap(m[0], slice(a, a + n), p=slice(0, n))
     def s8(name): j = 144 * SELS.index(name); return c("SEL", j + 15, j + 143, 16)
@@ -149,12 +151,11 @@ def build():
     LW = P["last"]; MW = 128 - LW; B0 = 16 * MW
     runs = [(B0, 2048, MW, 128), (0, B0, 0, MW), (2048, 3072, 128, 192)] + [(3072 + 256 * u, 3328 + 256 * u, 192 + 16 * u, 208 + 16 * u) for u in range(4)]
 
-    for j in range(4): dma(c("Y0N", 768 * j, 768 * j + 768), ap("y0", slice(768 * j, 768 * j + 768), p=slice(0, 128)), "ys"[j % 2])
-    for h in range(2):
-        for a, z, k0, k1 in runs[:3]: dma(ap("EI", h, slice(k0, k1)), ap("en0", slice(a, z), p=slice(h, 16, 2)), "ys"[h])
-    dma(c("XT", 0, 512), ap("x0", slice(0, 512), p=slice(0, 128)), "s")
-    dma(ap("SI"), ap("snd", slice(0, 24), p=slice(0, 128)), "s")
-    dma(ap("BI"), ap("bl0", slice(0, 512), p=slice(0, 128)), "y")
+    loads = [(ap("EI", h, slice(k0, k1)), ap("en0", slice(a, z), p=slice(h, 16, 2))) for a, z, k0, k1 in runs[:3] for h in range(2)] + [(ap("SI"), ap("snd", slice(0, 24), p=slice(0, 128)))]
+    loads += [(c("Y0N", 768 * j, 768 * j + 768), ap("y0", slice(768 * j, 768 * j + 768), p=slice(0, 128))) for j in range(4)]
+    loads.insert(P["xat"], (c("XT", 0, 512), ap("x0", slice(0, 512), p=slice(0, 128))))
+    for j, (o, i) in enumerate(loads):
+        dma(o, i, "ys"[j % 2], sum(x[3] * size(x) * 100 for x, y in loads[:j + 1])); ops[-1]["rd"].append(c("CI", 4 + j % 2, 5 + j % 2)); ops[-1]["wr"].append(c("CI", 4 + j % 2, 5 + j % 2)); ops[-1]["row"] = True
     fill(ap("ONE"), 1.0, "v")
     iota(c("CI", 0, 1), [[1, 1]], 0, 1)
     ONES, TRI, TM, TF, HOLE = mat("O"), mat("T"), mat("M"), mat("F"), mat("H")
@@ -163,7 +164,7 @@ def build():
     sel(idm(1), c("ONE", 0, 128), [[-1, 128]], A.is_equal, 0, 1)
     sel(TRI, ONES, [[1, 128]], A.is_gt, 0, -1)
     ts(c("CI", 1, 2), c("CI", 0, 1), 15, None, A.bitwise_and); cp(col(PM), c("CI", 1, 2))
-    iota(ap("IO"), [[1, 16]], 0, 0)
+    iota(ap("IO"), [[1, 16]], 0, 0); fill(c("TB", 0, 16), 2.0)
     ts(ap("OH"), ap("IO"), col(PM), None, A.is_equal)
     fill(ap("SEL"), 0.0, "v")
     def mksel(name, w1, w2=None):
@@ -173,7 +174,9 @@ def build():
     mksel("S", 1.0); mksel("P0", oh(0)); mksel("P16", oh(0), 16.0)
     for j in range(3): ev(c("I3", 128 * j, 128 * j + 128), idm(1), 0.0, -1024.0); ev(c("S24", 8 * j, 8 * j + 8), s8("S"), 0.0, -1.0)
     ts(col(WA_), oh(1), 16.0, oh(0), A.mult, A.add); mksel("PKW", col(WA_), 256.0)
-    ts(col(WB_), col(PM), 2.0, None, A.is_lt); mksel("PKT", col(WB_))
+    ev(c("W16", 0, 8), s8("PKW")); ts(c("W16", 8, 16), s8("S"), oh(2), None, A.mult); ev(c("W16", 16, 24), s8("PKW")); fill(ap("C3"), 0.0); ev(c("C3", 128, 256), idm(1), 0.0, 32.0)
+    if 1 in P["chain"]: ts(c("W16", 24, 32), s8("S"), oh(2), 2.0, A.mult, A.mult)
+    ts(col(WB_), col(PM), 2.0, None, A.is_lt)
     ts(col(WC_), oh(2), 1024.0, col(WB_), A.mult, A.add); ts(col(WD_), oh(3), 2048.0, col(WC_), A.mult, A.add); mksel("PKR", col(WD_))
     ts(col(WE_), col(PM), -256.0, None, A.add); mksel("RW", col(WE_))
     if any(P["relu"]): mksel("S4", 4.0); mksel("SN", -2.0)
@@ -187,83 +190,109 @@ def build():
     iota(c("T2", 0, 4), [[256, 4]], 3071, 0); ts(col(CB_), col(PM), -16384.0, None, A.mult); ts(ap("BC"), c("T2", 0, 4), col(CB_), None, A.add)
     iota(ap("IO1"), [[0, 2], [1, 256]], 1, 0); iota(ap("IOM"), [[1, 256]], -4095, 0); iota(ap("KT"), [[1, 96]], 0, 0)
     for a in range(0, RW_, 1008): fill(c("R", a, a + 1008), 0.0)
+    ev(ap("K2"), ap("ONE"), 0.0, 1366.0, "v")
     fill(ap("ZE"), 0.0); fill(ap("PL"), 0.0); fill(c("LIW", 256, 272), 192.0)
     fill(ap("ETA", 2, slice(0, 256)), 0.75)
     for j in range(2): fill(ap("ETA", j, slice(192, 256)), 0.25 * (j + 1))
     fill(c("WB", CST, CST + 16), 192.0); fill(c("WB", CST2, CST2 + 16), 192.0)
-    for a in (512, 1024): fill(c("WP", a, a + 512), -12.0); fill(c("BL", a, a + 512), -1.0); fill(c("WB", HIO + a, HIO + a + 512), 0.0)
+    for a in (512, 1024): fill(c("WP", a, a + 512), 0.0); fill(c("BL", a, a + 512), -1.0); fill(c("HH", a, a + 512), 64.0)
     for t in range(4): fill(c("DT", 272 * t, 272 * t + 256), 128.0 + DELTA[t]); fill(c("DT", 272 * t + 256, 272 * t + 272), 128.0)
     iota(c("T2", 256, 512), [[16, 256]], 0, 0); ts(ap("VC"), c("T2", 256, 512), col(PM), None, A.add)
     ev(c("ALT", 0, 256), ap("VC"), 4096.0 - LOO); ev(c("ALT", 256, 512), ap("VC"), YBO - LOO - 4096.0); ev(ap("NB"), c("VC", 0, 16), -0.5, -1.0)
-    fill(ap("BT"), 0.0); iota(ap("BD", 0, slice(0, 256)), [[0, 16], [1, 16]], -8, 0); iota(ap("BD", 1, slice(0, 256)), [[1, 16], [0, 16]], -8, 0)
-    for h in range(2): dma(ap("BT", slice(0, 256), p=slice(h, 128, 16)), ap("BD", h, slice(0, 256), p=slice(h, 128, 16)), "y", 4096)
+    iota(ap("JI"), [[128, 2], [0, 8]], 0, 1); fill(ap("BJ"), 0, "v"); fill(c("BT", 256, 272), 0.0)
+    for j, (sh_, m) in enumerate([(0, 15), (4, 15)] + [(u, 1) for u in range(8)]):
+        ts(ap("BJ", slice(0, 2), slice(j, 128, 16)), ap("JI"), sh_, m, A.logical_shift_right, A.bitwise_and)
+    cp(ap("KD"), ap("BJ")); ts(col(WF_ + 8), col(WB_), -8.0, None, A.mult)
+    for h in range(2): mm([(ps(4, 128 * h, 128 * h + 128), c("KD", 128 * h, 128 * h + 128), idm(1))])
+    act(c("BT", 0, 256), ps(4, 0, 256), F.Identity, col(WF_ + 8))
+    D8, D256 = mat("D8"), mat("D256"); PW, IN = WF_ + 9, WF_ + 10
+    add({"v": (lambda g, r: g.vector.tensor_tensor_scan(r(c("TA", 0, 16)), r(c("ONE", 0, 16)), r(c("TB", 0, 16)), 0.0625, A.mult, A.mult), vc(16, 1))}, [c("ONE", 0, 16), c("TB", 0, 16)], [c("TA", 0, 16)])
+    tt(c("TB", 0, 16), c("TA", 0, 16), ap("OH"), A.mult); total(col(PW), c("TB", 0, 16))
+    for m, (a, z) in enumerate(((2, 5), (5, 8), (8, 10), (2, 10))):
+        total(col(IN + m), c("OH", a, z)); tt(col(IN + 4 + m), col(IN + m), col(PW), A.mult)
+        ts(c("Z32", 8 * m, 8 * m + 8), s8("S"), col(IN + 4 + m), (2.0, 0.25, 1.0 / 32, 16.0)[m], A.mult, A.mult)
+    ts(D8, idm(1), col(IN + 3), 0.125, A.mult, A.mult); ts(D256, idm(1), col(WB_), 1.0 / 256, A.mult, A.mult)
     iota(ap("S16"), [[256, 4], [1, 16]], 0, 0); ts(ap("ULAST"), ap("S16"), col(PM16), None, A.add); ts(ap("NR"), ap("S16"), col(PM16), 512.0, A.add, A.add)
     def to_row(f, src, which):
         for a, z, k0, k1 in which: dma(ap("R", slice(RO + a, RO + z), p=slice(f, 128, 16)), src(k0, k1), "y")
     ei = lambda h: ap("EI", h, slice(0, 192)); e0 = lambda h: ap("E0", h, slice(0, 192))
+    tt(c("TVF", 0, 192), ei(0), ei(1), A.min); ev(ap("EB"), c("TVF", 0, 192), -256.0); to_row(0, lambda a, z: c("EB", a, z), runs[:3])
     ts(ap("NSW"), ei(0), 1536.0, 4096.0, A.is_lt, A.mult); tt(c("T2", 0, 192), ei(1), ap("NSW"), A.add); tt(e0(0), ei(0), c("T2", 0, 192), A.min)
-    ev(ap("EB"), e0(0), -256.0, eng="v"); to_row(0, lambda a, z: c("EB", a, z), runs[:3])
     tt(ap("SWF"), ei(0), ap("NSW"), A.subtract); tt(e0(1), ei(1), ap("SWF"), A.max); cp(e3("EU0", 0, 192), e3("E0", 0, 192))
     ev(ap("ETA", 0, slice(0, 192)), ap("NSW"), 0.5, -1.0 / 16384); ev(ap("ETA", 1, slice(0, 192)), ap("NSW"), 0.25, 1.0 / 16384)
-    ev(ap("FC"), ap("ONE"), 0.0, 5.0 - FO, "v"); ts(ap("EB"), e0(1), 1536.0, 16.0, A.is_ge, A.mult); ts(ap("FC", 1, slice(0, 192)), ap("EB"), 5.0 - FO, None, A.add)
+    fill(ap("FK"), 0.0); ts(ap("FK", 1, slice(0, 192)), e0(1), 1536.0, 2.0, A.is_ge, A.mult)
     ts(ap("TW"), ap("SI"), float(RO), None, A.add)
     gat(ap("GT"), ap("R"), ap("TW"))
-    mm(compact(ps(6, 0, 24), "PKT", "GT", 0, 24))
+    mm(compact(ps(6, 0, 24), "P0", "GT", 0, 24))
     ts(ap("OWU"), ps(6, 0, 24), 256.0, None, A.add); ev(ap("OWN"), ps(6, 0, 24), 256.0)
     for a, z, k0, k1 in (runs[1], runs[0], runs[2]): mm(across(ps(7, k0, k1), "S", "Y0N", a, k1 - k0))
     act(c("LV0", 0, 192), ps(7, 0, 192), F.Sign, -175.5, acc=col(LA))
+    dma(ap("BI"), ap("bl0", slice(0, 512), p=slice(0, 128)), "y"); ops[-1]["rd"].append(c("Y0N", 0, 3072))
 
     def cells_ahead(t):
         C = 512 + 256 * t
-        mm(compact(ps(0, 0, C // 16), "S", "XT", 0, C // 16)); ev(c("SX", 0, C // 16), ps(0, 0, C // 16), THETA[t] + 6144.0, -1.0)
+        mm(compact(ps(0, 0, C // 16), "S", "XT", 0, C // 16)); ev(c("SX", 0, C // 16), ps(0, 0, C // 16), THETA[t] + 4128.0 + 1536 + 128 * t, -1.0)
     def twins_ahead(t):
-        for d in range(3): gat(ap("SN%d" % (t % 2), d, slice(0, 128)), c("XT", 0, 512 + 256 * t), c("OWU", 8 * d, 8 * d + 8))
+        send(2 * t, c("XT", 0, 512 + 256 * t))
+    def send(j, table):
+        gat(ap("SN", j % 4, slice(0, 384)), table, ap("OWU"))
+        add({"q": (None, 600)}, [ap("SN", j % 4, slice(0, 384))], [], "send", j)
+        add({}, [], [ap("LN", j, slice(0, 384))], "arrive", j)
     def count_ahead(t):
-        o = ps(7, 0, 1); Kc = 32 + 16 * t
-        mm([(o, fmat("O", 0.5), col(LA + s)) for s in range(3 if t else 1)] + ([(o, fmat("O", 1.0 / 32), col(LIA))] if t else []))
-        ts(c("CI", 2, 3), o, 1.0 / 32, None, A.mult); ts(col(THR), c("CI", 2, 3), -32.0, o, A.mult, A.add)
-        ts(col(LQ), col(THR), 6128.5, None, A.add); ts(c("NSX", 0, Kc), c("SX", 0, Kc), col(THR), None, A.add)
+        o = ps(YB, 0, 1); Kc = 32 + 16 * t
+        if t: mm([(o, fmat("O", 1.0 / 32), col(LIA))] + [(o, fmat("O", 0.5), col(LA + s)) for s in range(2)], stop=False)
+        mm([(o, fmat("O", 0.5), col(LA + (2 if t else 0)))], start=not t)
+        ts(c("NSX", 0, Kc), c("SX", 0, Kc), o, None, A.add)
+        if t: ts(col(LQ), o, 1536 + 128 * t + 4112.5, None, A.add)
+        else: ts(c("QB", 0, 1), o, -1.0, -1536 - 4112.5, A.mult, A.add)
     cells_ahead(0); twins_ahead(0); count_ahead(0)
     for a, z, k0, k1 in (runs[2], runs[1], runs[0]):
-        for r in range(16): ev(c("WB", 16 * k0 + r, 16 * k1, 16), c("Y0N", a + (k1 - k0) * r, a + (k1 - k0) * (r + 1)), 192.0)
+        for k in range(k0, k1, 32):
+            bk = (1, 2, 3)[k // 32 % 3]; u = a + k - k0
+            mm([(ps(bk, r, 512, 16), idm(1), c("Y0N", u + (k1 - k0) * r, u + (k1 - k0) * r + 32)) for r in range(16)], each=True); ev(c("WB", 16 * k, 16 * k + 512), ps(bk, 0, 512), 192.0)
     ev(ap("FR"), c("Y0N", 0, 1024), 1532.5)
     for a in (0, 512): mm([(ps(1 + a // 512, 0, 512), idm(1), c("Y0N", a, a + 512)), (ps(1 + a // 512, 0, 512), idm(-1), c("FR", a, a + 512))])
-    ev(ap("DR"), c("PS", 512, 1536), 1533.0)
+    ev(ap("DR"), c("PS", 512, 1536), 1564.5)
     cp(c("BL", 0, 512), ap("BI"))
     reg = [0, 0]
     sm = lambda j, a=0, z=256: ap("SM", j, slice(a, z)); nm = lambda j: ap("NM", j, slice(0, 256))
     hp = lambda b, h: ps(b, 256 * h, 256 * h + 256)
-    def kept(bank, kind, w, a=0, z=256):
-        return [(ps(bank, a, z), mat(kind, w), sm(0, a, z))] + [(ps(bank, 256 * h + a, 256 * h + z), mat(kind, (-w, w)[h]), sm(j, a, z)) for h in range(2) for j in (1, 2)]
+    def kept(bank, kind, w, a=0, z=256, n=256, a0=0):
+        return [(ps(bank, a - a0, z - a0), mat(kind, w), sm(0, a, z))] + [(ps(bank, n * h + a - a0, n * h + z - a0), mat(kind, (-w, w)[h]), sm(j, a, z)) for h in range(2) for j in (1, 2)]
     def names(t):
         return ("E%d" % (t % 2), "E%d" % (1 - t % 2) if t < 3 else "EF", "EU%d" % (t % 2), "EU%d" % (1 - t % 2), "LV%d" % (t % 2), "LV%d" % (1 - t % 2),
                 (lambda a, b: c("WB", YBO + a, YBO + b), lambda a, b: c("WB", a, b), lambda a, b: c("WB", YBO + a, YBO + b), lambda a, b: c("YF", a, b))[t])
 
     def who(t):
         tag[0] = "w"
-        C = 512 + 256 * t; Kc = C // 16; k_ = lambda b: c(b, 0, Kc); lost = col(LOST) if t else c("ZE", 0, 1)
-        ts(c("QB", 0, 1), lost, -1.0, col(LQ), A.mult, A.add); cp(c("QB", 1, 2), lost)
-        ts(k_("CA"), k_("NSX"), c("QB", 0, 1), c("QB", 1, 2), A.subtract, A.is_le)
+        C = 512 + 256 * t; Kc = C // 16; k_ = lambda b: c(b, 0, Kc); lost = col(LOST)
+        if t:
+            ts(c("QB", 0, 1), lost, col(LOST + 23), col(LQ), A.add, A.subtract); ts(c("QB", 1, 2), lost, col(LOST + 23), None, A.add)
+            relu(e3("NM", 192, 256), ps(6, 0, 128), -1920.0)
+            ts(k_("CA"), k_("NSX"), c("QB", 0, 1), c("QB", 1, 2), A.add, A.is_le)
+        else: ts(k_("CA"), k_("NSX"), c("QB", 0, 1), 0.0, A.add, A.is_le)
         mm([(ps(5, 0, Kc), ONES, k_("CA")), (ps(5, 0, Kc), TM, k_("CA")), (ps(5, 1, Kc), mat("M", -1.0), c("CA", 0, Kc - 1))]); mm([(ps(5, 128, 128 + Kc), ONES, k_("CA"))])
         scan(k_("PL"), ps(5, 0, Kc))
         ts(k_("UBT"), k_("PL"), 4095.0, 256.0, A.add, A.min)
         scan(k_("CU"), ps(5, 128, 128 + Kc))
-        SN, LN = "SN%d" % (t % 2), "LN%d" % t
-        h3 = lambda b, j: ap(b, slice(0, 3), slice(128 * j, 128 * j + 128))
-        gtt(c("P2", 0, C), c("DT", 272 * t, 272 * t + 272), k_("UBT"), c("XT", 0, C), A.add)
-        for d in range(3): gat(ap(SN, d, slice(128, 256)), c("P2", 0, C), c("OWU", 8 * d, 8 * d + 8))
-        add({"q": (None, 600)}, [ap(SN)], [], "send", t)
-        add({}, [], [ap(LN)], "arrive", t)
+        for a in range(0, C, 512): z = min(C, a + 512); gtt(c("P2", a, z), c("DT", 272 * t, 272 * t + 272), c("UBT", a // 16, z // 16), c("XT", a, z), A.add)
+        send(2 * t + 1, c("P2", 0, C))
         gat(c("BTG", 0, C), ap("BT"), k_("UBT"))
-        def tables(a, z, x, p2, b0, b1, dig):
-            ts(c("HH", a, z), p2, 191.0, 0.5, A.min, A.mult); ts(c("WB", HIO + a, HIO + z), p2, 191.0, -128.0, A.min, A.add)
-            o = ps(b0, 0, z - a); mm([(o, idm(2), x), (o, idm(-1), p2)]); relu(c("WB", LOO + a, LOO + z), o, 128.0)
-            o = ps(b1, 0, z - a)
-            mm([(o, idm(1), c("WB", HIO + a, HIO + z)), (o, idm(-1), c("WB", LOO + a, LOO + z))] + ([(o, idm(1.0 / 256), c("BTG", a, z))] if dig else []))
-            ev(c("WP", a, z), o, -12.0)
+        def tables(a, z, x, p2, b0):
+            ts(c("HH", a, z), p2, 191.0, 0.5, A.min, A.mult)
+            o = ps(b0, 0, z - a); mm([(o, idm(2), x), (o, idm(-1), p2)])
+            if P["lf"][a // 512]: relu(c("LP", a, z), o, 128.0); ev(c("WB", LOO + a, LOO + z), c("LP", a, z), -31.5)
+            else: ts(c("WB", LOO + a, LOO + z), o, 96.5, -31.5, A.add, A.max)
         for j, a in enumerate(range(0, C, 512)):
-            z = min(C, a + 512); tables(a, z, c("XT", a, z), c("P2", a, z), (6, 0, 5)[j], (7, 1, 6)[j], True)
-        tables(1536, 1920, h3(LN, 0), h3(LN, 1), 7, 5, False)
+            z = min(C, a + 512); tables(a, z, c("XT", a, z), c("P2", a, z), (6, 1, 6)[j]); o = ps((0, 5, 0)[j], 0, z - a)
+            mm([(o, idm(2), c("HH", a, z)), (o, idm(-1), c("LP", a, z) if P["lf"][j] else c("WB", LOO + a, LOO + z)), (o, D256, c("BTG", a, z))]); ev(c("WP", a, z), o, -64.0 if P["lf"][j] else -79.75, 0.5)
+        for a in range(0, C, 512):
+            z = min(C, a + 512); o = ps(5, 0, z - a); mm([(o, idm(2), c("HH", a, z)), (o, D8, c("BTG", a, z))]); ev(c("WB", HIO + a, HIO + z), o, -159.5)
+        x, f = ap("LN", 2 * t, slice(0, 384)), ap("LN", 2 * t + 1, slice(0, 384)); o = ps(7, 0, 384); fa, fb = ap("FA", 0, slice(0, 384)), ap("FA", 1, slice(0, 384))
+        relu(fa, x, -float(DELTA[t])); relu(fb, x, DELTA[t] - 63.0)
+        mm([(o, idm(-0.5), fa), (o, idm(-0.5), fb), (o, idm(-1.5), x)], stop=False); mm([(o, idm(2), f)], start=False)
+        relu(c("WP", 1536, 1920), o, -256 - 1.5 * DELTA[t])
+        tables(1536, 1920, x, f, 5); ev(c("WB", HIO + 1536, HIO + 1920), c("HH", 1536, 1920), -159.5, 2.0)
 
     def dividers(t):
         tag[0] = "l"
@@ -276,10 +305,12 @@ def build():
         tt(ap("DM"), ps(YB, 0, 16), c("VC", 8 * t, 8 * t + 16), A.min); ts(ap("DL2"), ap("DM"), 256.0 + C // 2, None, A.add)
         mm(across(ps(YB, 16, 32), "RW", "MK", 0) + across(ps(YB, 16, 32), "P16", "KD", 0)); ev(ap("VR"), ps(YB, 16, 32), 256.0, eng="v")
         ts(c("NXT", 256 * t, 256 * t + 256), c("IO1", 0, 256), c("CU", Kc - 1, Kc), None, A.is_gt)
-        gat(c("WB", LOO + C, LOO + C + 256), c("WB", HIO, HIO + 1536), ap("DL2"))
-        gat(ap("OLD"), ap("BL"), ap("DL2")); ts(ap("OLU"), ap("OLD"), float(RO), None, A.add)
-        gat(c("LIW", 0, 256), c("WP", 0, 1536), ap("DL2"), 204.0)
-        if t < 3: mm([(ps(YB, 0, 256), ONES, c("LIW", 0, 256))]); act(ap("LI"), ps(YB, 0, 256), F.Sign, -3247.5, acc=col(LIA))
+        gat(c("WB", LOO + C, LOO + C + 256), c("HH", 0, 1536), ap("DL2"), -159.5, mul=2.0)
+        gat(ap("OLD"), ap("BL"), ap("DL2")); ts(ap("OLU"), ap("OLD"), float(RO), None, A.add); ts(ap("O16"), ap("OLD"), -2047.0, None, A.add)
+        gat(c("LIW", 0, 256), c("WP", 0, 1536), ap("DL2"), 192.0, mul=2.0)
+        if t < 3:
+            mm([(ps(YB, 0, 256), ONES, c("LIW", 0, 256))]); act(ap("LI"), ps(YB, 0, 256), F.Sign, -3247.5, acc=col(LIA))
+            dma(ap("LC"), ap("LI", slice(0, 256), p=slice(0, 128, 16)), "y", 4096)
 
     def bridges(t):
         C = 512 + 256 * t; K = 192 + 16 * t; base = C
@@ -292,34 +323,43 @@ def build():
         part = [(128, K), (0, 128)]; span = [(128, K), (0, MW), (MW, 128)]
         def upto(a, z, n): return cut(a, z, -(-(z - a) // n))
         def slot(j):
-            pool = P[("abank", "bbank")[j]]; b = pool[reg[j] % len(pool)]; reg[j] += 1
+            pool = P[("abank", "bbank")[j]][int(tag[0][1])]; b = pool[reg[j] % len(pool)]; reg[j] += 1
             return 512 * b
-        def wide(o, n, terms): mm([(c("PS", o, o + n), idm(x), c(b, a, a + n)) for x, b, a in terms])
+        def wide(o, n, terms):
+            for u in range(0, n, 512): w = min(512, n - u); mm([(c("PS", o + u, o + u + w), idm(x), c(b, a + u, a + u + w)) for x, b, a in terms])
         def phase_a(s):
             tag[0] = "a%d" % s
             k0, k1 = part[s]; Ks = k1 - k0
-            for (a, z) in upto(k0, min(k1, 192), P["gp"]) + ([(192, k1 - 16)] if k1 > 208 else []) + ([(k1 - 16, k1)] if k1 > 192 else []):
+            chain = P["chain"][s] == 1; both = P["chain"][s] == 2; WZ = "UH" if both else "WZ"
+            old, new, newest = upto(k0, min(k1, 192), P["gp"][s]), ([(192, k1 - 16)] if k1 > 208 else []), ([(k1 - 16, k1)] if k1 > 192 else [])
+            for (a, z) in (old + new + newest, new + newest + old, new + old + newest)[P["newfirst"]]:
                 a16, z16 = 16 * a, 16 * z; n = 1536 if a >= 192 else 1920
                 gtt(c("UH", a16, z16), c("HH", 0, 1536), ap(EU, 0, slice(a, z)), c("WB", ysrc + a16, ysrc + z16), A.subtract)
-                gat(c("WA", a16, z16), c("WP", 0, 1536), ap(EU, 0, slice(a, z)), eng="v")
+                gat(c("WA", a16, z16), c("WP", 0, 1536), ap(EU, 0, slice(a, z)), -12.0, "v", 2.0)
                 gtt(c("HZ", a16, z16), c("HH", 0, n), ap(EU, 1, slice(a, z)), c("UH", a16, z16), A.add)
-                gat(c("WZ", a16, z16), c("WP", 0, n), ap(EU, 1, slice(a, z)), eng="v")
+                if both: gat(c("UH", a16, z16), c("WP", 0, n), ap(EU, 1, slice(a, z)), -12.0, "v", 2.0)
+                elif chain:
+                    gtt(c("WZ", a16, z16), c("WP", 0, n), ap(EU, 1, slice(a, z)), c("HZ", a16, z16), A.subtract)
+                    act(c("AB", 3840 * 2 + a16, 3840 * 2 + z16), c("WZ", a16, z16), F.Abs, -128.0, 2.0)
+                else: gat(c("WZ", a16, z16), c("WP", 0, n), ap(EU, 1, slice(a, z)), -12.0, mul=2.0)
                 if P["relu"][s]: ts(c("AB", 3840 * 3 + a16, 3840 * 3 + z16), c("HZ", a16, z16), -64.0, None, A.max)
                 else: act(c("AB", 3840 * 3 + a16, 3840 * 3 + z16), c("HZ", a16, z16), F.Abs, 128.0, 2.0)
-                for (x, y) in upto(a, z, P["aw"]):
-                    a16, z16 = 16 * x, 16 * y; n = z16 - a16; hz, wz, wa = (2, "HZ", a16), (-1, "WZ", a16), (-1, "WA", a16)
-                    for j, terms in ((1, [hz, wa]), (2, [hz, wz]), (0, [hz, wa, wz])):
+                for (x, y) in upto(a, z, P["aw"][s]):
+                    a16, z16 = 16 * x, 16 * y; n = z16 - a16; hz, wz, wa = (2, "HZ", a16), (-1, WZ, a16), (-1, "WA", a16)
+                    for j, terms in ((1, [hz, wa]), (0, [(-2, "WZ", a16), wa])) if chain else ((1, [hz, wa]), (2, [hz, wz]), (0, [hz, wa, wz])):
                         o = slot(0); wide(o, n, terms); act(c("AB", 3840 * j + a16, 3840 * j + z16), c("PS", o, o + n), F.Abs, 140.0 - 12 * len(terms))
             XB = P["xb"][s]
-            for h in (0, 1): mm([(pt(XB, 128 * h + r, 128 * h + 128, Ks, 16), c(("WA", "WZ")[h], 16 * k0 + r, 16 * k1, 16), s8("PKW")) for r in range(16)], each=True)
+            ne = 2 if both else 1
+            mm([(pt(XB, 0, 128 + 128 * ne, Ks), c(LV, k0, k1), c("C3", 0, 128 + 128 * ne))], stop=False)
+            for b, u, w in [("WA", 0, c("W16", 0, 16))] + ([("HZ", 128, c("W16", 24, 32)), ("WZ", 128, c("W16", 24, 32))] if chain else [(WZ, 128, c("W16", 8, 8 + 8 * ne))]):
+                mm([(pt(XB, u + r, u + 16 * w[3], Ks, 16), c(b, 16 * k0 + r, 16 * k1, 16), w) for r in range(16)], False, b == WZ)
             tag[0] = "f%d" % s
-            tn = lambda b, j, n=1: ap(b, s, slice(128 * j, 128 * (j + n)), p=slice(0, Ks)); dec = ps(XB, 0, 2 * Ks)
-            ts(tn("FL", 0, 2), pt(XB, 0, 256, Ks), 1.0 / 256, FO - t + 8.5 / 256, A.mult, A.add)
-            o = pt(XB, 256, 384, Ks)
-            mm([(o, c(LV, k0, k1), idm(512))] + [(o, top(idm(1), Ks), tn("FL", h)) for h in range(2)])
-            act(tn("TT", 0), o, F.Sign, -(2.0 * (FO - t - 204) + 42.5 + 512))
-            ev(tn("FF", 0, 2), pt(XB, 0, 256, Ks), -120.0)
-            mm([(dec, idm(-256), e3("FC", k0, k1))] + [(ps(XB, Ks * h, Ks * h + Ks), tn(b, h), top(m, Ks)) for h in range(2) for b, m in (("FL", idm(-256)), ("FF", fmat("I", 1.0)))], stop=False)
+            tn = lambda b, j, n=1: ap(b, s, slice(128 * j, 128 * (j + n)), p=slice(0, Ks))
+            act(tn("TT", 0), pt(XB, 128, 256, Ks), F.Sign, -23.0 if chain else -11.0)
+            for h in range(ne): ts(tn("FL", h), pt(XB, 256 * h, 256 * h + 128, Ks), 1.0 / 256, FO - t + 8.5 / 256, A.mult, A.add)
+            for h in range(ne): ev(tn("FF", h), pt(XB, 256 * h, 256 * h + 128, Ks), 256.0 * (FO - 13) - 120)
+            mm(([(ps(XB, 0, 2 * Ks), idm(-4096), e3("FK", k0, k1))] if both else [])
+               + [(ps(XB, Ks * h, Ks * h + Ks), tn(b, h), top(m, Ks)) for h in range(ne) for b, m in (("FF", fmat("I", 1.0)), ("FL", idm(-256)))], stop=False)
             mm([(pt(YB, 0, 384, Ks), c(LV, k0, k1), ap("I3"))] + [(pt(YB, 128 * j, 128 * j + 128, Ks), ap("ETA", j, slice(k0, k1)), idm(1)) for j in range(3)], stop=False)
             turned = lambda j, b, a, m: [(pt(YB, 128 * j + r, 128 * j + 128, Ks, 16), c(b, a + 16 * k0 + r, a + 16 * k1, 16), s8(m)) for r in range(16)]
             if P["relu"][s]: mm([(pt(YB, 256, 384, Ks), c("ONE", 0, Ks), mat("O", 128.0))] + turned(2, "AB", 3840 * 3, "S4") + turned(2, "HZ", 0, "SN"), False, False)
@@ -328,7 +368,7 @@ def build():
             mm([(pt(YB, r, 384, Ks, 16), c("AB", 16 * k0 + r, 16 * k1, 16), ap("S24")) for r in range(16)], start=False)
         def decide(s):
             tag[0] = "d%d" % s
-            k0, k1 = part[s]; Ks = k1 - k0; XB = P["xb"][s]; dec = ps(XB, 0, 2 * Ks)
+            k0, k1 = part[s]; Ks = k1 - k0; XB = P["xb"][s]; dec = ps(XB, 0, Ks)
             tn = lambda b, j, n=1: ap(b, s, slice(128 * j, 128 * (j + n)), p=slice(0, Ks))
             S_ = lambda j: ap("SS", j - 1, slice(0, 128), p=slice(0, Ks)); T_ = lambda j: pt(YB, 128 * j - 128, 128 * j, Ks); Q_ = lambda j: tn("EQ", j - 1); P_ = lambda j: ps(YB, Ks * j, Ks * j + Ks)
             ts(S_(1), T_(1), -1024.0, None, A.min)
@@ -342,16 +382,31 @@ def build():
             ts(ap("IX", 1, slice(k0, k1)), P_(1), cs, float(CST if t % 2 == 0 else CST2 - LOO), A.add, mo)
             tt(c("IA", 0, Ks), P_(0), c("ALT", 256 * (t % 2) + k0, 256 * (t % 2) + k1), mo); ts(ap("IX", 0, slice(k0, k1)), c("IA", 0, Ks), cs, None, A.add)
             ev(c("EC", k0, k1), P_(2))
-            mm([(ps(XB, Ks * h, Ks * h + Ks), Q_(j), top(idm(2048), Ks)) for h in range(2) for j in pole[h]], start=False)
-            relu(e3("TR", k0, k1), dec, 1.0 - base)
-            tt(e3(En, k0, k1), dec, e3(E, k0, k1), A.max)
-            if t < 3: cp(e3(EUn, k0, k1), e3(En, k0, k1))
+            ne = 2 if P["chain"][s] == 2 else 1
+            mm([(ps(XB, Ks * h, Ks * h + Ks), Q_(j), top(idm(4096), Ks)) for h in range(ne) for j in pole[h]], start=False)
+            moved(slice(0, ne), ps(XB, 0, ne * Ks), k0, k1)
+        def moved(h, dec, k0, k1):
+            x = lambda b: ap(b, h, slice(k0, k1))
+            relu(x("TR"), dec, 1.0 - base); tt(x(En), dec, x(E), A.max)
+            if t < 3: cp(x(EUn), x(En))
+        def second(s, spans):
+            for u in spans:
+                tag[0] = "b%d" % u
+                for (a, z) in upto(span[u][0], span[u][1], P["zw"][u]): gat(c("D", 16 * a, 16 * z), win, ap("IX", 1, slice(a, z)))
+            tag[0] = "e%d" % s
+            if P["chain"][s] == 2: return
+            k0, k1 = part[s]; Ks = k1 - k0; XB = P["xb"][s]; dec = ps(XB, 0, Ks)
+            tn = lambda b, j, n=1: ap(b, s, slice(128 * j, 128 * (j + n)), p=slice(0, Ks))
+            mm([(pt(XB, r, 512, Ks, 16), c("D", 16 * k0 + r, 16 * k1, 16), ap("Z32")) for r in range(16)], each=True)
+            ts(tn("FL", 1, 3), pt(XB, 0, 384, Ks), 1300.0625, None, A.add); ev(tn("FF", 1), pt(XB, 384, 512, Ks), 584.0 * 1300 + 292 + base - 4096)
+            mm([(dec, tn("FF", 1), top(fmat("I", 1.0), Ks)), (dec, idm(-4096), ap("FK", 1, slice(k0, k1)))] + [(dec, tn("EQ", j), top(idm(4096), Ks)) for j in (0, 2)]
+               + [(dec, tn("FL", 1 + m), top(idm(-8.0 ** (m + 1)), Ks)) for m in range(3)])
+            moved(1, dec, k0, k1)
         def phase_b(s):
             tag[0] = "b%d" % s
             k0, k1 = span[s]; how = P["bmode"][s]
             for (a, z) in upto(k0, k1, P["bw"][s]):
                 a16, z16 = 16 * a, 16 * z; n = z16 - a16; D = lambda j: c("D", 3840 * j + a16, 3840 * j + z16); d_ = lambda w, j: (w, "D", 3840 * j + a16)
-                gat(D(0), win, ap("IX", 1, slice(a, z)))
                 if how == 2:
                     gat(D(1), win, ap("IX", 0, slice(a, z)))
                     o = slot(1); wide(o, n, [d_(1, 0), d_(-1, 1)]); act(D(2), c("PS", o, o + n), F.Abs)
@@ -363,6 +418,7 @@ def build():
                 ev(ydst(a16, z16), c("PS", o, o + n), 95.75)
         y_ = ydst(0, 16); yb, y0 = y_[0], y_[2][0].start
         def alive(s):
+            tag[0] = "b%d" % s
             k0, k1 = span[s]; Ks = k1 - k0; o = slot(1); o = c("PS", o, o + Ks)
             mm(compact(o, "S", yb, y0 + 16 * k0, Ks))
             act(c(LVn, k0, k1), o, F.Sign, -3247.5, acc=col(LA + s) if t < 3 else None)
@@ -376,7 +432,7 @@ def build():
         def cells_on():
             tag[0] = "c"
             Cn = C + 256
-            if t == 3: return dma(ap("yx", slice(0, 1536), p=slice(0, 128)), c("WB", LOO, LOO + 1536), "y")
+            if t == 3: ev(ap("XT"), c("WB", LOO, LOO + 1536), 31.5); return dma(ap("yx", slice(0, 1536), p=slice(0, 128)), ap("XT"), "y")
             for a in range(0, Cn, 512):
                 z = min(Cn, a + 512); bk = a // 512; o = ps(bk, 0, z - a); lst = [(o, idm(1), c("WB", LOO + a, LOO + z))]
                 if a >= 512: lst.append((o, idm(-128), c("NXT", a - 512, z - 512)))
@@ -388,74 +444,84 @@ def build():
                 z = min(Cn, a + 1024); ts(c("XT", a, z), c("PS", a, z), 0.0, 63.0, A.max, A.min)
         def to_rows(fs, which):
             for f in fs: to_row(f, (lambda a, z: ap("TR", 0, slice(a, z)), lambda a, z: ap("TR", 1, slice(a, z)), lambda a, z: c("EC", a, z), lambda a, z: c(LVn, a, z))[f], which)
-        phase_a(0); decide(0); to_rows((0, 1, 2), runs[2:3 + t]); phase_a(1); phase_b(0); alive(0); to_rows((3,), runs[2:3 + t]); decide(1); to_rows((0, 1, 2), runs[:2])
+        phase_a(0); decide(0); to_rows((0, 2), runs[2:3 + t]); phase_a(1); second(0, [0]); to_rows((1,), runs[2:3 + t]); phase_b(0); alive(0); to_rows((3,), runs[2:3 + t])
+        decide(1); to_rows((0, 1, 2) if P["chain"][1] == 2 else (0, 2), runs[:2])
         cells_on()
         if t < 3: cells_ahead(t + 1)
-        phase_b(1); alive(1); to_rows((3,), runs[1:2])
         tag[0] = "t"
+        if t < 3:
+            gat(ap("GT"), ap("R"), ap("TW"))
+            o = ps(YB, 0, 24); mm(compact(o, "P0", "GT", 0, 24))
+            ts(ap("TA"), o, 0.5, base - 1.0, A.is_gt, A.mult); tt(ap("TB"), o, ap("TA"), A.add); tt(ap("OWN"), ap("TB"), ap("OWN"), A.max); cp(ap("OWU"), ap("OWN"))
+            twins_ahead(t + 1)
+        second(1, [1, 2])
+        if P["chain"][1] != 2: to_rows((1,), runs[:2])
         if t == 3:
             ef = lambda h: ap("EF", h, slice(0, 192))
             tt(c("T2", 0, 192), ef(0), ap("NSW"), A.add); tt(ef(1), ef(1), c("T2", 0, 192), A.min); tt(ef(0), ef(0), ap("SWF"), A.max)
             for h in range(2):
                 for a, z, k0, k1 in runs[:6]: dma(ap("ye", slice(a, z), p=slice(h, 16, 2)), ap(En, h, slice(k0, k1)), "y")
-        phase_b(2)
+        phase_b(1); alive(1); to_rows((3,), runs[1:2]); phase_b(2)
         if t < 3 or not P["direct"]: alive(2)
         if P["direct"]: live_row()
         if not P["direct"]: to_rows((3,), runs[:1])
-        if t < 3:
-            count_ahead(t + 1)
-            tag[0] = "t"
-            gat(ap("GT"), ap("R"), ap("TW"))
-            o = ps(YB, 0, 24); mm(compact(o, "PKT", "GT", 0, 24))
-            ts(ap("TA"), o, 0.5, base - 1.0, A.is_gt, A.mult); tt(ap("TB"), o, ap("TA"), A.add); tt(ap("OWN"), ap("TB"), ap("OWN"), A.max); cp(ap("OWU"), ap("OWN"))
-            twins_ahead(t + 1)
+        if t < 3: count_ahead(t + 1)
         else:
             for a, z, k0, k1 in (runs[2], runs[1], runs[0]):
-                for r in range(16): ev(c("Y0N", a + (k1 - k0) * r, a + (k1 - k0) * (r + 1)), c("YF", 16 * k0 + r, 16 * k1, 16), -192.0)
+                w = k1 - k0; per = min(16, 1 << ((512 // w).bit_length() - 1))
+                for r0 in range(0, 16, per):
+                    bk = (7, YB)[r0 // per % 2]
+                    mm([(ps(bk, w * r, w * r + w), idm(1), c("YF", 16 * k0 + r0 + r, 16 * k1, 16)) for r in range(per)], each=True); ev(c("Y0N", a + w * r0, a + w * (r0 + per)), ps(bk, 0, w * per), -192.0)
                 dma(ap("yy", slice(a, z), p=slice(0, 128)), c("Y0N", a, z), "y")
             gat(c("FR", 0, 768), c("YF", 3072, 3840), c("ULAST", 0, 48), -192.0)
             dma(ap("yy", slice(3072, 3840), p=slice(0, 128)), c("FR", 0, 768), "y")
 
     def slots(t):
         tag[0] = "s"
-        mm([(ps(2, 0, 512), idm(-1), ap("ONE")), (hp(2, 0), idm(2048), c("NXT", 256 * t, 256 * t + 256))] + ([(hp(2, h), idm(1), ap("LI")) for h in range(2)] if t < 3 else []), stop=False)
-        for j in range(4):
-            gat(c("D", 1024 * j, 1024 * j + 1024), ap("R"), c("OLU", 64 * j, 64 * j + 64))
-            o = ps((0, 0, 1, 5)[j], 64 * (j == 1), 64 * (j == 1) + 64)
-            mm([(o, idm(-1), c("IO1", 64 * j, 64 * j + 64))] + compact(o, "PKR", "D", 1024 * j, 64))
-        for bk, a, z in ((0, 0, 128), (1, 128, 192), (5, 192, 256)):
+        for bk, a, z in ((2, 0, 192), (6, 192, 256)):
+            n = z - a; cn = lambda h: ps(bk, n * h, n * h + n)
+            mm([(ps(bk, 0, 2 * n), idm(-1), c("ONE", 0, 2 * n)), (cn(0), mat("O", 128.0), c("NXT", 256 * t + a, 256 * t + z))] + ([(cn(h), idm(1), c("LI", a, z)) for h in range(2)] if t < 3 else []), stop=False)
+        for bk, a, z in ((0, 0, 96), (1, 96, 192), (5, 192, 256)):
+            for u, w in ((a, (a + z) // 2), ((a + z) // 2, z)):
+                gat(c("D", 16 * u, 16 * w), ap("R"), c("OLU", u, w))
+                if t < 3 and P["lvfirst"]: ops[-1]["rd"].append(col(LA + 2))
             o = ps(bk, 0, z - a)
+            mm([(o, idm(-1), c("IO1", a, z))] + compact(o, "PKR", "D", 16 * a, z - a))
             ts(sm(0, a, z), o, 0.0, None, A.is_gt); ts(sm(1, a, z), o, 2048.0, None, A.is_equal); ts(sm(2, a, z), o, 2560.0, None, A.is_ge)
-            mm(kept(2, "O", 128.0, a, z), False, z == 256)
-        if t < 3: act(ap("T2"), ps(2, 0, 512), F.Relu, -2047.0, acc=col(LOST))
+            mm(kept(2, "O", 128.0, a, z, 192) if a < 192 else kept(6, "O", 128.0, a, z, 64, 192), False, z >= 192)
+            if t < 3 and z == 192: act(c("T2", 0, 384), ps(2, 0, 384), F.Relu, -2047.0, acc=col(LOST + 23))
+        if t < 3: act(c("T2", 384, 512), ps(6, 0, 128), F.Relu, -2047.0, acc=col(LOST))
 
     def books(t):
         tag[0] = "k"
         C = 512 + 256 * t; K = 192 + 16 * t
         E, En, EU, EUn, LV, LVn, ydst = names(t)
-        relu(ap("NM"), ps(2, 0, 512), -1920.0)
-        mm([(ps(2, 0, 32), sh("P0", r), e3("NM", 16 * r, 16 * r + 16)) for r in range(16)]); ev(ap("NC"), ps(2, 0, 32))
+        relu(e3("NM", 0, 192), ps(2, 0, 384), -1920.0)
+        if t == 3: relu(e3("NM", 192, 256), ps(6, 0, 128), -1920.0)
+        if P["ncdma"] and t < 3:
+            for h in range(2): dma(c("NC", 16 * h, 16 * h + 16), ap("NM", h, slice(0, 256), p=slice(0, 128, 16)), "y", 4096)
+        else: mm([(ps(2, 0, 32), sh("P0", r), e3("NM", 16 * r, 16 * r + 16)) for r in range(16)]); ev(ap("NC"), ps(2, 0, 32))
         q = lambda j: ps(2, 32 + 16 * j, 48 + 16 * j); nc = [c("NC", 0, 16), c("NC", 16, 32)]
-        for j, (x, w) in enumerate(((ap("VR"), -16), (c("NR", 16 * t, 16 * t + 16), -16), (c("NR", 0, 16), 16))): mm([(q(j), idm(1), x)] + [(q(j), idm(w), y) for y in nc])
-        if t < 3: mm(across(q(3), "P0", "LI", 0) + [(q(3), idm(-1), y) for y in nc])
-        ts(ap("DLM"), q(2), -512.0, 256.0, A.add, A.min)
-        gat(ydst(16 * K, 16 * K + 256), ap("LIW"), ap("DLM"))
+        for j, (x, w) in enumerate(((ap("VR"), -128), (c("NR", 16 * t, 16 * t + 16), -128), (c("NR", 0, 16), 16))[:3 if t < 3 else 2]): mm([(q(j), idm(1), x)] + [(q(j), idm(w), y) for y in nc])
+        if t < 3:
+            mm([(q(3), idm(1), ap("LC"))] + [(q(3), idm(-1), y) for y in nc])
+            ts(ap("DLM"), q(2), -512.0, 256.0, A.add, A.min)
+            gat(ydst(16 * K, 16 * K + 256), ap("LIW"), ap("DLM"))
         ts(e3(En, K, K + 16), ps(2, 32, 64), 0.0, None, A.max)
         if t < 3: ts(e3(EUn, K, K + 16), ps(2, 32, 64), 0.0, None, A.max); act(c(LVn, K, K + 16), q(3), F.Sign)
         else:
-            gat(c("FR", 768, 1024), c("YF", 3072, 4096), c("ULAST", 48, 64), -192.0)
+            o = ps(0, 0, 256); mm([(o, idm(1), c("LIW", 0, 256))] + [(o, idm(-1), nm(j)) for j in range(2)]); relu(c("FR", 768, 1024), o, -192.0)
             dma(ap("yy", slice(3840, 4096), p=slice(0, 128)), c("FR", 768, 1024), "s")
             for h in range(2): dma(ap("ye", slice(3840, 4096), p=slice(h, 16, 2)), ap(En, h, slice(240, 256)), "ys"[h])
-        mm([(ps(XB, 0, 512), idm(-16384), ap("ONE"))] + [(hp(XB, h), fmat("I", 1.0), ap("OLD")) for h in range(2)], stop=False)
-        mm(kept(XB, "I", 16384.0), start=False)
-        mm([(ps(YB, 0, 512), idm(1), ap("IO1"))] + kept(YB, "F", 16384.0), stop=False)
-        mm([(hp(YB, h), idm(-128), nm(j)) for h in range(2) for j in range(2)], start=False)
-        for h, o in enumerate((ap("TVF"), c("BL", C, C + 256))):
-            t2 = c("T2", 256 * h, 256 * h + 256)
-            ts(t2, hp(YB, h), c("BC", t, t + 1), -1.0, A.add, A.max)
-            tt(o, hp(XB, h), t2, A.max)
-            if h == 0: sca(ap("BL"), ap("DL2"), ap("TVF"))
-        if t == 3: dma(ap("yl", slice(0, 1536), p=slice(0, 128)), ap("BL"), "y")
+        mm([(ps(XB, 0, 512), idm(-1.5), ap("K2"))] + [(hp(XB, h), idm(1), ap("O16")) for h in range(2)], stop=False)
+        mm([(ps(YB, 0, 512), idm(1), ap("IO1"))], stop=False)
+        for a, z in ((0, 96), (96, 192), (192, 256)): mm(kept(XB, "I", 4096.0, a, z), False, z == 256); mm(kept(YB, "F", 16384.0, a, z), False, False)
+        for h in range(2): mm([(hp(YB, h), idm(-128), nm(j)) for j in range(2)], False, h == 1)
+        t2 = lambda h: c("T2", 256 * h, 256 * h + 256)
+        for h in range(2): ts(t2(h), hp(YB, h), c("BC", t, t + 1), -1.0, A.add, A.max)
+        tt(ap("TVF"), hp(XB, 0), t2(0), A.max); tt(c("BL", C, C + 256), hp(XB, 1), t2(1), A.max); sca(ap("BL"), ap("DL2"), ap("TVF"))
+        if t == 3:
+            for j in range(2): dma(ap("yl", slice(768 * j, 768 * j + 768), p=slice(0, 128)), c("BL", 768 * j, 768 * j + 768), "ys"[j])
 
     who(0)
     for t in range(4):
@@ -474,7 +540,7 @@ def depend(ops):
             for m, pm, cm, mw in seen.get(x[0], []):
                 if (w or mw or x[0] == "PS") and m != n and pm & x[4] and cm & x[5]:
                     hard = (mw and not w) or ((w or mw) and not P["war"]) or ops[m]["kind"] != "c" or o["kind"] != "c"
-                    if "p" in o["alts"] and "p" in ops[m]["alts"]: hard = False
+                    if ("p" in o["alts"] and "p" in ops[m]["alts"]) or ("row" in o and "row" in ops[m]): hard = False
                     deps[m] = deps.get(m, False) or hard
         for x, w in acc:
             lst = seen.setdefault(x[0], [])
@@ -484,19 +550,28 @@ def depend(ops):
         o["deps"] = deps
 
 
-def settle(ops, rounds=8):
+def settle(ops, others):
     lat, far, bias = P["lat"], P["far"], P["bias"]
     n = len(ops); kids = [{} for o in ops]
     for i, o in enumerate(ops):
         for d, hard in o["deps"].items(): kids[d][i] = hard
     tail = [far if o["kind"] == "arrive" else o["x"] if o["kind"] == "dma" else 0.0 for o in ops]
-    def lay(key, back, due=None):
+    def after(z, t):
+        a, b = 0, len(z)
+        while a < b:
+            m = (a + b) // 2
+            if z[m] > t: b = m
+            else: a = m + 1
+        return a
+    def lay(key, back, due=None, fixed=None):
         lines = {e: ([], []) for e in "vspqy"}; st = [0.0] * n; en = [0.0] * n; eng = [None] * n
         for i in sorted(range(n), key=key):
             o = ops[i]; near = kids[i] if back else o["deps"]; best = None
             for e, v in o["alts"].items():
-                t0 = max([en[d] + (lat if hard or eng[d] != e else 0.0) for d, hard in near.items()] + [0.0]) + (tail[i] if back else 0.0)
-                a, z = lines[e]; j = int(np.searchsorted(z, t0, side="right")) if z else 0; x = t0
+                if fixed and e != fixed[i]: continue
+                if back: t0 = max([en[d] + (lat + tail[i] if hard or eng[d] != e else 0.0) for d, hard in near.items()] + [tail[i]])
+                else: t0 = max([en[d] + lat if hard or eng[d] != e else en[d] - tail[d] for d, hard in near.items()] + [0.0])
+                a, z = lines[e]; j = after(z, t0); x = t0
                 while j < len(a) and a[j] < x + v[1]: x = max(x, z[j]); j += 1
                 if due is None: sc = x + v[1] * (bias if e == "v" else 1.0)
                 else: sc = max(x + v[1], due[i] - P["slack"]) + {"v": P["tilt"] * v[1], "q": 1e-3 * v[1]}.get(e, 0.0)
@@ -510,16 +585,48 @@ def settle(ops, rounds=8):
     for i in range(n - 1, -1, -1):
         pr[i] = min([v[1] for v in ops[i]["alts"].values()] + [0.0] * (not ops[i]["alts"])) + tail[i] + lat + max([pr[k] for k in kids[i]] + [0.0])
     st, en, eng = lay(lambda i: (-pr[i], i), False); top = (max(en), st, en, eng)
-    rng = np.random.default_rng(1)
     for k in range(P["rounds"]):
         on = P["due"] and k >= 2
-        if k >= 4 and P["shake"] and max(en) > top[0] + P["temp"]: st, en = top[1:3]
         sb, eb, x = lay(lambda i: (-en[i], -i), True, [max(en) - a for a in st] if on else None)
-        if k >= 4 and P["shake"]:
-            nz = rng.random(n) * P["shake"]
-            for i in range(n - 1, -1, -1): eb[i] = max([eb[i] + float(nz[i])] + [eb[j] for j in kids[i]])
-        st, en, eng = lay(lambda i: (-eb[i], i), False, [max(eb) - a + b for a, b in zip(sb, tail)] if on else None)
-        if max(en) < top[0]: top = (max(en), st, en, eng)
+        due = [max(eb) - a + b for a, b in zip(sb, tail)] if on else None
+        st, en, eng = lay(lambda i: (-eb[i], i), False, due)
+        if max(en) < top[0]: top = (max(en), st, en, eng, eb, due)
+    marks = [i for i in range(n) if ops[i]["wr"] and ops[i]["wr"][0][0] == "UBT"]
+    rng = np.random.default_rng(1)
+    def spans(st, eng):
+        order = sorted(range(n), key=lambda i: (st[i], i)); tot = 0.0
+        for alt, wake in others:
+            z = [0.0] * n; a = [0.0] * n; line = {e: 0.0 for e in "vspqy"}
+            for i in order:
+                e = eng[i]; o = alt[i]; t0 = line[e] if e else 0.0
+                for d, hard in ops[i]["deps"].items():
+                    if (hard or eng[d] != e) and z[d] + wake > t0: t0 = z[d] + wake
+                a[i] = t0
+                if e: t0 += o[0][e][1]; line[e] = t0
+                z[i] = t0 + o[1]
+            tot = tot + np.diff([0.0] + [a[i] for i in marks] + [max(z)])
+        return tot
+    free = [i for i in range(n) if "v" in ops[i]["alts"] and "s" in ops[i]["alts"]]
+    def again(eb, eng):
+        pr = list(eb)
+        for i in range(n - 1, -1, -1): pr[i] = max([pr[i]] + [pr[j] for j in kids[i]])
+        st, en, x = lay(lambda i: (-pr[i], i), False, None, eng); return st, en, spans(st, eng)
+    name = [o["tag"] + (o["wr"][0][0] if o["wr"] else "") for o in ops]; tags = sorted(set(name)); kind = np.array([tags.index(x) for x in name])
+    eb = np.array(top[4]); eng = list(top[3]); st, en = top[1:3]; best = spans(st, eng)
+    for k in range(P["tries"]):
+        seg = np.searchsorted([st[i] for i in marks], st, side="right"); new = list(eng); eb2 = eb
+        if k % P["every"] == P["every"] - 1: eb2 = lay(lambda i: (-en[i], -i), True, None, eng)[1]; eb2 = np.array(eb2) + (max(eb) - max(eb2))
+        elif k % 3 == 1: eb2 = eb + P["nz"] * (rng.random(n) - 0.5) * (rng.random(n) < 0.2)
+        elif k % 3 == 2: eb2 = eb + (500.0 * rng.integers(-2, 3, len(tags)) * (rng.random(len(tags)) < 0.2))[kind]
+        else:
+            for i in free:
+                if rng.random() < P["part"]: new[i] = "s" if eng[i] == "v" else "v"
+        st2, en2, now = again(eb2, new); good = now < best - 1.0
+        if good.any():
+            new = [new[i] if good[seg[i]] else eng[i] for i in range(n)]; eb2 = np.where(good[seg], eb2, eb)
+            if not good.all(): st2, en2, now = again(eb2, new)
+            if now.sum() < best.sum(): st, en, eng, eb, best = st2, en2, new, eb2, now
+    top = (max(en), st, en, eng)
     busy = {e: 0.0 for e in "vspqy"}
     for o, s, z, e in zip(ops, top[1], top[2], top[3]):
         o["st"] = s; o["end"] = z; o["e"] = e
@@ -528,7 +635,10 @@ def settle(ops, rounds=8):
 
 
 def plan():
-    ops = build(); depend(ops); order, busy = settle(ops)
+    keep = dict(P); others = []
+    for guess in GUESSES:
+        P.update(guess); others.append(([(o["alts"], P["far"] if o["kind"] == "arrive" else o["x"] if o["kind"] == "dma" else 0.0) for o in build()], P["lat"])); P.update(keep)
+    ops = build(); depend(ops); order, busy = settle(ops, others)
     count = {}; known = {e: {} for e in "vspqy"}; nd = 0; steps = []
     for i in order:
         o = ops[i]; e = o["e"]; kn = known[e]; need = {}
@@ -550,7 +660,7 @@ def plan():
         steps.append((o, [(s, v[0]) for s, v in need.items()]))
     last = dict(count)
     for j in range(nd): last["d%d" % j] = 16
-    for t in range(4): last["ls%d" % t] = 12; last["ar%d" % t] = 12
+    for t in range(8): last["ls%d" % t] = 12; last["ar%d" % t] = 12
     seen = {}
     for kn in known.values():
         for s, v in kn.items(): seen[s] = max(seen.get(s, 0), v)
@@ -581,7 +691,7 @@ def rank_program(g, core, T, topo):
                 en = topo.engines(core, peer); en = [e for e in en[0::2] + en[1::2] if e not in used][:4]; used += en
                 rid, pid = topo.addr(peer)[:2]
                 tr.append(RemoteDMATransfer(dst_ids=[DstId(rid=rid, pnc=pid)], dma_engine_mask=sum(1 << e for e in en), remote_sem=T.sem["ar%d" % t],
-                                            src=T["SN%d" % (t % 2)][:, d - 1], dst=T["LN%d" % t][:, 3 - d]))
+                                            src=T["SN"][:, t % 4, 128 * d - 128:128 * d], dst=T["LN"][:, t, 384 - 128 * d:512 - 128 * d]))
             g.remote_dma_fused(tr, local_sem=T.sem["ls%d" % t])
         else:
             o["alts"][o["e"]][0](g, r).then_inc(T.sem[o["sig"][0]], 16 if o["kind"] == "dma" else 1)

import numpy as np
from concourse.bass import DstId, RemoteDMATransfer
from concourse.mybir import dt, AluOpType, AxisListType, ActivationFunctionType

A = AluOpType
F = ActivationFunctionType
THETA, DELTA = (470, 540, 620, 560), (8, 6, 9, 7)
BF, HF, F32, I32, U16 = "bfloat16", "float16", "float32", "int32", "uint16"
CST, LOO, HIO, CST2, YBO, WBW = 3584, 3600, 5520, 7440, 7456, 11296
RO, RW_ = 192, 4032
FO = 1500
NMAT = 33
SB = {
    "Y0N": ([3072], BF), "WB": ([WBW], BF), "YF": ([4096], BF), "HH": ([1920], BF), "WP": ([1920], F32), "XT": ([1536], BF), "P2": ([1280], BF), "DT": ([4 * 272], BF),
    "UH": ([3840], HF), "WA": ([3840], HF), "WZ": ([3840], BF), "HZ": ([3840], BF), "AB": ([4 * 3840], BF), "D": ([3 * 3840], BF),
    "R": ([RW_], BF), "BL": ([1536], F32), "DR": ([1024], BF), "FR": ([1024], BF), "BTG": ([1280], BF), "NXT": ([1024], BF), "BC": ([4], F32), "IO1": ([512], BF),
    "EI": ([2, 192], I32), "BI": ([512], I32), "SI": ([24], I32), "NSW": ([192], F32), "SWF": ([192], F32), "EB": ([192], BF), "FK": ([2, 256], BF),
    "E0": ([2, 256], HF), "E1": ([2, 256], HF), "EF": ([2, 256], F32), "EU0": ([2, 256], U16), "EU1": ([2, 256], U16),
    "LV0": ([256], BF), "LV1": ([256], BF), "EQ": ([2, 384], BF), "EC": ([256], BF), "TR": ([2, 256], BF), "IX": ([2, 256], U16),
    "SS": ([3, 128], F32), "FL": ([2, 512], HF), "Z32": ([32], BF), "JI": ([16], I32), "BJ": ([2, 128], I32), "FF": ([2, 256], F32), "TT": ([2, 128], BF), "IA": ([128], F32), "I3": ([384], BF), "S24": ([24], BF),
    "JK": ([16, 80], BF), "SX": ([80], F32), "NSX": ([80], F32), "CA": ([80], BF), "CU": ([80], F32), "PL": ([96], F32), "UBT": ([80], U16),
    "COL": ([40], F32), "QB": ([2], BF), "CI": ([8], I32), "OH": ([16], F32), "ACC": ([16], F32), "KI": ([16], U16), "NB": ([16], F32), "KT": ([96], BF), "KD": ([256], BF), "MK": ([256], BF),
    "DM": ([16], F32), "DL2": ([16], U16), "VR": ([16], HF), "DLM": ([16], U16), "NC": ([32], BF), "S16": ([64], F32), "NR": ([64], HF), "ULAST": ([64], U16),
    "OLD": ([256], F32), "OLU": ([256], U16), "O16": ([256], HF), "LP": ([1280], BF), "K2": ([512], HF), "LIW": ([272], BF), "LI": ([256], BF), "SM": ([3, 256], BF), "NM": ([2, 256], BF), "T2": ([512], F32), "TVF": ([256], F32),
    "TW": ([24], U16), "TA": ([24], F32), "TB": ([24], F32), "OWN": ([24], F32), "OWU": ([24], U16), "GT": ([384], BF),
    "ONE": ([512], BF), "MAT": ([NMAT * 128], BF), "MF": ([4 * 128], F32), "SEL": ([8 * 144], BF), "ETA": ([3, 256], BF),
    "BT": ([272], BF), "VC": ([256], F32), "ALT": ([512], F32), "IO": ([16], F32), "IOM": ([256], F32), "ZE": ([80], F32),
    "SN": ([4, 384], BF), "LN": ([8, 384], BF), "FA": ([2, 384], BF), "C3": ([384], BF), "W16": ([32], BF), "LC": ([16], BF),
}
SCRATCH = {k: ("sbuf", [128] + v[0], v[1]) for k, v in SB.items()}
SCRATCH["PS"] = ("psum", [128, 4096], F32)
NDMA = 128
SEMAPHORES = ["v", "s", "p", "q"] + ["ar%d" % t for t in range(8)] + ["ls%d" % t for t in range(8)] + ["d%d" % i for i in range(NDMA)]
SELS = ("S", "PKW", "PKR", "P0", "P16", "RW", "S2", "SC")
P = {"g": 1.4, "s": 3.0, "ov": 20.0, "pe": 0.42, "nz": 300.0, "gp": [32, 32], "aw": [32, 32], "zw": [32, 32, 32], "abank": [[0, 1, 2, 6, 7], [0, 1]], "bbank": [[5, 6, 7], [5, 6, 7], [5, 6, 7]], "newfirst": 2, "xat": 10, "lf": [1, 1, 0, 0], "lvfirst": 0, "chain": [0, 1], "ncdma": 1, "bw": [16, 16, 16], "last": 32,
     "bmode": [1, 1, 1], "relu": [0, 0, 0], "lat": 240.0, "far": 3000.0, "dma": 1300.0, "bias": 2.0, "war": 0, "direct": 1, "xb": [3, 2], "rounds": 8, "tries": 1100, "part": 0.03, "every": 10, "due": 1, "slack": 800.0, "tilt": 0.1}
GUESSES = ({"ov": 45.0, "lat": 170.0, "g": 1.1}, {"ov": 15.0, "lat": 230.0, "g": 1.4, "pe": 0.47}, {"ov": 45.0, "lat": 200.0, "g": 1.8, "s": 5.0, "dma": 1600.0, "far": 3500.0})
CY, XB, YB = 0.83, 3, 4


def bits(idx):
    m = np.zeros(16384, np.uint8); m[idx] = 1
    return int.from_bytes(np.packbits(m, bitorder="little").tobytes(), "little")


def ap(buf, *idx, p=None):
    ps = slice(0, 128) if p is None else p
    if buf not in SCRATCH:
        return (buf, p, idx, 0, 0, 0)
    shape = SCRATCH[buf][1][1:]
    if not idx: idx = tuple(slice(0, n) for n in shape)
    cols = np.arange(int(np.prod(shape))).reshape(shape)[idx].reshape(-1)
    if buf == "PS": return (buf, ps, idx, len(cols), 1, bits(np.unique(cols // 512)))
    return (buf, ps, idx, len(cols), bits(np.arange(128)[ps]), bits(cols))


def c(buf, a, b, s=1): return ap(buf, slice(a, b, s) if s > 1 else slice(a, b))
def size(x): return {BF: 2, HF: 2, U16: 2, F32: 4, I32: 4}[SCRATCH[x[0]][2]]


def build():
    ops = []; tag = ["i"]

    def add(alts, rd, wr, kind="c", extra=None):
        ops.append({"alts": alts, "rd": [x for x in rd if isinstance(x, tuple) and x[0] in SCRATCH], "wr": [x for x in wr if x[0] in SCRATCH], "kind": kind, "x": extra, "tag": tag[0]})

    def vc(n, k): return P["ov"] + max(64, n * k) * CY
    def half(o, i): return 0.5 if size(o) == 2 and size(i) == 2 else 1.0
    def ts(o, i, s1, s2, op0, op1=None):
        if op1 is None: f = lambda g, r: g.vector.tensor_scalar(r(o), r(i), r(s1), None, op0)
        else: f = lambda g, r: g.vector.tensor_scalar(r(o), r(i), r(s1), r(s2), op0, op1)
        add({"v": (f, vc(o[3], half(o, i)))}, [i, s1, s2], [o])
    def tt(o, i0, i1, op):
        k = 1 if "PS" in (i0[0], i1[0]) else 2
        add({"v": (lambda g, r: g.vector.tensor_tensor(r(o), r(i0), r(i1), op), vc(o[3], k))}, [i0, i1], [o])
    def cp(o, i): add({"v": (lambda g, r: g.vector.tensor_copy(r(o), r(i)), vc(o[3], half(o, i)))}, [i], [o])
    def scan(o, i): z = c("ZE", 0, o[3]); add({"v": (lambda g, r: g.vector.tensor_tensor_scan(r(o), r(i), r(z), 0.0, A.add, A.add), vc(o[3], 1))}, [i, z], [o])
    def fill(o, v, eng="vq"):
        alts = {}
        if "v" in eng: alts["v"] = (lambda g, r: g.vector.memset(r(o), v), vc(o[3], size(o) / 4.0))
        if "q" in eng and v == int(v):
            alts["q"] = (lambda g, r: g.iota(r(o), [[0, o[3]]], int(v), 0, allow_small_or_imprecise_dtypes=True), 150 + 2 * CY * o[3])
        add(alts, [], [o])
    def act(o, i, fn, bias=0.0, scale=1.0, acc=None):
        add({"s": (lambda g, r: g.scalar.activation(r(o), r(i), fn, bias=r(bias), scale=scale, accum_out=None if acc is None else r(acc)), vc(o[3], 1) + (20 if acc else 0))},
            [i, bias], [o] + ([acc] if acc else []))
    def ev(o, i, add_=0.0, mul=1.0, eng="vs"):
        alts = {}
        if "v" in eng: alts["v"] = (lambda g, r: g.vector.tensor_scalar(r(o), r(i), mul, add_, A.mult, A.add), vc(o[3], half(o, i)))
        if "s" in eng: alts["s"] = (lambda g, r: g.scalar.activation(r(o), r(i), F.Identity, bias=add_, scale=mul), vc(o[3], 1))
        add(alts, [i], [o])
    def relu(o, i, bias):
        add({"v": (lambda g, r: g.vector.tensor_scalar(r(o), r(i), bias, 0.0, A.add, A.max), vc(o[3], half(o, i))),
             "s": (lambda g, r: g.scalar.activation(r(o), r(i), F.Relu, bias=bias), vc(o[3], 1))}, [i], [o])
    def gc_(n, e): return (50 if e == "v" else 65) + n * P["g"] * CY
    def total(o, i): add({"v": (lambda g, r: g.vector.tensor_reduce(r(o), r(i), AxisListType.X, A.add), vc(i[3], 1))}, [i], [o])
    def gat(o, w, off, add_=0.0, eng="vs", mul=1.0):
        alts = {}
        if "v" in eng:
            if add_: alts["v"] = (lambda g, r: g.vector.tensor_scalar(r(o), r(w).indirect(r(off)), mul, add_, A.mult, A.add), gc_(o[3], "v"))
            else: alts["v"] = (lambda g, r: g.vector.tensor_copy(r(o), r(w).indirect(r(off))), gc_(o[3], "v"))
        if "s" in eng: alts["s"] = (lambda g, r: g.scalar.activation(r(o), r(w).indirect(r(off)), F.Identity, bias=add_, scale=mul), gc_(o[3], "s"))
        add(alts, [w, off], [o])
    def gtt(o, w, off, i1, op):
        add({"v": (lambda g, r: g.vector.tensor_tensor(r(o), r(w).indirect(r(off)), r(i1), op), gc_(o[3], "v"))}, [w, off, i1], [o])
    def sca(w, off, i):
        add({"v": (lambda g, r: g.vector.tensor_copy(r(w).indirect(r(off)), r(i)), 50 + i[3] * P["s"] * CY)}, [off, i, w], [w])
    def mm(lst, start=True, stop=True, each=False):
        def f(g, r):
            for j, (o, l, x) in enumerate(lst): ins = g.tensor.matmul(r(o), r(l), r(x), each or (start and j == 0), each or (stop and j == len(lst) - 1))
            return ins
        add({"p": (f, sum(max(min(64, l[3]), x[3]) * P["pe"] * (4 if size(x) == 4 else 1) for o, l, x in lst))}, [y for o, l, x in lst for y in (l, x)], [o for o, l, x in lst])
    def pt(bank, a, b, n, s=1): return ap("PS", slice(512 * bank + a, 512 * bank + b, s), p=slice(0, n))
    def top(m, n): a = m[2][0].start; return ap(m[0], slice(a, a + n), p=slice(0, n))
    def s8(name): j = 144 * SELS.index(name); return c("SEL", j + 15, j + 143, 16)
    def iota(o, pat, base, cm):
        fl = SCRATCH[o[0]][2] != I32
        if fl: f = lambda g, r: g.iota(r(o), pat, base, cm, allow_small_or_imprecise_dtypes=True)
        else: f = lambda g, r: g.iota(r(o), pat, base, cm)
        add({"q": (f, 150 + 2 * CY * o[3])}, [], [o])
    def sel(o, i, pat, op, base, cm):
        add({"q": (lambda g, r: g.affine_select(r(o), r(i), pat, op, 0.0, base, cm), 170 + 2 * CY * o[3])}, [i], [o])
    def dma(o, i, q="y", nbytes=None):
        x = i if i[0] in SCRATCH else o
        nb = nbytes or x[3] * size(x) * 128
        fs = {"y": lambda g, r: g.sync.dma_start(r(o), r(i)), "s": lambda g, r: g.scalar.dma_start(r(o), r(i))}
        add({e: (fs[e], 100) for e in q}, [i], [o], "dma", P["dma"] + nb / 190.0)
    def ps(bank, a, b, s=1): return c("PS", 512 * bank + a, 512 * bank + b, s)
    mats = {}; fmats = {}
    def mat(kind, w=1.0):
        if (kind, w) not in mats:
            j = len(mats); mats[kind, w] = c("MAT", 128 * j, 128 * j + 128)
            if w != 1.0:
                keep = tag[0]; tag[0] = "i"; ev(mats[kind, w], mat(kind), 0.0, w); tag[0] = keep
        return mats[kind, w]
    def fmat(kind, w):
        if (kind, w) not in fmats:
            j = len(fmats); fmats[kind, w] = c("MF", 128 * j, 128 * j + 128)
            keep = tag[0]; tag[0] = "i"; ev(fmats[kind, w], mat(kind), 0.0, w); tag[0] = keep
        return fmats[kind, w]
    def idm(w): return mat("I", float(w))
    def sh(name, r): j = 144 * SELS.index(name); return c("SEL", j + 15 - r, j + 143 - r)
    def col(j): return c("COL", j, j + 1)
    def compact(out, m, buf, a, n):
        return [(out, sh(m, r), c(buf, a + r, a + 16 * n, 16)) for r in range(16)]
    def across(out, m, buf, a, n=16):
        return [(out, sh(m, r), c(buf, a + n * r, a + n * r + n)) for r in range(16)]
    def e3(b, a, z, n=2): return ap(b, slice(0, n), slice(a, z))
    PM, PM16, WA_, WB_, WC_, WD_, WE_, THR, LIA, LOST, CB_, LQ, LO_, HI_, WF_, WG_, WH_, LA = range(18)
    def oh(j): return c("OH", j, j + 1)
    LW = P["last"]; MW = 128 - LW; B0 = 16 * MW
    runs = [(B0, 2048, MW, 128), (0, B0, 0, MW), (2048, 3072, 128, 192)] + [(3072 + 256 * u, 3328 + 256 * u, 192 + 16 * u, 208 + 16 * u) for u in range(4)]

    loads = [(ap("EI", h, slice(k0, k1)), ap("en0", slice(a, z), p=slice(h, 16, 2))) for a, z, k0, k1 in runs[:3] for h in range(2)] + [(ap("SI"), ap("snd", slice(0, 24), p=slice(0, 128)))]
    loads += [(c("Y0N", 768 * j, 768 * j + 768), ap("y0", slice(768 * j, 768 * j + 768), p=slice(0, 128))) for j in range(4)]
    loads.insert(P["xat"], (c("XT", 0, 512), ap("x0", slice(0, 512), p=slice(0, 128))))
    for j, (o, i) in enumerate(loads):
        dma(o, i, "ys"[j % 2], sum(x[3] * size(x) * 100 for x, y in loads[:j + 1])); ops[-1]["rd"].append(c("CI", 4 + j % 2, 5 + j % 2)); ops[-1]["wr"].append(c("CI", 4 + j % 2, 5 + j % 2)); ops[-1]["row"] = True
    fill(ap("ONE"), 1.0, "v")
    iota(c("CI", 0, 1), [[1, 1]], 0, 1)
    ONES, TRI, TM, TF, HOLE = mat("O"), mat("T"), mat("M"), mat("F"), mat("H")
    sel(TRI, c("ONE", 0, 128), [[-16, 8], [0, 16]], A.is_ge, 0, 1)
    sel(ONES, TRI, [[16, 8], [0, 16]], A.is_ge, 15, -1)
    sel(idm(1), c("ONE", 0, 128), [[-1, 128]], A.is_equal, 0, 1)
    sel(TRI, ONES, [[1, 128]], A.is_gt, 0, -1)
    ts(c("CI", 1, 2), c("CI", 0, 1), 15, None, A.bitwise_and); cp(col(PM), c("CI", 1, 2))
    iota(ap("IO"), [[1, 16]], 0, 0); fill(c("TB", 0, 16), 2.0)
    ts(ap("OH"), ap("IO"), col(PM), None, A.is_equal)
    fill(ap("SEL"), 0.0, "v")
    def mksel(name, w1, w2=None):
        j = 144 * SELS.index(name); o = c("SEL", j + 15, j + 143, 16); i = (ONES[0], ONES[1], (slice(ONES[2][0].start, ONES[2][0].stop, 16),), 8, ONES[4], ONES[5])
        if w2 is None: ts(o, i, w1, None, A.mult)
        else: ts(o, i, w1, w2, A.mult, A.mult)
    mksel("S", 1.0); mksel("P0", oh(0)); mksel("P16", oh(0), 16.0)
    for j in range(3): ev(c("I3", 128 * j, 128 * j + 128), idm(1), 0.0, -1024.0); ev(c("S24", 8 * j, 8 * j + 8), s8("S"), 0.0, -1.0)
    ts(col(WA_), oh(1), 16.0, oh(0), A.mult, A.add); mksel("PKW", col(WA_), 256.0)
    ev(c("W16", 0, 8), s8("PKW")); ts(c("W16", 8, 16), s8("S"), oh(2), None, A.mult); ev(c("W16", 16, 24), s8("PKW")); fill(ap("C3"), 0.0); ev(c("C3", 128, 256), idm(1), 0.0, 32.0)
    if 1 in P["chain"]: ts(c("W16", 24, 32), s8("S"), oh(2), 2.0, A.mult, A.mult)
    ts(col(WB_), col(PM), 2.0, None, A.is_lt)
    ts(col(WC_), oh(2), 1024.0, col(WB_), A.mult, A.add); ts(col(WD_), oh(3), 2048.0, col(WC_), A.mult, A.add); mksel("PKR", col(WD_))
    ts(col(WE_), col(PM), -256.0, None, A.add); mksel("RW", col(WE_))
    if any(P["relu"]): mksel("S4", 4.0); mksel("SN", -2.0)
    if P["direct"]:
        mksel("S2", 2.0); ts(col(WF_), oh(0), -6400.0, None, A.mult); ts(col(WG_), oh(1), -95.0, col(WF_), A.mult, A.add); mksel("SC", col(WG_))
        ts(col(WH_), col(PM), 3.0, None, A.not_equal); ts(HOLE, idm(1), col(WH_), None, A.mult)
        ts(col(LO_), oh(3), 9999.0, -10000.0, A.mult, A.add); ts(col(HI_), oh(3), -9999.0, 10000.0, A.mult, A.add)
    tt(TM, TRI, ONES, A.subtract); tt(TM, TM, idm(-4096), A.min)
    tt(TF, TRI, idm(1), A.subtract)
    ts(col(PM16), col(PM), 16.0, None, A.mult)
    iota(c("T2", 0, 4), [[256, 4]], 3071, 0); ts(col(CB_), col(PM), -16384.0, None, A.mult); ts(ap("BC"), c("T2", 0, 4), col(CB_), None, A.add)
    iota(ap("IO1"), [[0, 2], [1, 256]], 1, 0); iota(ap("IOM"), [[1, 256]], -4095, 0); iota(ap("KT"), [[1, 96]], 0, 0)
    for a in range(0, RW_, 1008): fill(c("R", a, a + 1008), 0.0)
    ev(ap("K2"), ap("ONE"), 0.0, 1366.0, "v")
    fill(ap("ZE"), 0.0); fill(ap("PL"), 0.0); fill(c("LIW", 256, 272), 192.0)
    fill(ap("ETA", 2, slice(0, 256)), 0.75)
    for j in range(2): fill(ap("ETA", j, slice(192, 256)), 0.25 * (j + 1))
    fill(c("WB", CST, CST + 16), 192.0); fill(c("WB", CST2, CST2 + 16), 192.0)
    for a in (512, 1024): fill(c("WP", a, a + 512), 0.0); fill(c("BL", a, a + 512), -1.0); fill(c("HH", a, a + 512), 64.0)
    for t in range(4): fill(c("DT", 272 * t, 272 * t + 256), 128.0 + DELTA[t]); fill(c("DT", 272 * t + 256, 272 * t + 272), 128.0)
    iota(c("T2", 256, 512), [[16, 256]], 0, 0); ts(ap("VC"), c("T2", 256, 512), col(PM), None, A.add)
    ev(c("ALT", 0, 256), ap("VC"), 4096.0 - LOO); ev(c("ALT", 256, 512), ap("VC"), YBO - LOO - 4096.0); ev(ap("NB"), c("VC", 0, 16), -0.5, -1.0)
    iota(ap("JI"), [[128, 2], [0, 8]], 0, 1); fill(ap("BJ"), 0, "v"); fill(c("BT", 256, 272), 0.0)
    for j, (sh_, m) in enumerate([(0, 15), (4, 15)] + [(u, 1) for u in range(8)]):
        ts(ap("BJ", slice(0, 2), slice(j, 128, 16)), ap("JI"), sh_, m, A.logical_shift_right, A.bitwise_and)
    cp(ap("KD"), ap("BJ")); ts(col(WF_ + 8), col(WB_), -8.0, None, A.mult)
    for h in range(2): mm([(ps(4, 128 * h, 128 * h + 128), c("KD", 128 * h, 128 * h + 128), idm(1))])
    act(c("BT", 0, 256), ps(4, 0, 256), F.Identity, col(WF_ + 8))
    D8, D256 = mat("D8"), mat("D256"); PW, IN = WF_ + 9, WF_ + 10
    add({"v": (lambda g, r: g.vector.tensor_tensor_scan(r(c("TA", 0, 16)), r(c("ONE", 0, 16)), r(c("TB", 0, 16)), 0.0625, A.mult, A.mult), vc(16, 1))}, [c("ONE", 0, 16), c("TB", 0, 16)], [c("TA", 0, 16)])
    tt(c("TB", 0, 16), c("TA", 0, 16), ap("OH"), A.mult); total(col(PW), c("TB", 0, 16))
    for m, (a, z) in enumerate(((2, 5), (5, 8), (8, 10), (2, 10))):
        total(col(IN + m), c("OH", a, z)); tt(col(IN + 4 + m), col(IN + m), col(PW), A.mult)
        ts(c("Z32", 8 * m, 8 * m + 8), s8("S"), col(IN + 4 + m), (2.0, 0.25, 1.0 / 32, 16.0)[m], A.mult, A.mult)
    ts(D8, idm(1), col(IN + 3), 0.125, A.mult, A.mult); ts(D256, idm(1), col(WB_), 1.0 / 256, A.mult, A.mult)
    iota(ap("S16"), [[256, 4], [1, 16]], 0, 0); ts(ap("ULAST"), ap("S16"), col(PM16), None, A.add); ts(ap("NR"), ap("S16"), col(PM16), 512.0, A.add, A.add)
    def to_row(f, src, which):
        for a, z, k0, k1 in which: dma(ap("R", slice(RO + a, RO + z), p=slice(f, 128, 16)), src(k0, k1), "y")
    ei = lambda h: ap("EI", h, slice(0, 192)); e0 = lambda h: ap("E0", h, slice(0, 192))
    tt(c("TVF", 0, 192), ei(0), ei(1), A.min); ev(ap("EB"), c("TVF", 0, 192), -256.0); to_row(0, lambda a, z: c("EB", a, z), runs[:3])
    ts(ap("NSW"), ei(0), 1536.0, 4096.0, A.is_lt, A.mult); tt(c("T2", 0, 192), ei(1), ap("NSW"), A.add); tt(e0(0), ei(0), c("T2", 0, 192), A.min)
    tt(ap("SWF"), ei(0), ap("NSW"), A.subtract); tt(e0(1), ei(1), ap("SWF"), A.max); cp(e3("EU0", 0, 192), e3("E0", 0, 192))
    ev(ap("ETA", 0, slice(0, 192)), ap("NSW"), 0.5, -1.0 / 16384); ev(ap("ETA", 1, slice(0, 192)), ap("NSW"), 0.25, 1.0 / 16384)
    fill(ap("FK"), 0.0); ts(ap("FK", 1, slice(0, 192)), e0(1), 1536.0, 2.0, A.is_ge, A.mult)
    ts(ap("TW"), ap("SI"), float(RO), None, A.add)
    gat(ap("GT"), ap("R"), ap("TW"))
    mm(compact(ps(6, 0, 24), "P0", "GT", 0, 24))
    ts(ap("OWU"), ps(6, 0, 24), 256.0, None, A.add); ev(ap("OWN"), ps(6, 0, 24), 256.0)
    for a, z, k0, k1 in (runs[1], runs[0], runs[2]): mm(across(ps(7, k0, k1), "S", "Y0N", a, k1 - k0))
    act(c("LV0", 0, 192), ps(7, 0, 192), F.Sign, -175.5, acc=col(LA))
    dma(ap("BI"), ap("bl0", slice(0, 512), p=slice(0, 128)), "y"); ops[-1]["rd"].append(c("Y0N", 0, 3072))

    def cells_ahead(t):
        C = 512 + 256 * t
        mm(compact(ps(0, 0, C // 16), "S", "XT", 0, C // 16)); ev(c("SX", 0, C // 16), ps(0, 0, C // 16), THETA[t] + 4128.0 + 1536 + 128 * t, -1.0)
    def twins_ahead(t):
        send(2 * t, c("XT", 0, 512 + 256 * t))
    def send(j, table):
        gat(ap("SN", j % 4, slice(0, 384)), table, ap("OWU"))
        add({"q": (None, 600)}, [ap("SN", j % 4, slice(0, 384))], [], "send", j)
        add({}, [], [ap("LN", j, slice(0, 384))], "arrive", j)
    def count_ahead(t):
        o = ps(YB, 0, 1); Kc = 32 + 16 * t
        if t: mm([(o, fmat("O", 1.0 / 32), col(LIA))] + [(o, fmat("O", 0.5), col(LA + s)) for s in range(2)], stop=False)
        mm([(o, fmat("O", 0.5), col(LA + (2 if t else 0)))], start=not t)
        ts(c("NSX", 0, Kc), c("SX", 0, Kc), o, None, A.add)
        if t: ts(col(LQ), o, 1536 + 128 * t + 4112.5, None, A.add)
        else: ts(c("QB", 0, 1), o, -1.0, -1536 - 4112.5, A.mult, A.add)
    cells_ahead(0); twins_ahead(0); count_ahead(0)
    for a, z, k0, k1 in (runs[2], runs[1], runs[0]):
        for k in range(k0, k1, 32):
            bk = (1, 2, 3)[k // 32 % 3]; u = a + k - k0
            mm([(ps(bk, r, 512, 16), idm(1), c("Y0N", u + (k1 - k0) * r, u + (k1 - k0) * r + 32)) for r in range(16)], each=True); ev(c("WB", 16 * k, 16 * k + 512), ps(bk, 0, 512), 192.0)
    ev(ap("FR"), c("Y0N", 0, 1024), 1532.5)
    for a in (0, 512): mm([(ps(1 + a // 512, 0, 512), idm(1), c("Y0N", a, a + 512)), (ps(1 + a // 512, 0, 512), idm(-1), c("FR", a, a + 512))])
    ev(ap("DR"), c("PS", 512, 1536), 1564.5)
    cp(c("BL", 0, 512), ap("BI"))
    reg = [0, 0]
    sm = lambda j, a=0, z=256: ap("SM", j, slice(a, z)); nm = lambda j: ap("NM", j, slice(0, 256))
    hp = lambda b, h: ps(b, 256 * h, 256 * h + 256)
    def kept(bank, kind, w, a=0, z=256, n=256, a0=0):
        return [(ps(bank, a - a0, z - a0), mat(kind, w), sm(0, a, z))] + [(ps(bank, n * h + a - a0, n * h + z - a0), mat(kind, (-w, w)[h]), sm(j, a, z)) for h in range(2) for j in (1, 2)]
    def names(t):
        return ("E%d" % (t % 2), "E%d" % (1 - t % 2) if t < 3 else "EF", "EU%d" % (t % 2), "EU%d" % (1 - t % 2), "LV%d" % (t % 2), "LV%d" % (1 - t % 2),
                (lambda a, b: c("WB", YBO + a, YBO + b), lambda a, b: c("WB", a, b), lambda a, b: c("WB", YBO + a, YBO + b), lambda a, b: c("YF", a, b))[t])

    def who(t):
        tag[0] = "w"
        C = 512 + 256 * t; Kc = C // 16; k_ = lambda b: c(b, 0, Kc); lost = col(LOST)
        if t:
            ts(c("QB", 0, 1), lost, col(LOST + 23), col(LQ), A.add, A.subtract); ts(c("QB", 1, 2), lost, col(LOST + 23), None, A.add)
            relu(e3("NM", 192, 256), ps(6, 0, 128), -1920.0)
            ts(k_("CA"), k_("NSX"), c("QB", 0, 1), c("QB", 1, 2), A.add, A.is_le)
        else: ts(k_("CA"), k_("NSX"), c("QB", 0, 1), 0.0, A.add, A.is_le)
        mm([(ps(5, 0, Kc), ONES, k_("CA")), (ps(5, 0, Kc), TM, k_("CA")), (ps(5, 1, Kc), mat("M", -1.0), c("CA", 0, Kc - 1))]); mm([(ps(5, 128, 128 + Kc), ONES, k_("CA"))])
        scan(k_("PL"), ps(5, 0, Kc))
        ts(k_("UBT"), k_("PL"), 4095.0, 256.0, A.add, A.min)
        scan(k_("CU"), ps(5, 128, 128 + Kc))
        for a in range(0, C, 512): z = min(C, a + 512); gtt(c("P2", a, z), c("DT", 272 * t, 272 * t + 272), c("UBT", a // 16, z // 16), c("XT", a, z), A.add)
        send(2 * t + 1, c("P2", 0, C))
        gat(c("BTG", 0, C), ap("BT"), k_("UBT"))
        def tables(a, z, x, p2, b0):
            ts(c("HH", a, z), p2, 191.0, 0.5, A.min, A.mult)
            o = ps(b0, 0, z - a); mm([(o, idm(2), x), (o, idm(-1), p2)])
            if P["lf"][a // 512]: relu(c("LP", a, z), o, 128.0); ev(c("WB", LOO + a, LOO + z), c("LP", a, z), -31.5)
            else: ts(c("WB", LOO + a, LOO + z), o, 96.5, -31.5, A.add, A.max)
        for j, a in enumerate(range(0, C, 512)):
            z = min(C, a + 512); tables(a, z, c("XT", a, z), c("P2", a, z), (6, 1, 6)[j]); o = ps((0, 5, 0)[j], 0, z - a)
            mm([(o, idm(2), c("HH", a, z)), (o, idm(-1), c("LP", a, z) if P["lf"][j] else c("WB", LOO + a, LOO + z)), (o, D256, c("BTG", a, z))]); ev(c("WP", a, z), o, -64.0 if P["lf"][j] else -79.75, 0.5)
        for a in range(0, C, 512):
            z = min(C, a + 512); o = ps(5, 0, z - a); mm([(o, idm(2), c("HH", a, z)), (o, D8, c("BTG", a, z))]); ev(c("WB", HIO + a, HIO + z), o, -159.5)
        x, f = ap("LN", 2 * t, slice(0, 384)), ap("LN", 2 * t + 1, slice(0, 384)); o = ps(7, 0, 384); fa, fb = ap("FA", 0, slice(0, 384)), ap("FA", 1, slice(0, 384))
        relu(fa, x, -float(DELTA[t])); relu(fb, x, DELTA[t] - 63.0)
        mm([(o, idm(-0.5), fa), (o, idm(-0.5), fb), (o, idm(-1.5), x)], stop=False); mm([(o, idm(2), f)], start=False)
        relu(c("WP", 1536, 1920), o, -256 - 1.5 * DELTA[t])
        tables(1536, 1920, x, f, 5); ev(c("WB", HIO + 1536, HIO + 1920), c("HH", 1536, 1920), -159.5, 2.0)

    def dividers(t):
        tag[0] = "l"
        C = 512 + 256 * t; Kc = C // 16
        for j in range(16): act(ap("JK", j, slice(0, Kc)), c("CU", 0, Kc), F.Sign, c("NB", j, j + 1), acc=c("ACC", j, j + 1))
        ts(ap("KI"), ap("ACC"), -0.5, Kc / 2.0, A.mult, A.add)
        gtt(ap("MK"), ap("PL"), ap("KI"), ap("IOM"), A.is_equal)
        gat(ap("KD"), ap("KT"), ap("KI"))
        mm([(ps(YB, 0, 16), fmat("I", -8.0), ap("ACC"))] + compact(ps(YB, 0, 16), "RW", "MK", 0, 16))
        tt(ap("DM"), ps(YB, 0, 16), c("VC", 8 * t, 8 * t + 16), A.min); ts(ap("DL2"), ap("DM"), 256.0 + C // 2, None, A.add)
        mm(across(ps(YB, 16, 32), "RW", "MK", 0) + across(ps(YB, 16, 32), "P16", "KD", 0)); ev(ap("VR"), ps(YB, 16, 32), 256.0, eng="v")
        ts(c("NXT", 256 * t, 256 * t + 256), c("IO1", 0, 256), c("CU", Kc - 1, Kc), None, A.is_gt)
        gat(c("WB", LOO + C, LOO + C + 256), c("HH", 0, 1536), ap("DL2"), -159.5, mul=2.0)
        gat(ap("OLD"), ap("BL"), ap("DL2")); ts(ap("OLU"), ap("OLD"), float(RO), None, A.add); ts(ap("O16"), ap("OLD"), -2047.0, None, A.add)
        gat(c("LIW", 0, 256), c("WP", 0, 1536), ap("DL2"), 192.0, mul=2.0)
        if t < 3:
            mm([(ps(YB, 0, 256), ONES, c("LIW", 0, 256))]); act(ap("LI"), ps(YB, 0, 256), F.Sign, -3247.5, acc=col(LIA))
            dma(ap("LC"), ap("LI", slice(0, 256), p=slice(0, 128, 16)), "y", 4096)

    def bridges(t):
        C = 512 + 256 * t; K = 192 + 16 * t; base = C
        E, En, EU, EUn, LV, LVn, ydst = names(t)
        ysrc = 0 if t % 2 == 0 else YBO
        win = c("WB", 0, CST2) if t % 2 == 0 else c("WB", LOO, YBO + 16 * K)
        def cut(a, z, n):
            e = [a + 2 * ((z - a) * j // (2 * n)) for j in range(n)] + [z]
            return list(zip(e[:-1], e[1:]))
        part = [(128, K), (0, 128)]; span = [(128, K), (0, MW), (MW, 128)]
        def upto(a, z, n): return cut(a, z, -(-(z - a) // n))
        def slot(j):
            pool = P[("abank", "bbank")[j]][int(tag[0][1])]; b = pool[reg[j] % len(pool)]; reg[j] += 1
            return 512 * b
        def wide(o, n, terms):
            for u in range(0, n, 512): w = min(512, n - u); mm([(c("PS", o + u, o + u + w), idm(x), c(b, a + u, a + u + w)) for x, b, a in terms])
        def phase_a(s):
            tag[0] = "a%d" % s
            k0, k1 = part[s]; Ks = k1 - k0
            chain = P["chain"][s] == 1; both = P["chain"][s] == 2; WZ = "UH" if both else "WZ"
            old, new, newest = upto(k0, min(k1, 192), P["gp"][s]), ([(192, k1 - 16)] if k1 > 208 else []), ([(k1 - 16, k1)] if k1 > 192 else [])
            for (a, z) in (old + new + newest, new + newest + old, new + old + newest)[P["newfirst"]]:
                a16, z16 = 16 * a, 16 * z; n = 1536 if a >= 192 else 1920
                gtt(c("UH", a16, z16), c("HH", 0, 1536), ap(EU, 0, slice(a, z)), c("WB", ysrc + a16, ysrc + z16), A.subtract)
                gat(c("WA", a16, z16), c("WP", 0, 1536), ap(EU, 0, slice(a, z)), -12.0, "v", 2.0)
                gtt(c("HZ", a16, z16), c("HH", 0, n), ap(EU, 1, slice(a, z)), c("UH", a16, z16), A.add)
                if both: gat(c("UH", a16, z16), c("WP", 0, n), ap(EU, 1, slice(a, z)), -12.0, "v", 2.0)
                elif chain:
                    gtt(c("WZ", a16, z16), c("WP", 0, n), ap(EU, 1, slice(a, z)), c("HZ", a16, z16), A.subtract)
                    act(c("AB", 3840 * 2 + a16, 3840 * 2 + z16), c("WZ", a16, z16), F.Abs, -128.0, 2.0)
                else: gat(c("WZ", a16, z16), c("WP", 0, n), ap(EU, 1, slice(a, z)), -12.0, mul=2.0)
                if P["relu"][s]: ts(c("AB", 3840 * 3 + a16, 3840 * 3 + z16), c("HZ", a16, z16), -64.0, None, A.max)
                else: act(c("AB", 3840 * 3 + a16, 3840 * 3 + z16), c("HZ", a16, z16), F.Abs, 128.0, 2.0)
                for (x, y) in upto(a, z, P["aw"][s]):
                    a16, z16 = 16 * x, 16 * y; n = z16 - a16; hz, wz, wa = (2, "HZ", a16), (-1, WZ, a16), (-1, "WA", a16)
                    for j, terms in ((1, [hz, wa]), (0, [(-2, "WZ", a16), wa])) if chain else ((1, [hz, wa]), (2, [hz, wz]), (0, [hz, wa, wz])):
                        o = slot(0); wide(o, n, terms); act(c("AB", 3840 * j + a16, 3840 * j + z16), c("PS", o, o + n), F.Abs, 140.0 - 12 * len(terms))
            XB = P["xb"][s]
            ne = 2 if both else 1
            mm([(pt(XB, 0, 128 + 128 * ne, Ks), c(LV, k0, k1), c("C3", 0, 128 + 128 * ne))], stop=False)
            for b, u, w in [("WA", 0, c("W16", 0, 16))] + ([("HZ", 128, c("W16", 24, 32)), ("WZ", 128, c("W16", 24, 32))] if chain else [(WZ, 128, c("W16", 8, 8 + 8 * ne))]):
                mm([(pt(XB, u + r, u + 16 * w[3], Ks, 16), c(b, 16 * k0 + r, 16 * k1, 16), w) for r in range(16)], False, b == WZ)
            tag[0] = "f%d" % s
            tn = lambda b, j, n=1: ap(b, s, slice(128 * j, 128 * (j + n)), p=slice(0, Ks))
            act(tn("TT", 0), pt(XB, 128, 256, Ks), F.Sign, -23.0 if chain else -11.0)
            for h in range(ne): ts(tn("FL", h), pt(XB, 256 * h, 256 * h + 128, Ks), 1.0 / 256, FO - t + 8.5 / 256, A.mult, A.add)
            for h in range(ne): ev(tn("FF", h), pt(XB, 256 * h, 256 * h + 128, Ks), 256.0 * (FO - 13) - 120)
            mm(([(ps(XB, 0, 2 * Ks), idm(-4096), e3("FK", k0, k1))] if both else [])
               + [(ps(XB, Ks * h, Ks * h + Ks), tn(b, h), top(m, Ks)) for h in range(ne) for b, m in (("FF", fmat("I", 1.0)), ("FL", idm(-256)))], stop=False)
            mm([(pt(YB, 0, 384, Ks), c(LV, k0, k1), ap("I3"))] + [(pt(YB, 128 * j, 128 * j + 128, Ks), ap("ETA", j, slice(k0, k1)), idm(1)) for j in range(3)], stop=False)
            turned = lambda j, b, a, m: [(pt(YB, 128 * j + r, 128 * j + 128, Ks, 16), c(b, a + 16 * k0 + r, a + 16 * k1, 16), s8(m)) for r in range(16)]
            if P["relu"][s]: mm([(pt(YB, 256, 384, Ks), c("ONE", 0, Ks), mat("O", 128.0))] + turned(2, "AB", 3840 * 3, "S4") + turned(2, "HZ", 0, "SN"), False, False)
            else: mm(turned(2, "AB", 3840 * 3, "S"), False, False)
            for j in (1, 2): mm(turned(j - 1, "AB", 3840 * j, "S"), False, False)
            mm([(pt(YB, r, 384, Ks, 16), c("AB", 16 * k0 + r, 16 * k1, 16), ap("S24")) for r in range(16)], start=False)
        def decide(s):
            tag[0] = "d%d" % s
            k0, k1 = part[s]; Ks = k1 - k0; XB = P["xb"][s]; dec = ps(XB, 0, Ks)
            tn = lambda b, j, n=1: ap(b, s, slice(128 * j, 128 * (j + n)), p=slice(0, Ks))
            S_ = lambda j: ap("SS", j - 1, slice(0, 128), p=slice(0, Ks)); T_ = lambda j: pt(YB, 128 * j - 128, 128 * j, Ks); Q_ = lambda j: tn("EQ", j - 1); P_ = lambda j: ps(YB, Ks * j, Ks * j + Ks)
            ts(S_(1), T_(1), -1024.0, None, A.min)
            for j in (2, 3): tt(S_(j), T_(j), S_(j - 1), A.min)
            for j in (3, 1, 2): tt(Q_(j), T_(j), S_(3), A.is_equal)
            sg = 1.0 if t % 2 == 0 else -1.0; pole = ((2, 3), (1, 3))
            for h in (1, 0):
                mm([(P_(h), l, x) for l, x in [(idm(1), ap(E, h, slice(k0, k1))), (tn("TT", 0), top(idm(4096 * sg), Ks))] + [(Q_(j), top(idm(1920), Ks)) for j in pole[h]]])
            mm([(P_(2), Q_(3), top(idm(1), Ks))])
            cs = LOO - 4096.0 if t % 2 == 0 else 4096.0; mo = A.max if t % 2 == 0 else A.min
            ts(ap("IX", 1, slice(k0, k1)), P_(1), cs, float(CST if t % 2 == 0 else CST2 - LOO), A.add, mo)
            tt(c("IA", 0, Ks), P_(0), c("ALT", 256 * (t % 2) + k0, 256 * (t % 2) + k1), mo); ts(ap("IX", 0, slice(k0, k1)), c("IA", 0, Ks), cs, None, A.add)
            ev(c("EC", k0, k1), P_(2))
            ne = 2 if P["chain"][s] == 2 else 1
            mm([(ps(XB, Ks * h, Ks * h + Ks), Q_(j), top(idm(4096), Ks)) for h in range(ne) for j in pole[h]], start=False)
            moved(slice(0, ne), ps(XB, 0, ne * Ks), k0, k1)
        def moved(h, dec, k0, k1):
            x = lambda b: ap(b, h, slice(k0, k1))
            relu(x("TR"), dec, 1.0 - base); tt(x(En), dec, x(E), A.max)
            if t < 3: cp(x(EUn), x(En))
        def second(s, spans):
            for u in spans:
                tag[0] = "b%d" % u
                for (a, z) in upto(span[u][0], span[u][1], P["zw"][u]): gat(c("D", 16 * a, 16 * z), win, ap("IX", 1, slice(a, z)))
            tag[0] = "e%d" % s
            if P["chain"][s] == 2: return
            k0, k1 = part[s]; Ks = k1 - k0; XB = P["xb"][s]; dec = ps(XB, 0, Ks)
            tn = lambda b, j, n=1: ap(b, s, slice(128 * j, 128 * (j + n)), p=slice(0, Ks))
            mm([(pt(XB, r, 512, Ks, 16), c("D", 16 * k0 + r, 16 * k1, 16), ap("Z32")) for r in range(16)], each=True)
            ts(tn("FL", 1, 3), pt(XB, 0, 384, Ks), 1300.0625, None, A.add); ev(tn("FF", 1), pt(XB, 384, 512, Ks), 584.0 * 1300 + 292 + base - 4096)
            mm([(dec, tn("FF", 1), top(fmat("I", 1.0), Ks)), (dec, idm(-4096), ap("FK", 1, slice(k0, k1)))] + [(dec, tn("EQ", j), top(idm(4096), Ks)) for j in (0, 2)]
               + [(dec, tn("FL", 1 + m), top(idm(-8.0 ** (m + 1)), Ks)) for m in range(3)])
            moved(1, dec, k0, k1)
        def phase_b(s):
            tag[0] = "b%d" % s
            k0, k1 = span[s]; how = P["bmode"][s]
            for (a, z) in upto(k0, k1, P["bw"][s]):
                a16, z16 = 16 * a, 16 * z; n = z16 - a16; D = lambda j: c("D", 3840 * j + a16, 3840 * j + z16); d_ = lambda w, j: (w, "D", 3840 * j + a16)
                if how == 2:
                    gat(D(1), win, ap("IX", 0, slice(a, z)))
                    o = slot(1); wide(o, n, [d_(1, 0), d_(-1, 1)]); act(D(2), c("PS", o, o + n), F.Abs)
                else: gtt(D(1), win, ap("IX", 0, slice(a, z)), D(0), A.subtract)
                if how == 1: act(D(2), D(1), F.Abs)
                o = slot(1); y = (0.5, "WB", ysrc + a16)
                if how: wide(o, n, [y, d_(0.5, 2)])
                else: ts(D(2), D(1), 0.0, None, A.max); wide(o, n, [y, d_(-0.5, 1), d_(1, 2)])
                ev(ydst(a16, z16), c("PS", o, o + n), 95.75)
        y_ = ydst(0, 16); yb, y0 = y_[0], y_[2][0].start
        def alive(s):
            tag[0] = "b%d" % s
            k0, k1 = span[s]; Ks = k1 - k0; o = slot(1); o = c("PS", o, o + Ks)
            mm(compact(o, "S", yb, y0 + 16 * k0, Ks))
            act(c(LVn, k0, k1), o, F.Sign, -3247.5, acc=col(LA + s) if t < 3 else None)
        def live_row():
            nb = LW // 32; per = 16 // nb
            for j in range(nb):
                bk = (XB, YB)[j]; x = c("R", RO + B0 + 512 * j, RO + B0 + 512 * j + 512)
                mm([(ps(bk, 0, 512), sh("SC", 3), ap("ONE")), (ps(bk, 0, 512), HOLE, x)], stop=False)
                mm([(ps(bk, LW * r, LW * r + LW), sh("S2", 3), c(yb, y0 + B0 + per * j + r, y0 + 2048, 16)) for r in range(per)], start=False)
                ts(x, ps(bk, 0, 512), col(LO_), col(HI_), A.max, A.min)
        def cells_on():
            tag[0] = "c"
            Cn = C + 256
            if t == 3: ev(ap("XT"), c("WB", LOO, LOO + 1536), 31.5); return dma(ap("yx", slice(0, 1536), p=slice(0, 128)), ap("XT"), "y")
            for a in range(0, Cn, 512):
                z = min(Cn, a + 512); bk = a // 512; o = ps(bk, 0, z - a); lst = [(o, idm(1), c("WB", LOO + a, LOO + z))]
                if a >= 512: lst.append((o, idm(-128), c("NXT", a - 512, z - 512)))
                u = a
                while u < z:
                    s0 = (u + 331 * t) % 1024; n = min(z - u, 1024 - s0); lst.append((ps(bk, u - a, u - a + n), idm(1), c("DR", s0, s0 + n))); u += n
                mm(lst)
            for a in range(0, Cn, 1024):
                z = min(Cn, a + 1024); ts(c("XT", a, z), c("PS", a, z), 0.0, 63.0, A.max, A.min)
        def to_rows(fs, which):
            for f in fs: to_row(f, (lambda a, z: ap("TR", 0, slice(a, z)), lambda a, z: ap("TR", 1, slice(a, z)), lambda a, z: c("EC", a, z), lambda a, z: c(LVn, a, z))[f], which)
        phase_a(0); decide(0); to_rows((0, 2), runs[2:3 + t]); phase_a(1); second(0, [0]); to_rows((1,), runs[2:3 + t]); phase_b(0); alive(0); to_rows((3,), runs[2:3 + t])
        decide(1); to_rows((0, 1, 2) if P["chain"][1] == 2 else (0, 2), runs[:2])
        cells_on()
        if t < 3: cells_ahead(t + 1)
        tag[0] = "t"
        if t < 3:
            gat(ap("GT"), ap("R"), ap("TW"))
            o = ps(YB, 0, 24); mm(compact(o, "P0", "GT", 0, 24))
            ts(ap("TA"), o, 0.5, base - 1.0, A.is_gt, A.mult); tt(ap("TB"), o, ap("TA"), A.add); tt(ap("OWN"), ap("TB"), ap("OWN"), A.max); cp(ap("OWU"), ap("OWN"))
            twins_ahead(t + 1)
        second(1, [1, 2])
        if P["chain"][1] != 2: to_rows((1,), runs[:2])
        if t == 3:
            ef = lambda h: ap("EF", h, slice(0, 192))
            tt(c("T2", 0, 192), ef(0), ap("NSW"), A.add); tt(ef(1), ef(1), c("T2", 0, 192), A.min); tt(ef(0), ef(0), ap("SWF"), A.max)
            for h in range(2):
                for a, z, k0, k1 in runs[:6]: dma(ap("ye", slice(a, z), p=slice(h, 16, 2)), ap(En, h, slice(k0, k1)), "y")
        phase_b(1); alive(1); to_rows((3,), runs[1:2]); phase_b(2)
        if t < 3 or not P["direct"]: alive(2)
        if P["direct"]: live_row()
        if not P["direct"]: to_rows((3,), runs[:1])
        if t < 3: count_ahead(t + 1)
        else:
            for a, z, k0, k1 in (runs[2], runs[1], runs[0]):
                w = k1 - k0; per = min(16, 1 << ((512 // w).bit_length() - 1))
                for r0 in range(0, 16, per):
                    bk = (7, YB)[r0 // per % 2]
                    mm([(ps(bk, w * r, w * r + w), idm(1), c("YF", 16 * k0 + r0 + r, 16 * k1, 16)) for r in range(per)], each=True); ev(c("Y0N", a + w * r0, a + w * (r0 + per)), ps(bk, 0, w * per), -192.0)
                dma(ap("yy", slice(a, z), p=slice(0, 128)), c("Y0N", a, z), "y")
            gat(c("FR", 0, 768), c("YF", 3072, 3840), c("ULAST", 0, 48), -192.0)
            dma(ap("yy", slice(3072, 3840), p=slice(0, 128)), c("FR", 0, 768), "y")

    def slots(t):
        tag[0] = "s"
        for bk, a, z in ((2, 0, 192), (6, 192, 256)):
            n = z - a; cn = lambda h: ps(bk, n * h, n * h + n)
            mm([(ps(bk, 0, 2 * n), idm(-1), c("ONE", 0, 2 * n)), (cn(0), mat("O", 128.0), c("NXT", 256 * t + a, 256 * t + z))] + ([(cn(h), idm(1), c("LI", a, z)) for h in range(2)] if t < 3 else []), stop=False)
        for bk, a, z in ((0, 0, 96), (1, 96, 192), (5, 192, 256)):
            for u, w in ((a, (a + z) // 2), ((a + z) // 2, z)):
                gat(c("D", 16 * u, 16 * w), ap("R"), c("OLU", u, w))
                if t < 3 and P["lvfirst"]: ops[-1]["rd"].append(col(LA + 2))
            o = ps(bk, 0, z - a)
            mm([(o, idm(-1), c("IO1", a, z))] + compact(o, "PKR", "D", 16 * a, z - a))
            ts(sm(0, a, z), o, 0.0, None, A.is_gt); ts(sm(1, a, z), o, 2048.0, None, A.is_equal); ts(sm(2, a, z), o, 2560.0, None, A.is_ge)
            mm(kept(2, "O", 128.0, a, z, 192) if a < 192 else kept(6, "O", 128.0, a, z, 64, 192), False, z >= 192)
            if t < 3 and z == 192: act(c("T2", 0, 384), ps(2, 0, 384), F.Relu, -2047.0, acc=col(LOST + 23))
        if t < 3: act(c("T2", 384, 512), ps(6, 0, 128), F.Relu, -2047.0, acc=col(LOST))

    def books(t):
        tag[0] = "k"
        C = 512 + 256 * t; K = 192 + 16 * t
        E, En, EU, EUn, LV, LVn, ydst = names(t)
        relu(e3("NM", 0, 192), ps(2, 0, 384), -1920.0)
        if t == 3: relu(e3("NM", 192, 256), ps(6, 0, 128), -1920.0)
        if P["ncdma"] and t < 3:
            for h in range(2): dma(c("NC", 16 * h, 16 * h + 16), ap("NM", h, slice(0, 256), p=slice(0, 128, 16)), "y", 4096)
        else: mm([(ps(2, 0, 32), sh("P0", r), e3("NM", 16 * r, 16 * r + 16)) for r in range(16)]); ev(ap("NC"), ps(2, 0, 32))
        q = lambda j: ps(2, 32 + 16 * j, 48 + 16 * j); nc = [c("NC", 0, 16), c("NC", 16, 32)]
        for j, (x, w) in enumerate(((ap("VR"), -128), (c("NR", 16 * t, 16 * t + 16), -128), (c("NR", 0, 16), 16))[:3 if t < 3 else 2]): mm([(q(j), idm(1), x)] + [(q(j), idm(w), y) for y in nc])
        if t < 3:
            mm([(q(3), idm(1), ap("LC"))] + [(q(3), idm(-1), y) for y in nc])
            ts(ap("DLM"), q(2), -512.0, 256.0, A.add, A.min)
            gat(ydst(16 * K, 16 * K + 256), ap("LIW"), ap("DLM"))
        ts(e3(En, K, K + 16), ps(2, 32, 64), 0.0, None, A.max)
        if t < 3: ts(e3(EUn, K, K + 16), ps(2, 32, 64), 0.0, None, A.max); act(c(LVn, K, K + 16), q(3), F.Sign)
        else:
            o = ps(0, 0, 256); mm([(o, idm(1), c("LIW", 0, 256))] + [(o, idm(-1), nm(j)) for j in range(2)]); relu(c("FR", 768, 1024), o, -192.0)
            dma(ap("yy", slice(3840, 4096), p=slice(0, 128)), c("FR", 768, 1024), "s")
            for h in range(2): dma(ap("ye", slice(3840, 4096), p=slice(h, 16, 2)), ap(En, h, slice(240, 256)), "ys"[h])
        mm([(ps(XB, 0, 512), idm(-1.5), ap("K2"))] + [(hp(XB, h), idm(1), ap("O16")) for h in range(2)], stop=False)
        mm([(ps(YB, 0, 512), idm(1), ap("IO1"))], stop=False)
        for a, z in ((0, 96), (96, 192), (192, 256)): mm(kept(XB, "I", 4096.0, a, z), False, z == 256); mm(kept(YB, "F", 16384.0, a, z), False, False)
        for h in range(2): mm([(hp(YB, h), idm(-128), nm(j)) for j in range(2)], False, h == 1)
        t2 = lambda h: c("T2", 256 * h, 256 * h + 256)
        for h in range(2): ts(t2(h), hp(YB, h), c("BC", t, t + 1), -1.0, A.add, A.max)
        tt(ap("TVF"), hp(XB, 0), t2(0), A.max); tt(c("BL", C, C + 256), hp(XB, 1), t2(1), A.max); sca(ap("BL"), ap("DL2"), ap("TVF"))
        if t == 3:
            for j in range(2): dma(ap("yl", slice(768 * j, 768 * j + 768), p=slice(0, 128)), c("BL", 768 * j, 768 * j + 768), "ys"[j])

    who(0)
    for t in range(4):
        dividers(t); bridges(t); slots(t)
        if t < 3: who(t + 1)
        books(t)
    return ops


def depend(ops):
    seen = {}
    for n, o in enumerate(ops):
        deps = {}
        acc = [(x, False) for x in o["rd"]] + [(x, True) for x in o["wr"]]
        for x, w in acc:
            for m, pm, cm, mw in seen.get(x[0], []):
                if (w or mw or x[0] == "PS") and m != n and pm & x[4] and cm & x[5]:
                    hard = (mw and not w) or ((w or mw) and not P["war"]) or ops[m]["kind"] != "c" or o["kind"] != "c"
                    if ("p" in o["alts"] and "p" in ops[m]["alts"]) or ("row" in o and "row" in ops[m]): hard = False
                    deps[m] = deps.get(m, False) or hard
        for x, w in acc:
            lst = seen.setdefault(x[0], [])
            if w: lst[:] = [e for e in lst if (e[1] & ~x[4]) or (e[2] & ~x[5])]
            lst.append((n, x[4], x[5], w))
        if o["kind"] == "arrive": deps = {n - 1: True}
        o["deps"] = deps


def settle(ops, others):
    lat, far, bias = P["lat"], P["far"], P["bias"]
    n = len(ops); kids = [{} for o in ops]
    for i, o in enumerate(ops):
        for d, hard in o["deps"].items(): kids[d][i] = hard
    tail = [far if o["kind"] == "arrive" else o["x"] if o["kind"] == "dma" else 0.0 for o in ops]
    def after(z, t):
        a, b = 0, len(z)
        while a < b:
            m = (a + b) // 2
            if z[m] > t: b = m
            else: a = m + 1
        return a
    def lay(key, back, due=None, fixed=None):
        lines = {e: ([], []) for e in "vspqy"}; st = [0.0] * n; en = [0.0] * n; eng = [None] * n
        for i in sorted(range(n), key=key):
            o = ops[i]; near = kids[i] if back else o["deps"]; best = None
            for e, v in o["alts"].items():
                if fixed and e != fixed[i]: continue
                if back: t0 = max([en[d] + (lat + tail[i] if hard or eng[d] != e else 0.0) for d, hard in near.items()] + [tail[i]])
                else: t0 = max([en[d] + lat if hard or eng[d] != e else en[d] - tail[d] for d, hard in near.items()] + [0.0])
                a, z = lines[e]; j = after(z, t0); x = t0
                while j < len(a) and a[j] < x + v[1]: x = max(x, z[j]); j += 1
                if due is None: sc = x + v[1] * (bias if e == "v" else 1.0)
                else: sc = max(x + v[1], due[i] - P["slack"]) + {"v": P["tilt"] * v[1], "q": 1e-3 * v[1]}.get(e, 0.0)
                if best is None or sc < best[0]: best = (sc, x, e, j)
            if best is None: st[i] = en[i] = max([en[d] + lat for d in near] + [0.0]) + (tail[i] if back else 0.0)
            else:
                x, e, j = best[1:]; lines[e][0].insert(j, x); lines[e][1].insert(j, x + o["alts"][e][1]); st[i] = x; en[i] = x + o["alts"][e][1]; eng[i] = e
            if not back: en[i] += tail[i]
        return st, en, eng
    pr = [0.0] * n
    for i in range(n - 1, -1, -1):
        pr[i] = min([v[1] for v in ops[i]["alts"].values()] + [0.0] * (not ops[i]["alts"])) + tail[i] + lat + max([pr[k] for k in kids[i]] + [0.0])
    st, en, eng = lay(lambda i: (-pr[i], i), False); top = (max(en), st, en, eng)
    for k in range(P["rounds"]):
        on = P["due"] and k >= 2
        sb, eb, x = lay(lambda i: (-en[i], -i), True, [max(en) - a for a in st] if on else None)
        due = [max(eb) - a + b for a, b in zip(sb, tail)] if on else None
        st, en, eng = lay(lambda i: (-eb[i], i), False, due)
        if max(en) < top[0]: top = (max(en), st, en, eng, eb, due)
    marks = [i for i in range(n) if ops[i]["wr"] and ops[i]["wr"][0][0] == "UBT"]
    rng = np.random.default_rng(1)
    def spans(st, eng):
        order = sorted(range(n), key=lambda i: (st[i], i)); tot = 0.0
        for alt, wake in others:
            z = [0.0] * n; a = [0.0] * n; line = {e: 0.0 for e in "vspqy"}
            for i in order:
                e = eng[i]; o = alt[i]; t0 = line[e] if e else 0.0
                for d, hard in ops[i]["deps"].items():
                    if (hard or eng[d] != e) and z[d] + wake > t0: t0 = z[d] + wake
                a[i] = t0
                if e: t0 += o[0][e][1]; line[e] = t0
                z[i] = t0 + o[1]
            tot = tot + np.diff([0.0] + [a[i] for i in marks] + [max(z)])
        return tot
    free = [i for i in range(n) if "v" in ops[i]["alts"] and "s" in ops[i]["alts"]]
    def again(eb, eng):
        pr = list(eb)
        for i in range(n - 1, -1, -1): pr[i] = max([pr[i]] + [pr[j] for j in kids[i]])
        st, en, x = lay(lambda i: (-pr[i], i), False, None, eng); return st, en, spans(st, eng)
    name = [o["tag"] + (o["wr"][0][0] if o["wr"] else "") for o in ops]; tags = sorted(set(name)); kind = np.array([tags.index(x) for x in name])
    eb = np.array(top[4]); eng = list(top[3]); st, en = top[1:3]; best = spans(st, eng)
    for k in range(P["tries"]):
        seg = np.searchsorted([st[i] for i in marks], st, side="right"); new = list(eng); eb2 = eb
        if k % P["every"] == P["every"] - 1: eb2 = lay(lambda i: (-en[i], -i), True, None, eng)[1]; eb2 = np.array(eb2) + (max(eb) - max(eb2))
        elif k % 3 == 1: eb2 = eb + P["nz"] * (rng.random(n) - 0.5) * (rng.random(n) < 0.2)
        elif k % 3 == 2: eb2 = eb + (500.0 * rng.integers(-2, 3, len(tags)) * (rng.random(len(tags)) < 0.2))[kind]
        else:
            for i in free:
                if rng.random() < P["part"]: new[i] = "s" if eng[i] == "v" else "v"
        st2, en2, now = again(eb2, new); good = now < best - 1.0
        if good.any():
            new = [new[i] if good[seg[i]] else eng[i] for i in range(n)]; eb2 = np.where(good[seg], eb2, eb)
            if not good.all(): st2, en2, now = again(eb2, new)
            if now.sum() < best.sum(): st, en, eng, eb, best = st2, en2, new, eb2, now
    top = (max(en), st, en, eng)
    busy = {e: 0.0 for e in "vspqy"}
    for o, s, z, e in zip(ops, top[1], top[2], top[3]):
        o["st"] = s; o["end"] = z; o["e"] = e
        if e: busy[e] += o["alts"][e][1]
    return sorted([i for i in range(n) if ops[i]["e"]], key=lambda i: (ops[i]["st"], i)), busy


def plan():
    keep = dict(P); others = []
    for guess in GUESSES:
        P.update(guess); others.append(([(o["alts"], P["far"] if o["kind"] == "arrive" else o["x"] if o["kind"] == "dma" else 0.0) for o in build()], P["lat"])); P.update(keep)
    ops = build(); depend(ops); order, busy = settle(ops, others)
    count = {}; known = {e: {} for e in "vspqy"}; nd = 0; steps = []
    for i in order:
        o = ops[i]; e = o["e"]; kn = known[e]; need = {}
        for d, hard in sorted(o["deps"].items()):
            od = ops[d]
            if od["kind"] == "arrive": sig, ck = ("ar%d" % od["x"], 12), {}
            else: sig, ck = od["sig"], od["ck"]
            if od["e"] == e and not hard: continue
            if kn.get(sig[0], 0) < sig[1]: need[sig[0]] = (max(sig[1], need.get(sig[0], (0,))[0]), ck if sig[1] >= need.get(sig[0], (0,))[0] else need[sig[0]][1])
        for s in list(need):
            if any(s2 != s and need[s2][1].get(s, 0) >= need[s][0] for s2 in need): need.pop(s)
        for s, (v, ck) in need.items():
            kn[s] = v
            for s2, v2 in ck.items(): kn[s2] = max(kn.get(s2, 0), v2)
        if o["kind"] == "dma": o["sig"] = ("d%d" % nd, 16); nd += 1
        elif o["kind"] == "send": o["sig"] = ("ls%d" % o["x"], 12)
        else: count[e] = count.get(e, 0) + 1; o["sig"] = (e, count[e])
        o["ck"] = dict(kn)
        steps.append((o, [(s, v[0]) for s, v in need.items()]))
    last = dict(count)
    for j in range(nd): last["d%d" % j] = 16
    for t in range(8): last["ls%d" % t] = 12; last["ar%d" % t] = 12
    seen = {}
    for kn in known.values():
        for s, v in kn.items(): seen[s] = max(seen.get(s, 0), v)
    return steps, [(s, v) for s, v in last.items() if seen.get(s, 0) < v], ops, busy


PLAN = []


def rank_program(g, core, T, topo):
    rank = T.rank_of(core)
    if rank is None:
        return
    if not PLAN: PLAN.append(plan())
    steps, last = PLAN[0][:2]
    queue = {"v": g.vector, "s": g.scalar, "p": g.tensor, "q": g, "y": g.sync}

    def r(x):
        if not isinstance(x, tuple): return x
        return T[x[0]][(x[1],) + x[2]]

    for o, waits in steps:
        for s, v in waits: queue[o["e"]].wait_ge(T.sem[s], v)
        if o["kind"] == "send":
            t = o["x"]; peers = [(d, T.cores[(rank + d) % 4]) for d in (1, 2, 3)]
            used = []; tr = []
            for d, peer in sorted(peers, key=lambda x: topo.die(x[1]) == topo.die(core)):
                en = topo.engines(core, peer); en = [e for e in en[0::2] + en[1::2] if e not in used][:4]; used += en
                rid, pid = topo.addr(peer)[:2]
                tr.append(RemoteDMATransfer(dst_ids=[DstId(rid=rid, pnc=pid)], dma_engine_mask=sum(1 << e for e in en), remote_sem=T.sem["ar%d" % t],
                                            src=T["SN"][:, t % 4, 128 * d - 128:128 * d], dst=T["LN"][:, t, 384 - 128 * d:512 - 128 * d]))
            g.remote_dma_fused(tr, local_sem=T.sem["ls%d" % t])
        else:
            o["alts"][o["e"]][0](g, r).then_inc(T.sem[o["sig"][0]], 16 if o["kind"] == "dma" else 1)
    for s, v in last: g.sync.wait_ge(T.sem[s], v)
